import numpy as np
import ml_dtypes


def mxq(x, axis, fmt="e4m3"):
    dtype, down = {"e4m3": (ml_dtypes.float8_e4m3fn, 7), "e5m2": (ml_dtypes.float8_e5m2, 14)}[fmt]
    v = np.moveaxis(np.asarray(x, np.float32).astype(ml_dtypes.bfloat16).astype(np.float64), axis, -1)
    blocks = v.reshape(v.shape[:-1] + (-1, 32))
    amax = np.abs(blocks).max(-1, keepdims=True)
    byte = np.maximum(np.where(amax > 0, np.frexp(amax)[1] - 1 + 127, 0) - down, 1)
    scale = np.exp2(byte - 127.0)
    codes = (blocks / scale).astype(np.float32).astype(dtype).astype(np.float64)
    return np.moveaxis((codes * scale).reshape(v.shape), -1, axis)


WIDE = False


def mx_kscale(k):
    if not WIDE:
        return np.ones(k)
    levels = np.array([18, -18])
    if k % 512:
        return np.exp2(np.random.permutation(np.resize(levels, k // 32))).repeat(32)
    a = np.empty((k // 512, 16))
    for p in range(k // 512):
        a[p, :8] = np.random.permutation(np.resize(levels, 8))
        for g in range(8):
            far = levels[np.abs(levels - a[p, g]) >= 10]
            a[p, g + 8] = far[np.random.randint(len(far))]
    return np.exp2(a.ravel()).repeat(32)


def f64(x):
    return np.asarray(x).astype(np.float64)


def striped(idx):
    return np.tile(np.asarray(idx).reshape(-1, 16).T, (8, 1)).astype(np.uint16)


def unstriped(offs):
    return offs[:16].T.reshape(-1).astype(np.int64)


B, N, T, D, R = 2, 512, 2048, 512, 512
LR = 0.1
EPS = 0.001


def setup_inputs():
    n = np.random.standard_normal
    idx = np.random.permutation(T)[:B * N]
    s = mx_kscale(D)[:, None]
    z = mx_kscale(R)[:, None]
    x = n((B, D, R))
    return {
        "xT": (x * s).astype(np.float32),
        "wT": (n((D, T)) * (1.00 / np.sqrt(D)) / s).astype(np.float32),
        "y": np.random.randint(0, 2, (B, R, N)).astype(np.float32),
        "wt": (np.random.uniform(0.5, 1.5, (B, R, 1)) * 1.0 / np.sqrt(R) * z).astype(np.float32),
        "xm": (x.transpose(0, 2, 1) / z).astype(np.float32),
        "vT": (np.random.uniform(0.1, 0.5, (D, T))).astype(np.float32),
        "offs": striped(idx),
    }


def reference(xT, wT, y, wt, xm, vT, offs):
    idx = unstriped(offs)
    pick = lambda x: x[:, idx].reshape(x.shape[0], B, N).transpose(1, 0, 2)
    a = mxq(f64(xT), 1, "e4m3").transpose(0, 2, 1) @ mxq(pick(f64(wT)), 1, "e4m3")
    g = f64(wt) * (1.0 / (1.0 + np.exp(-a)) - f64(y))
    dw = mxq(f64(xm), 1, "e4m3").transpose(0, 2, 1) @ mxq(g, 1, "e5m2")
    nv = pick(f64(vT)) + dw * dw
    nw = -LR * dw / (np.sqrt(nv) + EPS)
    tables = []
    for old, new in ((wT, nw), (vT, nv),):
        table = f64(old) if old is not wT else np.zeros((D, T))
        table[:, idx] = new.transpose(1, 0, 2).reshape(D, B * N)
        tables.append(table)
    return tuple(tables)

@@ -1,0 +1,204 @@
+from contextlib import ExitStack
+
+import concourse.mybir as mybir
+
+B, N, T, D, R = 2, 512, 2048, 512, 512
+LR = 0.1
+EPS = 0.001
+FLOPS = 2 * 2 * B * N * D * R
+
+F32 = mybir.dt.float32
+BF16 = mybir.dt.bfloat16
+U32 = mybir.dt.uint32
+U16 = mybir.dt.uint16
+U8 = mybir.dt.uint8
+E4M3 = mybir.dt.float8_e4m3fn_x4
+E5M2 = mybir.dt.float8_e5m2_x4
+ACT = mybir.ActivationFunctionType
+ALU = mybir.AluOpType
+
+P = 128
+PACK = 4
+LIST_COLS = N // 16
+
+
+def tile_attend_gnce_ada_kernel(tc, xT, wT, y, wt, xm, vT, offs, out_0, out_1):
+    nc = tc.nc
+    with ExitStack() as ctx:
+        held = ctx.enter_context(tc.tile_pool(name="held", bufs=1))
+        loads = ctx.enter_context(tc.tile_pool(name="loads", bufs=8))
+        work = ctx.enter_context(tc.tile_pool(name="work", bufs=1))
+        psum = ctx.enter_context(tc.psum_pool(name="psum", bufs=8))
+
+        offsets = held.tile([P, B * LIST_COLS], U16, name="offsets")
+        nc.sync.dma_start(offsets[:], offs)
+        row_weight = held.tile([P, B, PACK], F32, name="row_weight")
+        nc.scalar.dma_start(row_weight[:], wt.rearrange("b (p t) o -> p b (t o)", t=PACK))
+
+        def group_list(b):
+            return offsets[:, b * LIST_COLS : (b + 1) * LIST_COLS]
+
+        def load_table(rows):
+            tile = loads.tile([P, T], F32, name="loaded")
+            nc.sync.dma_start(tile[:], rows)
+            return tile
+
+        def load_rows(matrix):
+            tile = loads.tile([P, PACK, 512], F32, name="loaded")
+            nc.sync.dma_start(tile[:], matrix.rearrange("(p t) c -> p t c", t=PACK))
+            return tile
+
+        step_window = [held.tile([P, T], F32, name=f"step_window{j}") for j in range(4)]
+        square_window = [held.tile([P, T], F32, name=f"square_window{j}") for j in range(4)]
+
+        def load_window(j):
+            nc.sync.dma_start(square_window[j][:], vT[j * P : (j + 1) * P, :])
+
+        def load_v(j):
+            return load_table(vT[j * P : (j + 1) * P, :])
+
+        w_rows = wT.rearrange("(p t) c -> p t c", t=PACK)
+        w_plane = [load_table(w_rows[:, t, :]) for t in range(PACK)]
+        x_raw, y_raw, xm_raw, v_source = {}, {}, {}, {}
+        x_raw[0] = load_rows(xT[0])
+        v_source[0] = load_v(0)
+        y_raw[0] = load_rows(y[0])
+        v_source[1] = load_v(1)
+        xm_raw[0] = load_rows(xm[0])
+        v_source[2] = load_v(2)
+        x_raw[1] = load_rows(xT[1])
+        v_source[3] = load_v(3)
+        load_window(0)
+        load_window(1)
+        y_raw[1] = load_rows(y[1])
+        load_window(2)
+        xm_raw[1] = load_rows(xm[1])
+        load_window(3)
+
+        warm = held.tile([P, 1], F32, name="warm")
+        nc.scalar.activation(warm[:], row_weight[:, 0, 0:1], ACT.Sigmoid)
+
+        for j in range(4):
+            nc.gpsimd.memset(step_window[j][:], 0.0)
+
+        def copy_on(engine, out, in_):
+            if engine == "vector":
+                nc.vector.tensor_copy(out, in_)
+            elif engine == "scalar":
+                nc.scalar.copy(out, in_)
+            else:
+                nc.gpsimd.tensor_scalar(out, in_, 1.0, 0.0, ALU.mult, ALU.add)
+
+        def quantize(grouped, fmt, name):
+            codes = held.tile([P, 512], U32, name=name + "_codes", align_bytes=64)
+            scales = held.tile([P, 512], U8, name=name + "_scales", align_bytes=64)
+            nc.vector.quantize_mx(out=codes[:].bitcast(fmt), scales=scales[:], in_=grouped[:])
+            return codes, scales
+
+        def grouped_tile(name):
+            return work.tile([P, 512 * PACK], BF16, name=name, align_bytes=64)
+
+        def interleave(engine, planes, name):
+            grouped = grouped_tile(name)
+            copy_on(engine, grouped[:].rearrange("p (c t) -> p c t", t=PACK), planes.rearrange("p t c -> p c t"))
+            return grouped
+
+        def group_cols(b):
+            return slice(b * N, (b + 1) * N)
+
+        w_listed = work.tile([P, PACK, B * N], F32, name="wide")
+        for t in range(PACK - 1):
+            nc.vector.tensor_copy(w_listed[:, t, :], w_plane[t][:].indirect(offsets[:]))
+        for b in range(B):
+            nc.vector.tensor_copy(w_listed[:, PACK - 1, group_cols(b)], w_plane[PACK - 1][:].indirect(group_list(b)))
+
+        nv = held.tile([P, 4, B * N], F32, name="nv")
+
+        def product(stationary, moving, moving_fmt):
+            tiles = []
+            for k in range(4):
+                acc = psum.tile([P, N], F32, name="acc")
+                nc.tensor.matmul_mx(
+                    out=acc[:],
+                    lhsT=stationary[0][:, k * P : (k + 1) * P].bitcast(E4M3),
+                    lhsT_scale=stationary[1][:, k * P : (k + 1) * P],
+                    rhs=moving[0][:].bitcast(moving_fmt),
+                    rhs_scale=moving[1][:],
+                    start=True,
+                    stop=True,
+                )
+                tiles.append(acc)
+            return tiles
+
+        def residual(b, x_engine, subtract_engine):
+            w_grouped = interleave("scalar", w_listed[:, :, group_cols(b)], ("w0_g0", "w1_xm1")[b])
+            x_grouped = grouped_tile(("x0_xm0", "x1_g1")[b])
+            copy_on(
+                x_engine,
+                x_grouped[:].rearrange("p (t m j) -> p m t j", t=PACK, j=PACK),
+                x_raw[b][:].rearrange("p j (m t) -> p m t j", t=PACK),
+            )
+            x_mx = quantize(x_grouped, E4M3, f"x{b}")
+            w_mx = quantize(w_grouped, E4M3, f"w{b}")
+            logits = product(x_mx, w_mx, E4M3)
+            for t in range(PACK):
+                prob = work.tile([P, N], F32, name="prob", bufs=4)
+                nc.scalar.activation(prob[:], logits[t][:], ACT.Sigmoid)
+                subtract_engine.tensor_tensor(y_raw[b][:, t, :], prob[:], y_raw[b][:, t, :], ALU.subtract)
+
+        def gradient(b, xm_engine):
+            g_planes = work.tile([P, PACK, N], BF16, name="g_planes")
+            for t in range(PACK):
+                nc.scalar.activation(g_planes[:, t, :], y_raw[b][:, t, :], ACT.Copy, scale=row_weight[:, b, t : t + 1])
+            g_mx = quantize(interleave("scalar", g_planes[:], ("w0_g0", "x1_g1")[b]), E5M2, f"g{b}")
+            xm_mx = quantize(interleave(xm_engine, xm_raw[b][:], ("x0_xm0", "w1_xm1")[b]), E4M3, f"xm{b}")
+            return product(xm_mx, g_mx, E5M2)
+
+        def add_squares(b, dw):
+            for j in range(4):
+                square = work.tile([P, N], F32, name="square", bufs=4)
+                nc.scalar.activation(square[:], dw[j][:], ACT.Square)
+                nc.gpsimd.tensor_tensor(nv[:, j, group_cols(b)], nv[:, j, group_cols(b)], square[:], ALU.add)
+
+        def roots(b):
+            nc.scalar.activation(rate[:, :, group_cols(b)], nv[:, :, group_cols(b)], ACT.Sqrt)
+
+        def make_step(b, j, dw):
+            cols = group_cols(b)
+            nc.scalar.activation(rate[:, j, cols], rate[:, j, cols], ACT.Square, bias=EPS)
+            nc.scalar.activation(rate[:, j, cols], rate[:, j, cols], ACT.Abs_reciprocal_sqrt)
+            step = work.tile([P, N], F32, name="step", bufs=4)
+            nc.scalar.activation(step[:], dw[j][:], ACT.Copy, scale=-LR)
+            nc.gpsimd.tensor_tensor(step[:], step[:], rate[:, j, cols], ALU.mult)
+            return step
+
+        def scatter_squares(b, j):
+            nc.vector.tensor_copy(square_window[j][:].indirect(group_list(b)), nv[:, j, group_cols(b)])
+
+        def scatter_step(b, j, step):
+            nc.vector.tensor_copy(step_window[j][:].indirect(group_list(b)), step[:])
+
+        residual(0, "vector", nc.vector)
+        dw0 = gradient(0, "gpsimd")
+        for j in range(4):
+            nc.vector.tensor_copy(nv[:, j, :], v_source[j][:].indirect(offsets[:]))
+        add_squares(0, dw0)
+        residual(1, "scalar", nc.gpsimd)
+        rate = work.tile([P, 4, B * N], F32, name="wide")
+        roots(0)
+        step0 = [make_step(0, j, dw0) for j in range(3)]
+        dw1 = gradient(1, "gpsimd")
+        step0 += [make_step(0, j, dw0) for j in range(3, 4)]
+        add_squares(1, dw1)
+        for j in range(4):
+            scatter_squares(0, j)
+        for j in range(4):
+            scatter_step(0, j, step0[j])
+        roots(1)
+        step1 = [make_step(1, j, dw1) for j in range(4)]
+        for j in range(4):
+            scatter_squares(1, j)
+            nc.sync.dma_start(out_1[j * P : (j + 1) * P, :], square_window[j][:])
+        for j in range(4):
+            scatter_step(1, j, step1[j])
+            nc.sync.dma_start(out_0[j * P : (j + 1) * P, :], step_window[j][:])

@@ -20,6 +20,7 @@ ALU = mybir.AluOpType
 P = 128
 PACK = 4
 LIST_COLS = N // 16
+CFG = {"loads": "w0 w1 w2 w3 x0 v0 y0 v1 m0 x1 v2 y1 v3 m1 W2 W3 W1 W0", "w0": "S", "w1": "S", "x0": "V", "x1": 2, "m0": "V", "m1": 2, "g0": "S", "g1": "V", "h0": "S", "h1": "Y", "text": "G0 V2 G1 V0 W0 X0 Q0 M0 W1 M1 D0 X1 V1 Q1 D1 V3 A0 A1 S0 R1 R0 S1 T01"}
 
 
 def tile_attend_gnce_ada_kernel(tc, xT, wT, y, wt, xm, vT, offs, out_0, out_1):
@@ -54,40 +55,36 @@ def tile_attend_gnce_ada_kernel(tc, xT, wT, y, wt, xm, vT, offs, out_0, out_1):
         def load_window(j):
             nc.sync.dma_start(square_window[j][:], vT[j * P : (j + 1) * P, :])
 
-        def load_v(j):
-            return load_table(vT[j * P : (j + 1) * P, :])
-
         w_rows = wT.rearrange("(p t) c -> p t c", t=PACK)
-        w_plane = [load_table(w_rows[:, t, :]) for t in range(PACK)]
-        x_raw, y_raw, xm_raw, v_source = {}, {}, {}, {}
-        x_raw[0] = load_rows(xT[0])
-        v_source[0] = load_v(0)
-        y_raw[0] = load_rows(y[0])
-        v_source[1] = load_v(1)
-        xm_raw[0] = load_rows(xm[0])
-        v_source[2] = load_v(2)
-        x_raw[1] = load_rows(xT[1])
-        v_source[3] = load_v(3)
-        load_window(0)
-        load_window(1)
-        y_raw[1] = load_rows(y[1])
-        load_window(2)
-        xm_raw[1] = load_rows(xm[1])
-        load_window(3)
+        w_plane, x_raw, y_raw, xm_raw, v_source = {}, {}, {}, {}, {}
+        for item in CFG["loads"].split():
+            kind, k = item[0], int(item[1])
+            if kind == "w":
+                w_plane[k] = load_table(w_rows[:, k, :])
+            elif kind == "x":
+                x_raw[k] = load_rows(xT[k])
+            elif kind == "y":
+                y_raw[k] = load_rows(y[k])
+            elif kind == "m":
+                xm_raw[k] = load_rows(xm[k])
+            elif kind == "v":
+                v_source[k] = load_table(vT[k * P : (k + 1) * P, :])
+            else:
+                load_window(k)
 
         warm = held.tile([P, 1], F32, name="warm")
         nc.scalar.activation(warm[:], row_weight[:, 0, 0:1], ACT.Sigmoid)
 
         for j in range(4):
-            nc.gpsimd.memset(step_window[j][:], 0.0)
+            nc.vector.memset(step_window[j][:], 0.0)
 
         def copy_on(engine, out, in_):
-            if engine == "vector":
-                nc.vector.tensor_copy(out, in_)
-            elif engine == "scalar":
-                nc.scalar.copy(out, in_)
-            else:
-                nc.gpsimd.tensor_scalar(out, in_, 1.0, 0.0, ALU.mult, ALU.add)
+            n = out.shape[1]
+            cut = n if engine == "V" else 0 if engine == "S" else n * engine // 8
+            if cut > 0:
+                nc.vector.tensor_copy(out[:, :cut], in_[:, :cut])
+            if cut < n:
+                nc.scalar.copy(out[:, cut:], in_[:, cut:])
 
         def quantize(grouped, fmt, name):
             codes = held.tile([P, 512], U32, name=name + "_codes", align_bytes=64)
@@ -107,12 +104,9 @@ def tile_attend_gnce_ada_kernel(tc, xT, wT, y, wt, xm, vT, offs, out_0, out_1):
             return slice(b * N, (b + 1) * N)
 
         w_listed = work.tile([P, PACK, B * N], F32, name="wide")
-        for t in range(PACK - 1):
-            nc.vector.tensor_copy(w_listed[:, t, :], w_plane[t][:].indirect(offsets[:]))
-        for b in range(B):
-            nc.vector.tensor_copy(w_listed[:, PACK - 1, group_cols(b)], w_plane[PACK - 1][:].indirect(group_list(b)))
-
         nv = held.tile([P, 4, B * N], F32, name="nv")
+        rate = held.tile([P, 4, B * N], F32, name="rate")
+        state = {}
 
         def product(stationary, moving, moving_fmt):
             tiles = []
@@ -130,75 +124,89 @@ def tile_attend_gnce_ada_kernel(tc, xT, wT, y, wt, xm, vT, offs, out_0, out_1):
                 tiles.append(acc)
             return tiles
 
-        def residual(b, x_engine, subtract_engine):
-            w_grouped = interleave("scalar", w_listed[:, :, group_cols(b)], ("w0_g0", "w1_xm1")[b])
-            x_grouped = grouped_tile(("x0_xm0", "x1_g1")[b])
+        def gather_w(b):
+            if b == 0:
+                for t in range(PACK - 1):
+                    nc.vector.tensor_copy(w_listed[:, t, :], w_plane[t][:].indirect(offsets[:]))
+            nc.vector.tensor_copy(w_listed[:, PACK - 1, group_cols(b)], w_plane[PACK - 1][:].indirect(group_list(b)))
+
+        def quantize_w(b):
+            state["w", b] = quantize(interleave(CFG["w%d" % b], w_listed[:, :, group_cols(b)], "gw%d" % b), E4M3, f"w{b}")
+
+        def quantize_x(b):
+            x_grouped = grouped_tile("gx")
             copy_on(
-                x_engine,
+                CFG["x%d" % b],
                 x_grouped[:].rearrange("p (t m j) -> p m t j", t=PACK, j=PACK),
                 x_raw[b][:].rearrange("p j (m t) -> p m t j", t=PACK),
             )
-            x_mx = quantize(x_grouped, E4M3, f"x{b}")
-            w_mx = quantize(w_grouped, E4M3, f"w{b}")
-            logits = product(x_mx, w_mx, E4M3)
-            for t in range(PACK):
-                prob = work.tile([P, N], F32, name="prob", bufs=4)
-                nc.scalar.activation(prob[:], logits[t][:], ACT.Sigmoid)
-                subtract_engine.tensor_tensor(y_raw[b][:, t, :], prob[:], y_raw[b][:, t, :], ALU.subtract)
+            state["x", b] = quantize(x_grouped, E4M3, f"x{b}")
 
-        def gradient(b, xm_engine):
+        def quantize_xm(b):
+            state["xm", b] = quantize(interleave(CFG["m%d" % b], xm_raw[b][:], "gm"), E4M3, f"xm{b}")
+
+        def quantize_g(b):
+            logits = product(state["x", b], state["w", b], E4M3)
             g_planes = work.tile([P, PACK, N], BF16, name="g_planes")
             for t in range(PACK):
-                nc.scalar.activation(g_planes[:, t, :], y_raw[b][:, t, :], ACT.Copy, scale=row_weight[:, b, t : t + 1])
-            g_mx = quantize(interleave("scalar", g_planes[:], ("w0_g0", "x1_g1")[b]), E5M2, f"g{b}")
-            xm_mx = quantize(interleave(xm_engine, xm_raw[b][:], ("x0_xm0", "w1_xm1")[b]), E4M3, f"xm{b}")
-            return product(xm_mx, g_mx, E5M2)
+                weight = row_weight[:, b, t : t + 1]
+                labels = y_raw[b][:, t, :]
+                prob = work.tile([P, N], F32, name="prob", bufs=4)
+                if CFG["h%d" % b] == "Y":
+                    nc.scalar.activation(labels, labels, ACT.Copy, scale=weight)
+                    nc.scalar.activation(prob[:], logits[t][:], ACT.Sigmoid)
+                    nc.vector.scalar_tensor_tensor(g_planes[:, t, :], prob[:], weight, labels, ALU.mult, ALU.subtract)
+                else:
+                    nc.scalar.activation(prob[:], logits[t][:], ACT.Sigmoid)
+                    nc.vector.tensor_tensor(labels, prob[:], labels, ALU.subtract)
+            for t in range(PACK):
+                weight = row_weight[:, b, t : t + 1]
+                if CFG["h%d" % b] == "S":
+                    nc.scalar.activation(g_planes[:, t, :], y_raw[b][:, t, :], ACT.Copy, scale=weight)
+                elif CFG["h%d" % b] == "V":
+                    nc.vector.tensor_scalar(g_planes[:, t, :], y_raw[b][:, t, :], weight, None, ALU.mult)
+            state["g", b] = quantize(interleave(CFG["g%d" % b], g_planes[:], "gw%d" % b), E5M2, f"g{b}")
 
-        def add_squares(b, dw):
+        def gradient(b):
+            state["dw", b] = product(state["xm", b], state["g", b], E5M2)
+
+        def gather_v(j):
+            nc.vector.tensor_copy(nv[:, j, :], v_source[j][:].indirect(offsets[:]))
+
+        def add_squares(b):
             for j in range(4):
-                square = work.tile([P, N], F32, name="square", bufs=4)
-                nc.scalar.activation(square[:], dw[j][:], ACT.Square)
-                nc.gpsimd.tensor_tensor(nv[:, j, group_cols(b)], nv[:, j, group_cols(b)], square[:], ALU.add)
+                square = work.tile([P, N], F32, name="square", bufs=2)
+                nc.scalar.activation(square[:], state["dw", b][j][:], ACT.Square)
+                nc.vector.tensor_tensor(nv[:, j, group_cols(b)], nv[:, j, group_cols(b)], square[:], ALU.add)
+
+        def scatter_squares(b):
+            for j in range(4):
+                nc.vector.tensor_copy(square_window[j][:].indirect(group_list(b)), nv[:, j, group_cols(b)])
+                if b == B - 1:
+                    nc.sync.dma_start(out_1[j * P : (j + 1) * P, :], square_window[j][:])
 
         def roots(b):
             nc.scalar.activation(rate[:, :, group_cols(b)], nv[:, :, group_cols(b)], ACT.Sqrt)
 
-        def make_step(b, j, dw):
-            cols = group_cols(b)
-            nc.scalar.activation(rate[:, j, cols], rate[:, j, cols], ACT.Square, bias=EPS)
-            nc.scalar.activation(rate[:, j, cols], rate[:, j, cols], ACT.Abs_reciprocal_sqrt)
-            step = work.tile([P, N], F32, name="step", bufs=4)
-            nc.scalar.activation(step[:], dw[j][:], ACT.Copy, scale=-LR)
-            nc.gpsimd.tensor_tensor(step[:], step[:], rate[:, j, cols], ALU.mult)
-            return step
+        def steps(groups):
+            cols = slice(groups[0] * N, (groups[-1] + 1) * N)
+            listed = offsets[:, groups[0] * LIST_COLS : (groups[-1] + 1) * LIST_COLS]
+            for j in range(4):
+                nc.scalar.activation(rate[:, j, cols], rate[:, j, cols], ACT.Square, bias=EPS)
+                nc.scalar.activation(rate[:, j, cols], rate[:, j, cols], ACT.Abs_reciprocal_sqrt)
+                for b in groups:
+                    step = rate[:, j, group_cols(b)]
+                    nc.vector.scalar_tensor_tensor(step, state["dw", b][j][:], -LR, step, ALU.mult, ALU.mult)
+                nc.vector.tensor_copy(step_window[j][:].indirect(listed), rate[:, j, cols])
+                if groups[-1] == B - 1:
+                    nc.sync.dma_start(out_0[j * P : (j + 1) * P, :], step_window[j][:])
 
-        def scatter_squares(b, j):
-            nc.vector.tensor_copy(square_window[j][:].indirect(group_list(b)), nv[:, j, group_cols(b)])
-
-        def scatter_step(b, j, step):
-            nc.vector.tensor_copy(step_window[j][:].indirect(group_list(b)), step[:])
-
-        residual(0, "vector", nc.vector)
-        dw0 = gradient(0, "gpsimd")
-        for j in range(4):
-            nc.vector.tensor_copy(nv[:, j, :], v_source[j][:].indirect(offsets[:]))
-        add_squares(0, dw0)
-        residual(1, "scalar", nc.gpsimd)
-        rate = work.tile([P, 4, B * N], F32, name="wide")
-        roots(0)
-        step0 = [make_step(0, j, dw0) for j in range(3)]
-        dw1 = gradient(1, "gpsimd")
-        step0 += [make_step(0, j, dw0) for j in range(3, 4)]
-        add_squares(1, dw1)
-        for j in range(4):
-            scatter_squares(0, j)
-        for j in range(4):
-            scatter_step(0, j, step0[j])
-        roots(1)
-        step1 = [make_step(1, j, dw1) for j in range(4)]
-        for j in range(4):
-            scatter_squares(1, j)
-            nc.sync.dma_start(out_1[j * P : (j + 1) * P, :], square_window[j][:])
-        for j in range(4):
-            scatter_step(1, j, step1[j])
-            nc.sync.dma_start(out_0[j * P : (j + 1) * P, :], step_window[j][:])
+        blocks = {
+            "G": gather_w, "W": quantize_w, "X": quantize_x, "M": quantize_xm, "Q": quantize_g, "D": gradient,
+            "V": gather_v, "A": add_squares, "S": scatter_squares, "R": roots,
+        }
+        for item in CFG["text"].split():
+            if item[0] == "T":
+                steps([int(c) for c in item[1:]])
+            else:
+                blocks[item[0]](int(item[1]))

@@ -20,21 +20,20 @@ ALU = mybir.AluOpType
 P = 128
 PACK = 4
 LIST_COLS = N // 16
-CFG = {"loads": "w0 w1 w2 w3 x0 v0 y0 v1 m0 x1 v2 y1 v3 m1 W2 W3 W1 W0", "w0": "S", "w1": "S", "x0": "V", "x1": 2, "m0": "V", "m1": 2, "g0": "S", "g1": "V", "h0": "S", "h1": "Y", "text": "G0 V2 G1 V0 W0 X0 Q0 M0 W1 M1 D0 X1 V1 Q1 D1 V3 A0 A1 S0 R1 R0 S1 T01"}
+CFG = {"ring": 7, "late": 2, "loads": "w0 w1 w2 w3 x0 v0 y0 v1 m0 v2 x1 W0 v3 y1 W1 W2 W3 m1", "w0": "S", "w1": "S", "x0": "V", "x1": "S", "m0": "V", "m1": "S", "g0": "S", "g1": "S", "h0": "S", "h1": "S", "d0": "V", "d1": "G", "a00": "V", "a01": "V", "a02": "G", "a03": "V", "a10": "G", "a11": "G", "a12": "G", "a13": "G", "p0": "G", "p1": "V", "tw0": "", "tw1": "", "tx0": "", "tx1": "", "txm0": "", "txm1": "", "tg0": "", "tg1": "", "z": "", "text": "G0 G1 W0 X0 E0 Q0 M0 D0 W1 V0 V1 V2 V3 A00 A01 A02 A03 X1 E1 R0 P00 P01 P02 M1 Q1 D1 P03 A10 A11 A12 A13 C2 C3 S00 S01 S02 S03 O00 O01 O02 O03 R1 P10 P11 P12 P13 S10 S11 S12 S13 O10 O11 O12 O13", "tags": "ABCCDDAB"}
 
 
 def tile_attend_gnce_ada_kernel(tc, xT, wT, y, wt, xm, vT, offs, out_0, out_1):
     nc = tc.nc
     with ExitStack() as ctx:
         held = ctx.enter_context(tc.tile_pool(name="held", bufs=1))
-        loads = ctx.enter_context(tc.tile_pool(name="loads", bufs=8))
+        loads = ctx.enter_context(tc.tile_pool(name="loads", bufs=CFG["ring"]))
         work = ctx.enter_context(tc.tile_pool(name="work", bufs=1))
         psum = ctx.enter_context(tc.psum_pool(name="psum", bufs=8))
 
         offsets = held.tile([P, B * LIST_COLS], U16, name="offsets")
         nc.sync.dma_start(offsets[:], offs)
         row_weight = held.tile([P, B, PACK], F32, name="row_weight")
-        nc.scalar.dma_start(row_weight[:], wt.rearrange("b (p t) o -> p b (t o)", t=PACK))
 
         def group_list(b):
             return offsets[:, b * LIST_COLS : (b + 1) * LIST_COLS]
@@ -49,7 +48,7 @@ def tile_attend_gnce_ada_kernel(tc, xT, wT, y, wt, xm, vT, offs, out_0, out_1):
             nc.sync.dma_start(tile[:], matrix.rearrange("(p t) c -> p t c", t=PACK))
             return tile
 
-        step_window = [held.tile([P, T], F32, name=f"step_window{j}") for j in range(4)]
+        step_window = {}
         square_window = [held.tile([P, T], F32, name=f"square_window{j}") for j in range(4)]
 
         def load_window(j):
@@ -63,22 +62,39 @@ def tile_attend_gnce_ada_kernel(tc, xT, wT, y, wt, xm, vT, offs, out_0, out_1):
                 w_plane[k] = load_table(w_rows[:, k, :])
             elif kind == "x":
                 x_raw[k] = load_rows(xT[k])
+                if k == 0:
+                    nc.sync.dma_start(row_weight[:], wt.rearrange("b (p t) o -> p b (t o)", t=PACK))
             elif kind == "y":
                 y_raw[k] = load_rows(y[k])
             elif kind == "m":
                 xm_raw[k] = load_rows(xm[k])
             elif kind == "v":
-                v_source[k] = load_table(vT[k * P : (k + 1) * P, :])
+                if k >= 4 - CFG["late"]:
+                    v_source[k] = work.tile([P, T], F32, name="table%d" % k, align_bytes=64)
+                    nc.sync.dma_start(v_source[k][:], vT[k * P : (k + 1) * P, :])
+                else:
+                    v_source[k] = load_table(vT[k * P : (k + 1) * P, :])
             else:
                 load_window(k)
 
         warm = held.tile([P, 1], F32, name="warm")
-        nc.scalar.activation(warm[:], row_weight[:, 0, 0:1], ACT.Sigmoid)
+        nc.gpsimd.memset(warm[:], 0.0)
+        nc.scalar.activation(warm[:], warm[:], ACT.Sigmoid)
 
-        for j in range(4):
-            nc.vector.memset(step_window[j][:], 0.0)
+        def clear_window(j):
+            step_window[j] = work.tile([P, T], F32, name="table%d" % j, align_bytes=64)
+            nc.gpsimd.memset(step_window[j][:], 0.0)
+
+        for j in range(4 - CFG["late"]):
+            clear_window(j)
+
+        def engine_of(key):
+            return nc.vector if CFG[key] == "V" else nc.gpsimd
 
         def copy_on(engine, out, in_):
+            if engine == "G":
+                nc.gpsimd.tensor_scalar(out, in_, 1.0, 0.0, ALU.mult, ALU.add)
+                return
             n = out.shape[1]
             cut = n if engine == "V" else 0 if engine == "S" else n * engine // 8
             if cut > 0:
@@ -87,7 +103,7 @@ def tile_attend_gnce_ada_kernel(tc, xT, wT, y, wt, xm, vT, offs, out_0, out_1):
                 nc.scalar.copy(out[:, cut:], in_[:, cut:])
 
         def quantize(grouped, fmt, name):
-            codes = held.tile([P, 512], U32, name=name + "_codes", align_bytes=64)
+            codes = work.tile([P, 512], U32, name=name + "_codes", tag=CFG["t" + name] or name, align_bytes=64)
             scales = held.tile([P, 512], U8, name=name + "_scales", align_bytes=64)
             nc.vector.quantize_mx(out=codes[:].bitcast(fmt), scales=scales[:], in_=grouped[:])
             return codes, scales
@@ -105,7 +121,7 @@ def tile_attend_gnce_ada_kernel(tc, xT, wT, y, wt, xm, vT, offs, out_0, out_1):
 
         w_listed = work.tile([P, PACK, B * N], F32, name="wide")
         nv = held.tile([P, 4, B * N], F32, name="nv")
-        rate = held.tile([P, 4, B * N], F32, name="rate")
+        rate = {}
         state = {}
 
         def product(stationary, moving, moving_fmt):
@@ -131,10 +147,10 @@ def tile_attend_gnce_ada_kernel(tc, xT, wT, y, wt, xm, vT, offs, out_0, out_1):
             nc.vector.tensor_copy(w_listed[:, PACK - 1, group_cols(b)], w_plane[PACK - 1][:].indirect(group_list(b)))
 
         def quantize_w(b):
-            state["w", b] = quantize(interleave(CFG["w%d" % b], w_listed[:, :, group_cols(b)], "gw%d" % b), E4M3, f"w{b}")
+            state["w", b] = quantize(interleave(CFG["w%d" % b], w_listed[:, :, group_cols(b)], CFG["tags"][b]), E4M3, f"w{b}")
 
         def quantize_x(b):
-            x_grouped = grouped_tile("gx")
+            x_grouped = grouped_tile(CFG["tags"][2 + b])
             copy_on(
                 CFG["x%d" % b],
                 x_grouped[:].rearrange("p (t m j) -> p m t j", t=PACK, j=PACK),
@@ -143,11 +159,12 @@ def tile_attend_gnce_ada_kernel(tc, xT, wT, y, wt, xm, vT, offs, out_0, out_1):
             state["x", b] = quantize(x_grouped, E4M3, f"x{b}")
 
         def quantize_xm(b):
-            state["xm", b] = quantize(interleave(CFG["m%d" % b], xm_raw[b][:], "gm"), E4M3, f"xm{b}")
+            state["xm", b] = quantize(interleave(CFG["m%d" % b], xm_raw[b][:], CFG["tags"][4 + b]), E4M3, f"xm{b}")
 
-        def quantize_g(b):
+        def residual(b):
             logits = product(state["x", b], state["w", b], E4M3)
-            g_planes = work.tile([P, PACK, N], BF16, name="g_planes")
+            if CFG["h%d" % b] == "Y":
+                state["planes", b] = work.tile([P, PACK, N], BF16, name="g_planes")
             for t in range(PACK):
                 weight = row_weight[:, b, t : t + 1]
                 labels = y_raw[b][:, t, :]
@@ -155,17 +172,24 @@ def tile_attend_gnce_ada_kernel(tc, xT, wT, y, wt, xm, vT, offs, out_0, out_1):
                 if CFG["h%d" % b] == "Y":
                     nc.scalar.activation(labels, labels, ACT.Copy, scale=weight)
                     nc.scalar.activation(prob[:], logits[t][:], ACT.Sigmoid)
-                    nc.vector.scalar_tensor_tensor(g_planes[:, t, :], prob[:], weight, labels, ALU.mult, ALU.subtract)
+                    nc.vector.scalar_tensor_tensor(state["planes", b][:, t, :], prob[:], weight, labels, ALU.mult, ALU.subtract)
                 else:
                     nc.scalar.activation(prob[:], logits[t][:], ACT.Sigmoid)
-                    nc.vector.tensor_tensor(labels, prob[:], labels, ALU.subtract)
+                    engine_of("d%d" % b).tensor_tensor(labels, prob[:], labels, ALU.subtract)
+
+        def quantize_g(b):
+            if CFG["h%d" % b] != "Y":
+                state["planes", b] = work.tile([P, PACK, N], BF16, name="g_planes")
+            g_planes = state["planes", b]
             for t in range(PACK):
                 weight = row_weight[:, b, t : t + 1]
-                if CFG["h%d" % b] == "S":
+                if CFG["h%d" % b] == "G":
+                    nc.gpsimd.tensor_scalar(g_planes[:, t, :], y_raw[b][:, t, :], weight, 0.0, ALU.mult, ALU.add)
+                elif CFG["h%d" % b] == "S":
                     nc.scalar.activation(g_planes[:, t, :], y_raw[b][:, t, :], ACT.Copy, scale=weight)
                 elif CFG["h%d" % b] == "V":
                     nc.vector.tensor_scalar(g_planes[:, t, :], y_raw[b][:, t, :], weight, None, ALU.mult)
-            state["g", b] = quantize(interleave(CFG["g%d" % b], g_planes[:], "gw%d" % b), E5M2, f"g{b}")
+            state["g", b] = quantize(interleave(CFG["g%d" % b], g_planes[:], CFG["tags"][6 + b]), E5M2, f"g{b}")
 
         def gradient(b):
             state["dw", b] = product(state["xm", b], state["g", b], E5M2)
@@ -173,40 +197,49 @@ def tile_attend_gnce_ada_kernel(tc, xT, wT, y, wt, xm, vT, offs, out_0, out_1):
         def gather_v(j):
             nc.vector.tensor_copy(nv[:, j, :], v_source[j][:].indirect(offsets[:]))
 
-        def add_squares(b):
-            for j in range(4):
-                square = work.tile([P, N], F32, name="square", bufs=2)
-                nc.scalar.activation(square[:], state["dw", b][j][:], ACT.Square)
-                nc.vector.tensor_tensor(nv[:, j, group_cols(b)], nv[:, j, group_cols(b)], square[:], ALU.add)
+        def clear_late(j):
+            if j >= 4 - CFG["late"]:
+                clear_window(j)
 
-        def scatter_squares(b):
-            for j in range(4):
-                nc.vector.tensor_copy(square_window[j][:].indirect(group_list(b)), nv[:, j, group_cols(b)])
-                if b == B - 1:
-                    nc.sync.dma_start(out_1[j * P : (j + 1) * P, :], square_window[j][:])
+        def add_square(b, j):
+            square = work.tile([P, N], F32, name="square", bufs=4)
+            nc.scalar.activation(square[:], state["dw", b][j][:], ACT.Square)
+            engine_of("a%d%d" % (b, j)).tensor_tensor(nv[:, j, group_cols(b)], nv[:, j, group_cols(b)], square[:], ALU.add)
+
+        def scatter_square(b, j):
+            nc.vector.tensor_copy(square_window[j][:].indirect(group_list(b)), nv[:, j, group_cols(b)])
+            if b == B - 1:
+                nc.sync.dma_start(out_1[j * P : (j + 1) * P, :], square_window[j][:])
 
         def roots(b):
-            nc.scalar.activation(rate[:, :, group_cols(b)], nv[:, :, group_cols(b)], ACT.Sqrt)
+            rate[b] = work.tile([P, 4, N], F32, name="rate", bufs=2)
+            nc.scalar.activation(rate[b][:], nv[:, :, group_cols(b)], ACT.Sqrt)
 
-        def steps(groups):
-            cols = slice(groups[0] * N, (groups[-1] + 1) * N)
-            listed = offsets[:, groups[0] * LIST_COLS : (groups[-1] + 1) * LIST_COLS]
-            for j in range(4):
-                nc.scalar.activation(rate[:, j, cols], rate[:, j, cols], ACT.Square, bias=EPS)
-                nc.scalar.activation(rate[:, j, cols], rate[:, j, cols], ACT.Abs_reciprocal_sqrt)
-                for b in groups:
-                    step = rate[:, j, group_cols(b)]
-                    nc.vector.scalar_tensor_tensor(step, state["dw", b][j][:], -LR, step, ALU.mult, ALU.mult)
-                nc.vector.tensor_copy(step_window[j][:].indirect(listed), rate[:, j, cols])
-                if groups[-1] == B - 1:
-                    nc.sync.dma_start(out_0[j * P : (j + 1) * P, :], step_window[j][:])
+        def make_step(b, j):
+            nc.scalar.activation(rate[b][:, j, :], rate[b][:, j, :], ACT.Square, bias=EPS)
+            nc.scalar.activation(rate[b][:, j, :], rate[b][:, j, :], ACT.Abs_reciprocal_sqrt)
+            if CFG["z"] == "%d%d" % (b, j):
+                descent = work.tile([P, N], F32, name="descent_late", tag=CFG["tags"][7], align_bytes=64)
+            else:
+                descent = work.tile([P, N], F32, name="descent", bufs=4)
+            nc.scalar.activation(descent[:], state["dw", b][j][:], ACT.Copy, scale=-LR)
+            if CFG["p%d" % b] == "G":
+                nc.gpsimd.tensor_tensor(descent[:], descent[:], rate[b][:, j, :], ALU.mult)
+            state["step", b, j] = descent
+
+        def scatter_step(b, j):
+            window = step_window[j][:].indirect(group_list(b))
+            if CFG["p%d" % b] == "G":
+                nc.vector.tensor_copy(window, state["step", b, j][:])
+            else:
+                nc.vector.tensor_tensor(window, state["step", b, j][:], rate[b][:, j, :], ALU.mult)
+            if b == B - 1:
+                nc.sync.dma_start(out_0[j * P : (j + 1) * P, :], step_window[j][:])
 
         blocks = {
-            "G": gather_w, "W": quantize_w, "X": quantize_x, "M": quantize_xm, "Q": quantize_g, "D": gradient,
-            "V": gather_v, "A": add_squares, "S": scatter_squares, "R": roots,
+            "G": gather_w, "W": quantize_w, "X": quantize_x, "M": quantize_xm, "E": residual, "Q": quantize_g,
+            "D": gradient, "V": gather_v, "A": add_square, "S": scatter_square, "R": roots, "P": make_step,
+            "O": scatter_step, "C": clear_late,
         }
         for item in CFG["text"].split():
-            if item[0] == "T":
-                steps([int(c) for c in item[1:]])
-            else:
-                blocks[item[0]](int(item[1]))
+            blocks[item[0]](*[int(c) for c in item[1:]])

@@ -19,227 +19,213 @@ ALU = mybir.AluOpType
 
 P = 128
 PACK = 4
+COLS = 512
+D_TILES = D // P
 LIST_COLS = N // 16
-CFG = {"ring": 7, "late": 2, "loads": "w0 w1 w2 w3 x0 v0 y0 v1 m0 v2 x1 W0 v3 y1 W1 W2 W3 m1", "w0": "S", "w1": "S", "x0": "V", "x1": "S", "m0": "V", "m1": "S", "g0": "S", "g1": "S", "h0": "S", "h1": "S", "d0": "V", "d1": "G", "a00": "V", "a01": "V", "a02": "G", "a03": "V", "a10": "G", "a11": "G", "a12": "G", "a13": "G", "p0": "G", "p1": "V", "tw0": "", "tw1": "", "tx0": "", "tx1": "", "txm0": "", "txm1": "", "tg0": "", "tg1": "", "z": "", "text": "G0 G1 W0 X0 E0 Q0 M0 D0 W1 V0 V1 V2 V3 A00 A01 A02 A03 X1 E1 R0 P00 P01 P02 M1 Q1 D1 P03 A10 A11 A12 A13 C2 C3 S00 S01 S02 S03 O00 O01 O02 O03 R1 P10 P11 P12 P13 S10 S11 S12 S13 O10 O11 O12 O13", "tags": "ABCCDDAB"}
+MX_ALIGN = 64
+LOAD_BUFS = 5
+GPSIMD_COLS = 256
 
 
 def tile_attend_gnce_ada_kernel(tc, xT, wT, y, wt, xm, vT, offs, out_0, out_1):
     nc = tc.nc
     with ExitStack() as ctx:
         held = ctx.enter_context(tc.tile_pool(name="held", bufs=1))
-        loads = ctx.enter_context(tc.tile_pool(name="loads", bufs=CFG["ring"]))
+        loads = ctx.enter_context(tc.tile_pool(name="loads", bufs=LOAD_BUFS))
         work = ctx.enter_context(tc.tile_pool(name="work", bufs=1))
         psum = ctx.enter_context(tc.psum_pool(name="psum", bufs=8))
+
 
         offsets = held.tile([P, B * LIST_COLS], U16, name="offsets")
         nc.sync.dma_start(offsets[:], offs)
         row_weight = held.tile([P, B, PACK], F32, name="row_weight")
+        nv_table = [held.tile([P, T], F32, name=f"nv_table{j}") for j in range(D_TILES)]
 
         def group_list(b):
             return offsets[:, b * LIST_COLS : (b + 1) * LIST_COLS]
 
-        def load_table(rows):
-            tile = loads.tile([P, T], F32, name="loaded")
-            nc.sync.dma_start(tile[:], rows)
-            return tile
-
-        def load_rows(matrix):
-            tile = loads.tile([P, PACK, 512], F32, name="loaded")
-            nc.sync.dma_start(tile[:], matrix.rearrange("(p t) c -> p t c", t=PACK))
-            return tile
-
-        step_window = {}
-        square_window = [held.tile([P, T], F32, name=f"square_window{j}") for j in range(4)]
-
-        def load_window(j):
-            nc.sync.dma_start(square_window[j][:], vT[j * P : (j + 1) * P, :])
-
-        w_rows = wT.rearrange("(p t) c -> p t c", t=PACK)
-        w_plane, x_raw, y_raw, xm_raw, v_source = {}, {}, {}, {}, {}
-        for item in CFG["loads"].split():
-            kind, k = item[0], int(item[1])
-            if kind == "w":
-                w_plane[k] = load_table(w_rows[:, k, :])
-            elif kind == "x":
-                x_raw[k] = load_rows(xT[k])
-                if k == 0:
-                    nc.sync.dma_start(row_weight[:], wt.rearrange("b (p t) o -> p b (t o)", t=PACK))
-            elif kind == "y":
-                y_raw[k] = load_rows(y[k])
-            elif kind == "m":
-                xm_raw[k] = load_rows(xm[k])
-            elif kind == "v":
-                if k >= 4 - CFG["late"]:
-                    v_source[k] = work.tile([P, T], F32, name="table%d" % k, align_bytes=64)
-                    nc.sync.dma_start(v_source[k][:], vT[k * P : (k + 1) * P, :])
-                else:
-                    v_source[k] = load_table(vT[k * P : (k + 1) * P, :])
-            else:
-                load_window(k)
-
-        warm = held.tile([P, 1], F32, name="warm")
-        nc.gpsimd.memset(warm[:], 0.0)
-        nc.scalar.activation(warm[:], warm[:], ACT.Sigmoid)
-
-        def clear_window(j):
-            step_window[j] = work.tile([P, T], F32, name="table%d" % j, align_bytes=64)
-            nc.gpsimd.memset(step_window[j][:], 0.0)
-
-        for j in range(4 - CFG["late"]):
-            clear_window(j)
-
-        def engine_of(key):
-            return nc.vector if CFG[key] == "V" else nc.gpsimd
-
-        def copy_on(engine, out, in_):
-            if engine == "G":
-                nc.gpsimd.tensor_scalar(out, in_, 1.0, 0.0, ALU.mult, ALU.add)
-                return
-            n = out.shape[1]
-            cut = n if engine == "V" else 0 if engine == "S" else n * engine // 8
-            if cut > 0:
-                nc.vector.tensor_copy(out[:, :cut], in_[:, :cut])
-            if cut < n:
-                nc.scalar.copy(out[:, cut:], in_[:, cut:])
-
-        def quantize(grouped, fmt, name):
-            codes = work.tile([P, 512], U32, name=name + "_codes", tag=CFG["t" + name] or name, align_bytes=64)
-            scales = held.tile([P, 512], U8, name=name + "_scales", align_bytes=64)
-            nc.vector.quantize_mx(out=codes[:].bitcast(fmt), scales=scales[:], in_=grouped[:])
-            return codes, scales
-
-        def grouped_tile(name):
-            return work.tile([P, 512 * PACK], BF16, name=name, align_bytes=64)
-
-        def interleave(engine, planes, name):
-            grouped = grouped_tile(name)
-            copy_on(engine, grouped[:].rearrange("p (c t) -> p c t", t=PACK), planes.rearrange("p t c -> p c t"))
-            return grouped
-
         def group_cols(b):
             return slice(b * N, (b + 1) * N)
 
-        w_listed = work.tile([P, PACK, B * N], F32, name="wide")
-        nv = held.tile([P, 4, B * N], F32, name="nv")
-        rate = {}
-        state = {}
+        def tile_rows(j):
+            return slice(j * P, (j + 1) * P)
+
+        def load(tile, source):
+            nc.sync.dma_start(tile[:], source)
+            return tile
+
+        def load_table(rows):
+            return load(loads.tile([P, T], F32, name="loaded"), rows)
+
+        def as_planes(matrix):
+            return matrix.rearrange("(p t) c -> p t c", t=PACK)
+
+        def load_planes(matrix, tag):
+            return load(work.tile([P, PACK, COLS], F32, name="raw", tag=tag, align_bytes=MX_ALIGN), as_planes(matrix))
+
+        def load_labels(b):
+            return load(loads.tile([P, PACK, N], F32, name="loaded"), as_planes(y[b]))
+
+        w_rows = wT.rearrange("(p t) c -> p t c", t=PACK)
+        w_plane = [load_table(w_rows[:, t, :]) for t in range(PACK)]
+        x_raw0 = load_planes(xT[0], "x_buffer")
+        load(row_weight, wt.rearrange("b (p t) o -> p b (t o)", t=PACK))
+        v_source = [load_table(vT[tile_rows(0), :])]
+        labels0 = load_labels(0)
+        v_source.append(load_table(vT[tile_rows(1), :]))
+        xm_raw0 = load_planes(xm[0], "xm_buffer")
+
+        step_table = []
+        for j in range(D_TILES):
+            step_table.append(work.tile([P, T], F32, name=f"step_table{j}", align_bytes=MX_ALIGN))
+            nc.gpsimd.memset(step_table[j][:], 0.0)
+
+        w_listed = work.tile([P, PACK, B * N], F32, name="w_listed")
+        nv = held.tile([P, D_TILES, B * N], F32, name="nv")
+
+        def on_gpsimd(out, in0, in1, op):
+            for c in range(0, N, GPSIMD_COLS):
+                cols = slice(c, c + GPSIMD_COLS)
+                nc.gpsimd.tensor_tensor(out[:, cols], in0[:, cols], in1[:, cols], op)
+
+        def staged_tile(tag):
+            return work.tile([P, COLS * PACK], BF16, name="staged", tag=tag, align_bytes=MX_ALIGN)
+
+        def interleave(copy, planes, tag):
+            staged = staged_tile(tag)
+            copy(staged[:].rearrange("p (c t) -> p c t", t=PACK), planes.rearrange("p t c -> p c t"))
+            return staged
+
+        def quantize(staged, fmt, name, codes_tag):
+            codes = work.tile([P, COLS], U32, name=name + "_codes", tag=codes_tag, align_bytes=MX_ALIGN)
+            scales = held.tile([P, COLS], U8, name=name + "_scales", align_bytes=MX_ALIGN)
+            nc.vector.quantize_mx(out=codes[:].bitcast(fmt), scales=scales[:], in_=staged[:])
+            return codes, scales
+
+        def quantize_x(b, x_raw, copy, stage_tag, codes_tag):
+            staged = staged_tile(stage_tag)
+            copy(
+                staged[:].rearrange("p (t m k) -> p m t k", t=PACK, k=PACK),
+                x_raw[:].rearrange("p k (m t) -> p m t k", t=PACK),
+            )
+            return quantize(staged, E4M3, f"x{b}", codes_tag)
+
+        def quantize_w(b, stage_tag, codes_tag):
+            staged = staged_tile(stage_tag)
+            interleaved = staged[:].rearrange("p (c t) -> p c t", t=PACK)
+            planes = w_listed[:, :, group_cols(b)].rearrange("p t c -> p c t")
+            for t in range(0, PACK, 2):
+                nc.scalar.copy(interleaved[:, :, t : t + 2], planes[:, :, t : t + 2])
+            return quantize(staged, E4M3, f"w{b}", codes_tag)
 
         def product(stationary, moving, moving_fmt):
-            tiles = []
-            for k in range(4):
-                acc = psum.tile([P, N], F32, name="acc")
+            banks = []
+            for i in range(COLS // P):
+                bank = psum.tile([P, COLS], F32, name="bank")
                 nc.tensor.matmul_mx(
-                    out=acc[:],
-                    lhsT=stationary[0][:, k * P : (k + 1) * P].bitcast(E4M3),
-                    lhsT_scale=stationary[1][:, k * P : (k + 1) * P],
+                    out=bank[:],
+                    lhsT=stationary[0][:, i * P : (i + 1) * P].bitcast(E4M3),
+                    lhsT_scale=stationary[1][:, i * P : (i + 1) * P],
                     rhs=moving[0][:].bitcast(moving_fmt),
                     rhs_scale=moving[1][:],
                     start=True,
                     stop=True,
                 )
-                tiles.append(acc)
-            return tiles
+                banks.append(bank)
+            return banks
 
-        def gather_w(b):
-            if b == 0:
-                for t in range(PACK - 1):
-                    nc.vector.tensor_copy(w_listed[:, t, :], w_plane[t][:].indirect(offsets[:]))
-            nc.vector.tensor_copy(w_listed[:, PACK - 1, group_cols(b)], w_plane[PACK - 1][:].indirect(group_list(b)))
-
-        def quantize_w(b):
-            state["w", b] = quantize(interleave(CFG["w%d" % b], w_listed[:, :, group_cols(b)], CFG["tags"][b]), E4M3, f"w{b}")
-
-        def quantize_x(b):
-            x_grouped = grouped_tile(CFG["tags"][2 + b])
-            copy_on(
-                CFG["x%d" % b],
-                x_grouped[:].rearrange("p (t m j) -> p m t j", t=PACK, j=PACK),
-                x_raw[b][:].rearrange("p j (m t) -> p m t j", t=PACK),
-            )
-            state["x", b] = quantize(x_grouped, E4M3, f"x{b}")
-
-        def quantize_xm(b):
-            state["xm", b] = quantize(interleave(CFG["m%d" % b], xm_raw[b][:], CFG["tags"][4 + b]), E4M3, f"xm{b}")
-
-        def residual(b):
-            logits = product(state["x", b], state["w", b], E4M3)
-            if CFG["h%d" % b] == "Y":
-                state["planes", b] = work.tile([P, PACK, N], BF16, name="g_planes")
+        def residual(x_mx, w_mx, labels, subtract):
+            logits = product(x_mx, w_mx, E4M3)
             for t in range(PACK):
-                weight = row_weight[:, b, t : t + 1]
-                labels = y_raw[b][:, t, :]
-                prob = work.tile([P, N], F32, name="prob", bufs=4)
-                if CFG["h%d" % b] == "Y":
-                    nc.scalar.activation(labels, labels, ACT.Copy, scale=weight)
-                    nc.scalar.activation(prob[:], logits[t][:], ACT.Sigmoid)
-                    nc.vector.scalar_tensor_tensor(state["planes", b][:, t, :], prob[:], weight, labels, ALU.mult, ALU.subtract)
-                else:
-                    nc.scalar.activation(prob[:], logits[t][:], ACT.Sigmoid)
-                    engine_of("d%d" % b).tensor_tensor(labels, prob[:], labels, ALU.subtract)
+                prob = work.tile([P, N], F32, name="prob", tag="f32_ring", bufs=4)
+                nc.scalar.activation(prob[:], logits[t][:], ACT.Sigmoid)
+                subtract(labels[:, t, :], prob[:], labels[:, t, :], ALU.subtract)
 
-        def quantize_g(b):
-            if CFG["h%d" % b] != "Y":
-                state["planes", b] = work.tile([P, PACK, N], BF16, name="g_planes")
-            g_planes = state["planes", b]
+        def quantize_g(b, residuals, planes_tag, stage_tag, codes_tag):
+            g_planes = work.tile([P, PACK, N], BF16, name="g_planes", tag=planes_tag, align_bytes=MX_ALIGN)
             for t in range(PACK):
-                weight = row_weight[:, b, t : t + 1]
-                if CFG["h%d" % b] == "G":
-                    nc.gpsimd.tensor_scalar(g_planes[:, t, :], y_raw[b][:, t, :], weight, 0.0, ALU.mult, ALU.add)
-                elif CFG["h%d" % b] == "S":
-                    nc.scalar.activation(g_planes[:, t, :], y_raw[b][:, t, :], ACT.Copy, scale=weight)
-                elif CFG["h%d" % b] == "V":
-                    nc.vector.tensor_scalar(g_planes[:, t, :], y_raw[b][:, t, :], weight, None, ALU.mult)
-            state["g", b] = quantize(interleave(CFG["g%d" % b], g_planes[:], CFG["tags"][6 + b]), E5M2, f"g{b}")
+                nc.scalar.activation(g_planes[:, t, :], residuals[:, t, :], ACT.Copy, scale=row_weight[:, b, t : t + 1])
+            return quantize(interleave(nc.scalar.copy, g_planes[:], stage_tag), E5M2, f"g{b}", codes_tag)
 
-        def gradient(b):
-            state["dw", b] = product(state["xm", b], state["g", b], E5M2)
-
-        def gather_v(j):
-            nc.vector.tensor_copy(nv[:, j, :], v_source[j][:].indirect(offsets[:]))
-
-        def clear_late(j):
-            if j >= 4 - CFG["late"]:
-                clear_window(j)
-
-        def add_square(b, j):
-            square = work.tile([P, N], F32, name="square", bufs=4)
-            nc.scalar.activation(square[:], state["dw", b][j][:], ACT.Square)
-            engine_of("a%d%d" % (b, j)).tensor_tensor(nv[:, j, group_cols(b)], nv[:, j, group_cols(b)], square[:], ALU.add)
-
-        def scatter_square(b, j):
-            nc.vector.tensor_copy(square_window[j][:].indirect(group_list(b)), nv[:, j, group_cols(b)])
-            if b == B - 1:
-                nc.sync.dma_start(out_1[j * P : (j + 1) * P, :], square_window[j][:])
+        def add_squares(b, dw):
+            for j in range(D_TILES):
+                square = work.tile([P, N], F32, name="square", bufs=D_TILES)
+                nc.scalar.activation(square[:], dw[j][:], ACT.Square)
+                add = nc.vector.tensor_tensor if j == 0 else on_gpsimd
+                add(nv[:, j, group_cols(b)], nv[:, j, group_cols(b)], square[:], ALU.add)
 
         def roots(b):
-            rate[b] = work.tile([P, 4, N], F32, name="rate", bufs=2)
-            nc.scalar.activation(rate[b][:], nv[:, :, group_cols(b)], ACT.Sqrt)
+            rate = work.tile([P, D_TILES, N], F32, name=f"rate{b}", align_bytes=MX_ALIGN)
+            nc.scalar.activation(rate[:], nv[:, :, group_cols(b)], ACT.Sqrt)
+            return rate
 
-        def make_step(b, j):
-            nc.scalar.activation(rate[b][:, j, :], rate[b][:, j, :], ACT.Square, bias=EPS)
-            nc.scalar.activation(rate[b][:, j, :], rate[b][:, j, :], ACT.Abs_reciprocal_sqrt)
-            if CFG["z"] == "%d%d" % (b, j):
-                descent = work.tile([P, N], F32, name="descent_late", tag=CFG["tags"][7], align_bytes=64)
-            else:
-                descent = work.tile([P, N], F32, name="descent", bufs=4)
-            nc.scalar.activation(descent[:], state["dw", b][j][:], ACT.Copy, scale=-LR)
-            if CFG["p%d" % b] == "G":
-                nc.gpsimd.tensor_tensor(descent[:], descent[:], rate[b][:, j, :], ALU.mult)
-            state["step", b, j] = descent
+        def finish_rate(rate, j):
+            nc.scalar.activation(rate[:, j, :], rate[:, j, :], ACT.Square, bias=EPS)
+            nc.scalar.activation(rate[:, j, :], rate[:, j, :], ACT.Abs_reciprocal_sqrt)
 
-        def scatter_step(b, j):
-            window = step_window[j][:].indirect(group_list(b))
-            if CFG["p%d" % b] == "G":
-                nc.vector.tensor_copy(window, state["step", b, j][:])
-            else:
-                nc.vector.tensor_tensor(window, state["step", b, j][:], rate[b][:, j, :], ALU.mult)
-            if b == B - 1:
-                nc.sync.dma_start(out_0[j * P : (j + 1) * P, :], step_window[j][:])
+        def copy_descent(descent, dw_bank):
+            nc.scalar.activation(descent[:], dw_bank[:], ACT.Copy, scale=-LR)
+            return descent
 
-        blocks = {
-            "G": gather_w, "W": quantize_w, "X": quantize_x, "M": quantize_xm, "E": residual, "Q": quantize_g,
-            "D": gradient, "V": gather_v, "A": add_square, "S": scatter_square, "R": roots, "P": make_step,
-            "O": scatter_step, "C": clear_late,
-        }
-        for item in CFG["text"].split():
-            blocks[item[0]](*[int(c) for c in item[1:]])
+        def step_factors(rate, dw, j):
+            finish_rate(rate, j)
+            return copy_descent(work.tile([P, N], F32, name="descent", tag="f32_ring", bufs=4), dw[j])
+
+        def scatter_nv(b, j):
+            nc.vector.tensor_copy(nv_table[j][:].indirect(group_list(b)), nv[:, j, group_cols(b)])
+
+        def scatter_step(b, j, descent, rate):
+            nc.vector.tensor_tensor(step_table[j][:].indirect(group_list(b)), descent[:], rate[:, j, :], ALU.mult)
+
+        for t in range(PACK - 1):
+            nc.vector.tensor_copy(w_listed[:, t, :], w_plane[t][:].indirect(offsets[:]))
+        for b in range(B):
+            nc.vector.tensor_copy(w_listed[:, PACK - 1, group_cols(b)], w_plane[PACK - 1][:].indirect(group_list(b)))
+
+        x_mx0 = quantize_x(0, x_raw0, nc.vector.tensor_copy, "stage_c", "x0_codes")
+        w_mx0 = quantize_w(0, "stage_a", "x_buffer")
+        w_mx1 = quantize_w(1, "stage_b", "stage_c")
+        residual(x_mx0, w_mx0, labels0, nc.vector.tensor_tensor)
+
+        x_raw1 = load_planes(xT[1], "x_buffer")
+        v_source.append(load(work.tile([P, T], F32, name="v2_buffer", align_bytes=MX_ALIGN), vT[tile_rows(2), :]))
+        v_source.append(load_table(vT[tile_rows(3), :]))
+        for j in range(D_TILES):
+            load(nv_table[j], vT[tile_rows(j), :])
+        labels1 = load_labels(1)
+
+        xm_mx0 = quantize(interleave(nc.vector.tensor_copy, xm_raw0[:], "stage_d"), E4M3, "xm0", "xm0_codes")
+        g_mx0 = quantize_g(0, labels0, "g0_planes", "stage_a", "xm_buffer")
+        dw0 = product(xm_mx0, g_mx0, E5M2)
+        xm_raw1 = load_planes(xm[1], "xm_buffer")
+
+        for j in range(D_TILES):
+            nc.vector.tensor_copy(nv[:, j, :], v_source[j][:].indirect(offsets[:]))
+        add_squares(0, dw0)
+
+        x_mx1 = quantize_x(1, x_raw1, nc.scalar.copy, "stage_b", "v2_buffer")
+        residual(x_mx1, w_mx1, labels1, on_gpsimd)
+        last = D_TILES - 1
+        rate0 = roots(0)
+        descent0 = [step_factors(rate0, dw0, j) for j in range(last)]
+        xm_mx1 = quantize(interleave(nc.scalar.copy, xm_raw1[:], "stage_d"), E4M3, "xm1", "xm1_codes")
+        g_mx1 = quantize_g(1, labels1, "xm_buffer", "stage_c", "g1_codes")
+        dw1 = product(xm_mx1, g_mx1, E5M2)
+        finish_rate(rate0, last)
+        last_descent = work.tile([P, N], F32, name="last_descent", tag="xm_buffer", align_bytes=MX_ALIGN)
+        descent0.append(copy_descent(last_descent, dw0[last]))
+        add_squares(1, dw1)
+
+        for j in range(D_TILES):
+            scatter_nv(0, j)
+        for j in range(D_TILES):
+            scatter_step(0, j, descent0[j], rate0)
+
+        rate1 = roots(1)
+        descent1 = [step_factors(rate1, dw1, j) for j in range(D_TILES)]
+        for j in range(D_TILES):
+            scatter_nv(1, j)
+            nc.sync.dma_start(out_1[tile_rows(j), :], nv_table[j][:])
+        for j in range(D_TILES):
+            scatter_step(1, j, descent1[j], rate1)
+            nc.sync.dma_start(out_0[tile_rows(j), :], step_table[j][:])

@@ -78,7 +78,7 @@ def tile_attend_gnce_ada_kernel(tc, xT, wT, y, wt, xm, vT, offs, out_0, out_1):
         step_table = []
         for j in range(D_TILES):
             step_table.append(work.tile([P, T], F32, name=f"step_table{j}", align_bytes=MX_ALIGN))
-            nc.gpsimd.memset(step_table[j][:], 0.0)
+            nc.vector.memset(step_table[j][:].bitcast(U32), 0)
 
         w_listed = work.tile([P, PACK, B * N], F32, name="w_listed")
         nv = held.tile([P, D_TILES, B * N], F32, name="nv")

@@ -17,6 +17,13 @@ E5M2 = mybir.dt.float8_e5m2_x4
 ACT = mybir.ActivationFunctionType
 ALU = mybir.AluOpType
 
+ORDER = 1
+YW = "S"
+GS = 512
+X1 = "S"
+XM1 = "S"
+LN = 0
+VS = 0
 P = 128
 PACK = 4
 COLS = 512
@@ -24,7 +31,7 @@ D_TILES = D // P
 LIST_COLS = N // 16
 MX_ALIGN = 64
 LOAD_BUFS = 5
-GPSIMD_COLS = 256
+GPSIMD_COLS = 512
 
 
 def tile_attend_gnce_ada_kernel(tc, xT, wT, y, wt, xm, vT, offs, out_0, out_1):
@@ -35,11 +42,11 @@ def tile_attend_gnce_ada_kernel(tc, xT, wT, y, wt, xm, vT, offs, out_0, out_1):
         work = ctx.enter_context(tc.tile_pool(name="work", bufs=1))
         psum = ctx.enter_context(tc.psum_pool(name="psum", bufs=8))
 
-
         offsets = held.tile([P, B * LIST_COLS], U16, name="offsets")
         nc.sync.dma_start(offsets[:], offs)
-        row_weight = held.tile([P, B, PACK], F32, name="row_weight")
+        row_weight = [held.tile([P, PACK], F32, name=f"row_weight{b}") for b in range(B)]
         nv_table = [held.tile([P, T], F32, name=f"nv_table{j}") for j in range(D_TILES)]
+        last = D_TILES - 1
 
         def group_list(b):
             return offsets[:, b * LIST_COLS : (b + 1) * LIST_COLS]
@@ -63,22 +70,22 @@ def tile_attend_gnce_ada_kernel(tc, xT, wT, y, wt, xm, vT, offs, out_0, out_1):
         def load_planes(matrix, tag):
             return load(work.tile([P, PACK, COLS], F32, name="raw", tag=tag, align_bytes=MX_ALIGN), as_planes(matrix))
 
-        def load_labels(b):
-            return load(loads.tile([P, PACK, N], F32, name="loaded"), as_planes(y[b]))
+        def load_row_weight(b):
+            load(row_weight[b], wt[b].rearrange("(p t) o -> p (t o)", t=PACK))
 
         w_rows = wT.rearrange("(p t) c -> p t c", t=PACK)
         w_plane = [load_table(w_rows[:, t, :]) for t in range(PACK)]
         x_raw0 = load_planes(xT[0], "x_buffer")
-        load(row_weight, wt.rearrange("b (p t) o -> p b (t o)", t=PACK))
         v_source = [load_table(vT[tile_rows(0), :])]
-        labels0 = load_labels(0)
+        load_row_weight(0)
+        labels0 = load_planes(y[0], "y_buffer")
         v_source.append(load_table(vT[tile_rows(1), :]))
         xm_raw0 = load_planes(xm[0], "xm_buffer")
 
         step_table = []
         for j in range(D_TILES):
             step_table.append(work.tile([P, T], F32, name=f"step_table{j}", align_bytes=MX_ALIGN))
-            nc.vector.memset(step_table[j][:].bitcast(U32), 0)
+            nc.gpsimd.memset(step_table[j][:].bitcast(U32), 0)
 
         w_listed = work.tile([P, PACK, B * N], F32, name="w_listed")
         nv = held.tile([P, D_TILES, B * N], F32, name="nv")
@@ -96,136 +103,209 @@ def tile_attend_gnce_ada_kernel(tc, xT, wT, y, wt, xm, vT, offs, out_0, out_1):
             copy(staged[:].rearrange("p (c t) -> p c t", t=PACK), planes.rearrange("p t c -> p c t"))
             return staged
 
-        def quantize(staged, fmt, name, codes_tag):
+        def mx_tiles(name, codes_tag):
             codes = work.tile([P, COLS], U32, name=name + "_codes", tag=codes_tag, align_bytes=MX_ALIGN)
             scales = held.tile([P, COLS], U8, name=name + "_scales", align_bytes=MX_ALIGN)
+            return codes, scales
+
+        def quantize(staged, fmt, name, codes_tag):
+            codes, scales = mx_tiles(name, codes_tag)
             nc.vector.quantize_mx(out=codes[:].bitcast(fmt), scales=scales[:], in_=staged[:])
             return codes, scales
 
-        def quantize_x(b, x_raw, copy, stage_tag, codes_tag):
+        def stage_x(x_raw, copy, stage_tag):
             staged = staged_tile(stage_tag)
             copy(
                 staged[:].rearrange("p (t m k) -> p m t k", t=PACK, k=PACK),
                 x_raw[:].rearrange("p k (m t) -> p m t k", t=PACK),
             )
-            return quantize(staged, E4M3, f"x{b}", codes_tag)
+            return staged
 
-        def quantize_w(b, stage_tag, codes_tag):
-            staged = staged_tile(stage_tag)
-            interleaved = staged[:].rearrange("p (c t) -> p c t", t=PACK)
-            planes = w_listed[:, :, group_cols(b)].rearrange("p t c -> p c t")
-            for t in range(0, PACK, 2):
-                nc.scalar.copy(interleaved[:, :, t : t + 2], planes[:, :, t : t + 2])
-            return quantize(staged, E4M3, f"w{b}", codes_tag)
+        def multiply(stationary, i, moving, moving_fmt):
+            bank = psum.tile([P, COLS], F32, name="bank")
+            nc.tensor.matmul_mx(
+                out=bank[:],
+                lhsT=stationary[0][:, i * P : (i + 1) * P].bitcast(E4M3),
+                lhsT_scale=stationary[1][:, i * P : (i + 1) * P],
+                rhs=moving[0][:].bitcast(moving_fmt),
+                rhs_scale=moving[1][:],
+                start=True,
+                stop=True,
+            )
+            return bank
 
         def product(stationary, moving, moving_fmt):
-            banks = []
-            for i in range(COLS // P):
-                bank = psum.tile([P, COLS], F32, name="bank")
-                nc.tensor.matmul_mx(
-                    out=bank[:],
-                    lhsT=stationary[0][:, i * P : (i + 1) * P].bitcast(E4M3),
-                    lhsT_scale=stationary[1][:, i * P : (i + 1) * P],
-                    rhs=moving[0][:].bitcast(moving_fmt),
-                    rhs_scale=moving[1][:],
-                    start=True,
-                    stop=True,
-                )
-                banks.append(bank)
-            return banks
+            return [multiply(stationary, i, moving, moving_fmt) for i in range(COLS // P)]
 
-        def residual(x_mx, w_mx, labels, subtract):
+        def probabilities(x_mx, w_mx):
             logits = product(x_mx, w_mx, E4M3)
+            probs = []
             for t in range(PACK):
-                prob = work.tile([P, N], F32, name="prob", tag="f32_ring", bufs=4)
-                nc.scalar.activation(prob[:], logits[t][:], ACT.Sigmoid)
-                subtract(labels[:, t, :], prob[:], labels[:, t, :], ALU.subtract)
-
-        def quantize_g(b, residuals, planes_tag, stage_tag, codes_tag):
-            g_planes = work.tile([P, PACK, N], BF16, name="g_planes", tag=planes_tag, align_bytes=MX_ALIGN)
-            for t in range(PACK):
-                nc.scalar.activation(g_planes[:, t, :], residuals[:, t, :], ACT.Copy, scale=row_weight[:, b, t : t + 1])
-            return quantize(interleave(nc.scalar.copy, g_planes[:], stage_tag), E5M2, f"g{b}", codes_tag)
+                probs.append(work.tile([P, N], F32, name="prob", tag="f32_ring", bufs=4))
+                nc.scalar.activation(probs[t][:], logits[t][:], ACT.Sigmoid)
+            return probs
 
         def add_squares(b, dw):
             for j in range(D_TILES):
-                square = work.tile([P, N], F32, name="square", bufs=D_TILES)
+                square = work.tile([P, N], F32, name="square")
                 nc.scalar.activation(square[:], dw[j][:], ACT.Square)
-                add = nc.vector.tensor_tensor if j == 0 else on_gpsimd
-                add(nv[:, j, group_cols(b)], nv[:, j, group_cols(b)], square[:], ALU.add)
+                on_gpsimd(nv[:, j, group_cols(b)], nv[:, j, group_cols(b)], square[:], ALU.add)
 
-        def roots(b):
-            rate = work.tile([P, D_TILES, N], F32, name=f"rate{b}", align_bytes=MX_ALIGN)
-            nc.scalar.activation(rate[:], nv[:, :, group_cols(b)], ACT.Sqrt)
+        def gp_copy(out, in_):
+            n = out.shape[1] // 8
+            for c in range(8):
+                nc.gpsimd.tensor_scalar(out[:, c * n : (c + 1) * n], in_[:, c * n : (c + 1) * n], 1.0, 0.0, ALU.mult, ALU.add)
+
+        def roots(sums):
+            rate = work.tile([P, D_TILES, N], F32, name="rate", align_bytes=MX_ALIGN)
+            nc.scalar.activation(rate[:], sums, ACT.Ln if LN else ACT.Sqrt)
             return rate
 
         def finish_rate(rate, j):
+            if LN:
+                nc.scalar.activation(rate[:, j, :], rate[:, j, :], ACT.Sigmoid)
+                return
             nc.scalar.activation(rate[:, j, :], rate[:, j, :], ACT.Square, bias=EPS)
             nc.scalar.activation(rate[:, j, :], rate[:, j, :], ACT.Abs_reciprocal_sqrt)
 
-        def copy_descent(descent, dw_bank):
+        def copy_descent(dw_bank, tag):
+            descent = work.tile([P, N], F32, name="descent", tag=tag, bufs=4 if tag == "f32_ring" else 1)
             nc.scalar.activation(descent[:], dw_bank[:], ACT.Copy, scale=-LR)
             return descent
 
-        def step_factors(rate, dw, j):
-            finish_rate(rate, j)
-            return copy_descent(work.tile([P, N], F32, name="descent", tag="f32_ring", bufs=4), dw[j])
+        def gather_v(j):
+            if VS:
+                for b in range(B):
+                    nc.vector.tensor_copy(nv[:, j, group_cols(b)], v_source[j][:].indirect(group_list(b)))
+            else:
+                nc.vector.tensor_copy(nv[:, j, :], v_source[j][:].indirect(offsets[:]))
 
-        def scatter_nv(b, j):
-            nc.vector.tensor_copy(nv_table[j][:].indirect(group_list(b)), nv[:, j, group_cols(b)])
+        def scatter_nv(b, j, values):
+            nc.vector.tensor_copy(nv_table[j][:].indirect(group_list(b)), values)
 
         def scatter_step(b, j, descent, rate):
-            nc.vector.tensor_tensor(step_table[j][:].indirect(group_list(b)), descent[:], rate[:, j, :], ALU.mult)
+            nc.vector.tensor_tensor(step_table[j][:].indirect(group_list(b)), descent[:], rate, ALU.mult)
 
         for t in range(PACK - 1):
             nc.vector.tensor_copy(w_listed[:, t, :], w_plane[t][:].indirect(offsets[:]))
         for b in range(B):
             nc.vector.tensor_copy(w_listed[:, PACK - 1, group_cols(b)], w_plane[PACK - 1][:].indirect(group_list(b)))
 
-        x_mx0 = quantize_x(0, x_raw0, nc.vector.tensor_copy, "stage_c", "x0_codes")
-        w_mx0 = quantize_w(0, "stage_a", "x_buffer")
-        w_mx1 = quantize_w(1, "stage_b", "stage_c")
-        residual(x_mx0, w_mx0, labels0, nc.vector.tensor_tensor)
+        def load_v(j):
+            v_source.append(load_table(vT[tile_rows(j), :]))
+
+        def load_nv_table(j):
+            load(nv_table[j], vT[tile_rows(j), :])
+
+
+        w_staged = [staged_tile("stage_a"), staged_tile("stage_b")]
+        for t in range(0, PACK, 2):
+            for b in range(B):
+                nc.scalar.copy(
+                    w_staged[b][:].rearrange("p (c t) -> p c t", t=PACK)[:, :, t : t + 2],
+                    w_listed[:, t : t + 2, group_cols(b)].rearrange("p t c -> p c t"),
+                )
+        x_staged0 = stage_x(x_raw0, nc.vector.tensor_copy, "stage_c")
+        w_mx0 = quantize(w_staged[0], E4M3, "w0", "x_buffer")
+        x_mx0 = quantize(x_staged0, E4M3, "x0", "x0_codes")
+        gather_v(0)
+        logits0 = product(x_mx0, w_mx0, E4M3)
+        w_mx1 = quantize(w_staged[1], E4M3, "w1", "stage_c")
+        g_planes0 = work.tile([P, PACK, N], BF16, name="g_planes0", tag="g0_planes", align_bytes=MX_ALIGN)
+        for t in range(PACK):
+            weight = row_weight[0][:, t : t + 1]
+            prob = work.tile([P, N], F32, name="prob", tag="f32_ring", bufs=4)
+            nc.scalar.activation(prob[:], logits0[t][:], ACT.Sigmoid)
+            if YW == "S":
+                nc.scalar.activation(labels0[:, t, :], labels0[:, t, :], ACT.Copy, scale=weight)
+            else:
+                for c in range(0, N, 256):
+                    nc.gpsimd.tensor_scalar(labels0[:, t, c : c + 256], labels0[:, t, c : c + 256], weight, 0.0, ALU.mult, ALU.add)
+            nc.vector.scalar_tensor_tensor(g_planes0[:, t, :], prob[:], weight, labels0[:, t, :], ALU.mult, ALU.subtract)
+            if t == 0:
+                gather_v(1)
 
         x_raw1 = load_planes(xT[1], "x_buffer")
         v_source.append(load(work.tile([P, T], F32, name="v2_buffer", align_bytes=MX_ALIGN), vT[tile_rows(2), :]))
-        v_source.append(load_table(vT[tile_rows(3), :]))
-        for j in range(D_TILES):
-            load(nv_table[j], vT[tile_rows(j), :])
-        labels1 = load_labels(1)
+        load_nv_table(0)
+        load_row_weight(1)
+        load_v(3)
+        load_nv_table(1)
+        load_nv_table(2)
+        load_nv_table(3)
+        labels1 = load_planes(y[1], "y_buffer")
 
-        xm_mx0 = quantize(interleave(nc.vector.tensor_copy, xm_raw0[:], "stage_d"), E4M3, "xm0", "xm0_codes")
-        g_mx0 = quantize_g(0, labels0, "g0_planes", "stage_a", "xm_buffer")
+        xm_staged0 = interleave(nc.scalar.copy, xm_raw0[:], "stage_d")
+        xm_mx0 = quantize(xm_staged0, E4M3, "xm0", "xm0_codes")
+        if GS == 512:
+            g_mx0 = quantize(interleave(nc.vector.tensor_copy, g_planes0[:], "stage_a"), E5M2, "g0", "xm_buffer")
+        else:
+            g_mx0 = mx_tiles("g0", "g0_codes")
+            for copy, tag, c0, c1 in ((nc.vector.tensor_copy, "stage_a", 0, GS), (nc.scalar.copy, "xm_buffer", GS, N)):
+                part = work.tile([P, (c1 - c0) * PACK], BF16, name="part", tag=tag, align_bytes=MX_ALIGN)
+                copy(part[:].rearrange("p (c t) -> p c t", t=PACK), g_planes0[:, :, c0:c1].rearrange("p t c -> p c t"))
+                for a in range(c0, c1, 256):
+                    b = min(a + 256, c1)
+                    nc.vector.quantize_mx(out=g_mx0[0][:, a:b].bitcast(E5M2), scales=g_mx0[1][:, a:b], in_=part[:, (a - c0) * PACK : (b - c0) * PACK])
+        xm_raw1 = load_planes(xm[1], "x_buffer")
+        x_staged1 = stage_x(x_raw1, nc.scalar.copy, "stage_b")
+        gather_v(2)
+        x_mx1 = quantize(x_staged1, E4M3, "x1", "v2_buffer")
         dw0 = product(xm_mx0, g_mx0, E5M2)
-        xm_raw1 = load_planes(xm[1], "xm_buffer")
 
+        def square_of(square, dw_bank):
+            nc.scalar.activation(square, dw_bank[:], ACT.Square)
+            return square
+
+        def add_square(add, b, j, square):
+            add(nv[:, j, group_cols(b)], nv[:, j, group_cols(b)], square[j], ALU.add)
+
+        square0 = [square_of(work.tile([P, N], F32, name="square", bufs=D_TILES)[:], dw0[0])]
+        nc.vector.tensor_tensor(nv_table[0][:].indirect(group_list(0)), nv[:, 0, group_cols(0)], square0[0], ALU.add)
+        sums0 = work.tile([P, D_TILES + 1, N], F32, name="sums0", tag="stage_b", align_bytes=MX_ALIGN)
+        for j in range(1, D_TILES):
+            square0.append(square_of(sums0[:, j, :], dw0[j]))
+        gather_v(3)
+        place0 = [1, 0, 2, 3]
+        for j in place0:
+            on_gpsimd(sums0[:, place0[j], :], nv[:, j, group_cols(0)], square0[j], ALU.add)
+
+        descent0 = [copy_descent(dw0[j], f"descent0{j}") for j in range(2)]
+        probs1 = probabilities(x_mx1, w_mx1)
+        descent0.append(sums0[:, D_TILES, :])
+        nc.scalar.activation(descent0[2], dw0[2][:], ACT.Copy, scale=-LR)
+        for j in range(1, D_TILES):
+            scatter_nv(0, j, sums0[:, place0[j], :])
+        for t in range(PACK):
+            on_gpsimd(labels1[:, t, :], probs1[t][:], labels1[:, t, :], ALU.subtract)
+        rate0 = roots(sums0[:, :D_TILES, :])
         for j in range(D_TILES):
-            nc.vector.tensor_copy(nv[:, j, :], v_source[j][:].indirect(offsets[:]))
-        add_squares(0, dw0)
+            finish_rate(rate0, place0[j])
 
-        x_mx1 = quantize_x(1, x_raw1, nc.scalar.copy, "stage_b", "v2_buffer")
-        residual(x_mx1, w_mx1, labels1, on_gpsimd)
-        last = D_TILES - 1
-        rate0 = roots(0)
-        descent0 = [step_factors(rate0, dw0, j) for j in range(last)]
-        xm_mx1 = quantize(interleave(nc.scalar.copy, xm_raw1[:], "stage_d"), E4M3, "xm1", "xm1_codes")
-        g_mx1 = quantize_g(1, labels1, "xm_buffer", "stage_c", "g1_codes")
+        g_planes1 = work.tile([P, PACK, N], BF16, name="g_planes1", tag="g0_planes", align_bytes=MX_ALIGN)
+        for t in range(PACK):
+            nc.scalar.activation(g_planes1[:, t, :], labels1[:, t, :], ACT.Copy, scale=row_weight[1][:, t : t + 1])
+        for j in range(last):
+            scatter_step(0, j, descent0[j], rate0[:, place0[j], :])
+        xm_mx1 = quantize(interleave(nc.scalar.copy if XM1 == "S" else gp_copy, xm_raw1[:], "stage_d"), E4M3, "xm1", "xm1_codes")
+        g_mx1 = quantize(interleave(nc.scalar.copy, g_planes1[:], "stage_c"), E5M2, "g1", "g1_codes")
+        last_descent = work.tile([P, N], F32, name="last_descent", tag="g0_planes", align_bytes=MX_ALIGN)
+        nc.scalar.activation(last_descent[:], dw0[last][:], ACT.Copy, scale=-LR)
         dw1 = product(xm_mx1, g_mx1, E5M2)
-        finish_rate(rate0, last)
-        last_descent = work.tile([P, N], F32, name="last_descent", tag="xm_buffer", align_bytes=MX_ALIGN)
-        descent0.append(copy_descent(last_descent, dw0[last]))
-        add_squares(1, dw1)
+        scatter_step(0, last, last_descent, rate0[:, place0[last], :])
+        sums1 = work.tile([P, D_TILES + 1, N], F32, name="sums1", tag="w_listed")
+        for j in range(D_TILES):
+            square_of(sums1[:, j + 1, :], dw1[j])
+            add = nc.vector.tensor_tensor if j == 0 else on_gpsimd
+            add(sums1[:, j, :], nv[:, j, group_cols(1)], sums1[:, j + 1, :], ALU.add)
 
+        descent1 = [copy_descent(dw1[j], "f32_ring") for j in range(D_TILES)]
+        rate1 = roots(sums1[:, :D_TILES, :])
         for j in range(D_TILES):
-            scatter_nv(0, j)
+            finish_rate(rate1, j)
         for j in range(D_TILES):
-            scatter_step(0, j, descent0[j], rate0)
-
-        rate1 = roots(1)
-        descent1 = [step_factors(rate1, dw1, j) for j in range(D_TILES)]
-        for j in range(D_TILES):
-            scatter_nv(1, j)
+            scatter_nv(1, j, sums1[:, j, :])
             nc.sync.dma_start(out_1[tile_rows(j), :], nv_table[j][:])
         for j in range(D_TILES):
-            scatter_step(1, j, descent1[j], rate1)
+            scatter_step(1, j, descent1[j], rate1[:, j, :])
             nc.sync.dma_start(out_0[tile_rows(j), :], step_table[j][:])

@@ -44,8 +44,9 @@ def tile_attend_gnce_ada_kernel(tc, xT, wT, y, wt, xm, vT, offs, out_0, out_1):
 
         offsets = held.tile([P, B * LIST_COLS], U16, name="offsets")
         nc.sync.dma_start(offsets[:], offs)
-        row_weight = [held.tile([P, PACK], F32, name=f"row_weight{b}") for b in range(B)]
-        nv_table = [held.tile([P, T], F32, name=f"nv_table{j}") for j in range(D_TILES)]
+        row_weight = held.tile([P, B, PACK], F32, name="row_weight")
+        nc.scalar.dma_start(row_weight[:], wt.rearrange("b (p t) o -> p b (t o)", t=PACK))
+        nv_table = [held.tile([P, T], F32, name=f"nv_table{j}") for j in range(D_TILES - 1)]
         last = D_TILES - 1
 
         def group_list(b):
@@ -70,14 +71,10 @@ def tile_attend_gnce_ada_kernel(tc, xT, wT, y, wt, xm, vT, offs, out_0, out_1):
         def load_planes(matrix, tag):
             return load(work.tile([P, PACK, COLS], F32, name="raw", tag=tag, align_bytes=MX_ALIGN), as_planes(matrix))
 
-        def load_row_weight(b):
-            load(row_weight[b], wt[b].rearrange("(p t) o -> p (t o)", t=PACK))
-
         w_rows = wT.rearrange("(p t) c -> p t c", t=PACK)
         w_plane = [load_table(w_rows[:, t, :]) for t in range(PACK)]
         x_raw0 = load_planes(xT[0], "x_buffer")
         v_source = [load_table(vT[tile_rows(0), :])]
-        load_row_weight(0)
         labels0 = load_planes(y[0], "y_buffer")
         v_source.append(load_table(vT[tile_rows(1), :]))
         xm_raw0 = load_planes(xm[0], "xm_buffer")
@@ -100,7 +97,7 @@ def tile_attend_gnce_ada_kernel(tc, xT, wT, y, wt, xm, vT, offs, out_0, out_1):
 
         def interleave(copy, planes, tag):
             staged = staged_tile(tag)
-            copy(staged[:].rearrange("p (c t) -> p c t", t=PACK), planes.rearrange("p t c -> p c t"))
+            copy(staged[:].rearrange("p (c i t) -> p c t i", t=PACK, i=4), planes.rearrange("p t (c i) -> p c t i", i=4))
             return staged
 
         def mx_tiles(name, codes_tag):
@@ -158,15 +155,23 @@ def tile_attend_gnce_ada_kernel(tc, xT, wT, y, wt, xm, vT, offs, out_0, out_1):
 
         def roots(sums):
             rate = work.tile([P, D_TILES, N], F32, name="rate", align_bytes=MX_ALIGN)
-            nc.scalar.activation(rate[:], sums, ACT.Ln if LN else ACT.Sqrt)
+            for j in range(0, D_TILES, 2):
+                nc.scalar.activation(rate[:, j : j + 2, :], sums[:, j : j + 2, :], ACT.Sqrt)
             return rate
 
-        def finish_rate(rate, j):
-            if LN:
-                nc.scalar.activation(rate[:, j, :], rate[:, j, :], ACT.Sigmoid)
-                return
+        def square_rate(rate, j):
             nc.scalar.activation(rate[:, j, :], rate[:, j, :], ACT.Square, bias=EPS)
+
+        def invert_rate(rate, j):
             nc.scalar.activation(rate[:, j, :], rate[:, j, :], ACT.Abs_reciprocal_sqrt)
+
+        def finish_rates(rate):
+            square_rate(rate, 0)
+            invert_rate(rate, 0)
+            for j in range(1, D_TILES):
+                square_rate(rate, j)
+            for j in range(1, D_TILES):
+                invert_rate(rate, j)
 
         def copy_descent(dw_bank, tag):
             descent = work.tile([P, N], F32, name="descent", tag=tag, bufs=4 if tag == "f32_ring" else 1)
@@ -212,27 +217,31 @@ def tile_attend_gnce_ada_kernel(tc, xT, wT, y, wt, xm, vT, offs, out_0, out_1):
         logits0 = product(x_mx0, w_mx0, E4M3)
         w_mx1 = quantize(w_staged[1], E4M3, "w1", "stage_c")
         g_planes0 = work.tile([P, PACK, N], BF16, name="g_planes0", tag="g0_planes", align_bytes=MX_ALIGN)
+        weighted = [work.tile([P, N], F32, name="weighted", tag="f32_ring", bufs=4) for t in range(PACK)]
+        probs0 = [work.tile([P, N], F32, name="prob0")[:]] + [labels0[:, t, :] for t in range(PACK - 1)]
+
+        def weigh_labels(t):
+            nc.scalar.activation(weighted[t][:], labels0[:, t, :], ACT.Copy, scale=row_weight[:, 0, t : t + 1])
+
+        nc.scalar.activation(probs0[0], logits0[0][:], ACT.Sigmoid)
+        weigh_labels(0)
         for t in range(PACK):
-            weight = row_weight[0][:, t : t + 1]
-            prob = work.tile([P, N], F32, name="prob", tag="f32_ring", bufs=4)
-            nc.scalar.activation(prob[:], logits0[t][:], ACT.Sigmoid)
-            if YW == "S":
-                nc.scalar.activation(labels0[:, t, :], labels0[:, t, :], ACT.Copy, scale=weight)
-            else:
-                for c in range(0, N, 256):
-                    nc.gpsimd.tensor_scalar(labels0[:, t, c : c + 256], labels0[:, t, c : c + 256], weight, 0.0, ALU.mult, ALU.add)
-            nc.vector.scalar_tensor_tensor(g_planes0[:, t, :], prob[:], weight, labels0[:, t, :], ALU.mult, ALU.subtract)
-            if t == 0:
+            if t > 0:
+                nc.scalar.activation(probs0[t], logits0[t][:], ACT.Sigmoid)
+            if t + 1 < PACK:
+                weigh_labels(t + 1)
+            nc.vector.scalar_tensor_tensor(
+                g_planes0[:, t, :], probs0[t], row_weight[:, 0, t : t + 1], weighted[t][:], ALU.mult, ALU.subtract
+            )
+            if t == 1:
                 gather_v(1)
 
         x_raw1 = load_planes(xT[1], "x_buffer")
         v_source.append(load(work.tile([P, T], F32, name="v2_buffer", align_bytes=MX_ALIGN), vT[tile_rows(2), :]))
-        load_nv_table(0)
-        load_row_weight(1)
         load_v(3)
+        load_nv_table(0)
         load_nv_table(1)
         load_nv_table(2)
-        load_nv_table(3)
         labels1 = load_planes(y[1], "y_buffer")
 
         xm_staged0 = interleave(nc.scalar.copy, xm_raw0[:], "stage_d")
@@ -260,49 +269,50 @@ def tile_attend_gnce_ada_kernel(tc, xT, wT, y, wt, xm, vT, offs, out_0, out_1):
         def add_square(add, b, j, square):
             add(nv[:, j, group_cols(b)], nv[:, j, group_cols(b)], square[j], ALU.add)
 
-        square0 = [square_of(work.tile([P, N], F32, name="square", bufs=D_TILES)[:], dw0[0])]
-        nc.vector.tensor_tensor(nv_table[0][:].indirect(group_list(0)), nv[:, 0, group_cols(0)], square0[0], ALU.add)
-        sums0 = work.tile([P, D_TILES + 1, N], F32, name="sums0", tag="stage_b", align_bytes=MX_ALIGN)
-        for j in range(1, D_TILES):
-            square0.append(square_of(sums0[:, j, :], dw0[j]))
+        squares0 = work.tile([P, D_TILES, N], F32, name="squares0")
+        for j in range(D_TILES):
+            square_of(squares0[:, j, :], dw0[j])
+        sums0 = work.tile([P, D_TILES, N], F32, name="sums0", tag="stage_b", align_bytes=MX_ALIGN)
         gather_v(3)
-        place0 = [1, 0, 2, 3]
+        place0 = [0, 1, 2, 3]
         for j in place0:
-            on_gpsimd(sums0[:, place0[j], :], nv[:, j, group_cols(0)], square0[j], ALU.add)
+            on_gpsimd(sums0[:, j, :], nv[:, j, group_cols(0)], squares0[:, j, :], ALU.add)
 
         descent0 = [copy_descent(dw0[j], f"descent0{j}") for j in range(2)]
         probs1 = probabilities(x_mx1, w_mx1)
-        descent0.append(sums0[:, D_TILES, :])
-        nc.scalar.activation(descent0[2], dw0[2][:], ACT.Copy, scale=-LR)
-        for j in range(1, D_TILES):
+        for j in range(last):
             scatter_nv(0, j, sums0[:, place0[j], :])
         for t in range(PACK):
             on_gpsimd(labels1[:, t, :], probs1[t][:], labels1[:, t, :], ALU.subtract)
-        rate0 = roots(sums0[:, :D_TILES, :])
-        for j in range(D_TILES):
-            finish_rate(rate0, place0[j])
+        rate0 = roots(sums0)
+        later = work.tile([P, 2, N], F32, name="later", tag="squares0")
+        descent0.append(later[:, 0, :])
+        finish_rates(rate0)
+        for j in range(2, D_TILES):
+            nc.scalar.activation(later[:, j - 2, :], dw0[j][:], ACT.Copy, scale=-LR)
 
         g_planes1 = work.tile([P, PACK, N], BF16, name="g_planes1", tag="g0_planes", align_bytes=MX_ALIGN)
         for t in range(PACK):
-            nc.scalar.activation(g_planes1[:, t, :], labels1[:, t, :], ACT.Copy, scale=row_weight[1][:, t : t + 1])
+            nc.scalar.activation(g_planes1[:, t, :], labels1[:, t, :], ACT.Copy, scale=row_weight[:, 1, t : t + 1])
         for j in range(last):
             scatter_step(0, j, descent0[j], rate0[:, place0[j], :])
         xm_mx1 = quantize(interleave(nc.scalar.copy if XM1 == "S" else gp_copy, xm_raw1[:], "stage_d"), E4M3, "xm1", "xm1_codes")
+        nv_table.append(work.tile([P, T], F32, name="nv_table3", tag="y_buffer", align_bytes=MX_ALIGN))
+        load_nv_table(last)
         g_mx1 = quantize(interleave(nc.scalar.copy, g_planes1[:], "stage_c"), E5M2, "g1", "g1_codes")
-        last_descent = work.tile([P, N], F32, name="last_descent", tag="g0_planes", align_bytes=MX_ALIGN)
-        nc.scalar.activation(last_descent[:], dw0[last][:], ACT.Copy, scale=-LR)
         dw1 = product(xm_mx1, g_mx1, E5M2)
-        scatter_step(0, last, last_descent, rate0[:, place0[last], :])
-        sums1 = work.tile([P, D_TILES + 1, N], F32, name="sums1", tag="w_listed")
+        last_step = work.tile([P, N], F32, name="last_step", tag="stage_c", align_bytes=MX_ALIGN)
+        on_gpsimd(last_step[:], later[:, 1, :], rate0[:, last, :], ALU.mult)
+        scatter_nv(0, last, sums0[:, last, :])
+        nc.vector.tensor_copy(step_table[last][:].indirect(group_list(0)), last_step[:])
+        sums1 = work.tile([P, D_TILES, N], F32, name="sums1", tag="w_listed")
         for j in range(D_TILES):
-            square_of(sums1[:, j + 1, :], dw1[j])
-            add = nc.vector.tensor_tensor if j == 0 else on_gpsimd
-            add(sums1[:, j, :], nv[:, j, group_cols(1)], sums1[:, j + 1, :], ALU.add)
+            square_of(sums1[:, j, :], dw1[j])
+            on_gpsimd(sums1[:, j, :], nv[:, j, group_cols(1)], sums1[:, j, :], ALU.add)
 
         descent1 = [copy_descent(dw1[j], "f32_ring") for j in range(D_TILES)]
-        rate1 = roots(sums1[:, :D_TILES, :])
-        for j in range(D_TILES):
-            finish_rate(rate1, j)
+        rate1 = roots(sums1)
+        finish_rates(rate1)
         for j in range(D_TILES):
             scatter_nv(1, j, sums1[:, j, :])
             nc.sync.dma_start(out_1[tile_rows(j), :], nv_table[j][:])

@@ -224,16 +224,17 @@ def tile_attend_gnce_ada_kernel(tc, xT, wT, y, wt, xm, vT, offs, out_0, out_1):
             nc.scalar.activation(weighted[t][:], labels0[:, t, :], ACT.Copy, scale=row_weight[:, 0, t : t + 1])
 
         nc.scalar.activation(probs0[0], logits0[0][:], ACT.Sigmoid)
-        weigh_labels(0)
+        for t in range(PACK):
+            weigh_labels(t)
         for t in range(PACK):
             if t > 0:
                 nc.scalar.activation(probs0[t], logits0[t][:], ACT.Sigmoid)
-            if t + 1 < PACK:
-                weigh_labels(t + 1)
-            nc.vector.scalar_tensor_tensor(
-                g_planes0[:, t, :], probs0[t], row_weight[:, 0, t : t + 1], weighted[t][:], ALU.mult, ALU.subtract
-            )
-            if t == 1:
+            for c in range(0, N, N // 2 if t == PACK - 1 else N):
+                cols = slice(c, c + N // 2) if t == PACK - 1 else slice(0, N)
+                nc.vector.scalar_tensor_tensor(
+                    g_planes0[:, t, cols], probs0[t][:, cols], row_weight[:, 0, t : t + 1], weighted[t][:, cols], ALU.mult, ALU.subtract
+                )
+            if t == 0:
                 gather_v(1)
 
         x_raw1 = load_planes(xT[1], "x_buffer")
@@ -241,13 +242,21 @@ def tile_attend_gnce_ada_kernel(tc, xT, wT, y, wt, xm, vT, offs, out_0, out_1):
         load_v(3)
         load_nv_table(0)
         load_nv_table(1)
+        labels1 = work.tile([P, PACK, N], F32, name="labels1", tag="y_buffer", align_bytes=MX_ALIGN)
+        nc.sync.dma_start(labels1[:, :2, :], as_planes(y[1])[:, :2, :])
         load_nv_table(2)
-        labels1 = load_planes(y[1], "y_buffer")
+        nc.sync.dma_start(labels1[:, 2:, :], as_planes(y[1])[:, 2:, :])
 
         xm_staged0 = interleave(nc.scalar.copy, xm_raw0[:], "stage_d")
         xm_mx0 = quantize(xm_staged0, E4M3, "xm0", "xm0_codes")
         if GS == 512:
-            g_mx0 = quantize(interleave(nc.vector.tensor_copy, g_planes0[:], "stage_a"), E5M2, "g0", "xm_buffer")
+            g_staged0 = staged_tile("stage_a")
+            for c in range(0, N, N // 2):
+                nc.vector.tensor_copy(
+                    g_staged0[:, c * PACK : (c + N // 2) * PACK].rearrange("p (c i t) -> p c t i", t=PACK, i=4),
+                    g_planes0[:, :, c : c + N // 2].rearrange("p t (c i) -> p c t i", i=4),
+                )
+            g_mx0 = quantize(g_staged0, E5M2, "g0", "xm_buffer")
         else:
             g_mx0 = mx_tiles("g0", "g0_codes")
             for copy, tag, c0, c1 in ((nc.vector.tensor_copy, "stage_a", 0, GS), (nc.scalar.copy, "xm_buffer", GS, N)):
@@ -294,21 +303,21 @@ def tile_attend_gnce_ada_kernel(tc, xT, wT, y, wt, xm, vT, offs, out_0, out_1):
         g_planes1 = work.tile([P, PACK, N], BF16, name="g_planes1", tag="g0_planes", align_bytes=MX_ALIGN)
         for t in range(PACK):
             nc.scalar.activation(g_planes1[:, t, :], labels1[:, t, :], ACT.Copy, scale=row_weight[:, 1, t : t + 1])
-        for j in range(last):
+        descent0.append(later[:, 1, :])
+        for j in range(D_TILES):
             scatter_step(0, j, descent0[j], rate0[:, place0[j], :])
         xm_mx1 = quantize(interleave(nc.scalar.copy if XM1 == "S" else gp_copy, xm_raw1[:], "stage_d"), E4M3, "xm1", "xm1_codes")
         nv_table.append(work.tile([P, T], F32, name="nv_table3", tag="y_buffer", align_bytes=MX_ALIGN))
         load_nv_table(last)
         g_mx1 = quantize(interleave(nc.scalar.copy, g_planes1[:], "stage_c"), E5M2, "g1", "g1_codes")
         dw1 = product(xm_mx1, g_mx1, E5M2)
-        last_step = work.tile([P, N], F32, name="last_step", tag="stage_c", align_bytes=MX_ALIGN)
-        on_gpsimd(last_step[:], later[:, 1, :], rate0[:, last, :], ALU.mult)
         scatter_nv(0, last, sums0[:, last, :])
-        nc.vector.tensor_copy(step_table[last][:].indirect(group_list(0)), last_step[:])
         sums1 = work.tile([P, D_TILES, N], F32, name="sums1", tag="w_listed")
         for j in range(D_TILES):
-            square_of(sums1[:, j, :], dw1[j])
-            on_gpsimd(sums1[:, j, :], nv[:, j, group_cols(1)], sums1[:, j, :], ALU.add)
+            for c in range(0, N, N // 2 if j == 0 else N):
+                cols = slice(c, c + N // 2) if j == 0 else slice(0, N)
+                nc.scalar.activation(sums1[:, j, cols], dw1[j][:, cols], ACT.Square)
+                nc.gpsimd.tensor_tensor(sums1[:, j, cols], nv[:, j, group_cols(1)][:, cols], sums1[:, j, cols], ALU.add)
 
         descent1 = [copy_descent(dw1[j], "f32_ring") for j in range(D_TILES)]
         rate1 = roots(sums1)

@@ -97,7 +97,7 @@ def tile_attend_gnce_ada_kernel(tc, xT, wT, y, wt, xm, vT, offs, out_0, out_1):
 
         def interleave(copy, planes, tag):
             staged = staged_tile(tag)
-            copy(staged[:].rearrange("p (c i t) -> p c t i", t=PACK, i=4), planes.rearrange("p t (c i) -> p c t i", i=4))
+            copy(staged[:].rearrange("p (c t) -> p c t", t=PACK), planes.rearrange("p t c -> p c t"))
             return staged
 
         def mx_tiles(name, codes_tag):
@@ -253,8 +253,8 @@ def tile_attend_gnce_ada_kernel(tc, xT, wT, y, wt, xm, vT, offs, out_0, out_1):
             g_staged0 = staged_tile("stage_a")
             for c in range(0, N, N // 2):
                 nc.vector.tensor_copy(
-                    g_staged0[:, c * PACK : (c + N // 2) * PACK].rearrange("p (c i t) -> p c t i", t=PACK, i=4),
-                    g_planes0[:, :, c : c + N // 2].rearrange("p t (c i) -> p c t i", i=4),
+                    g_staged0[:, c * PACK : (c + N // 2) * PACK].rearrange("p (c t) -> p c t", t=PACK),
+                    g_planes0[:, :, c : c + N // 2].rearrange("p t c -> p c t"),
                 )
             g_mx0 = quantize(g_staged0, E5M2, "g0", "xm_buffer")
         else:

@@ -82,7 +82,7 @@ def tile_attend_gnce_ada_kernel(tc, xT, wT, y, wt, xm, vT, offs, out_0, out_1):
         step_table = []
         for j in range(D_TILES):
             step_table.append(work.tile([P, T], F32, name=f"step_table{j}", align_bytes=MX_ALIGN))
-            nc.gpsimd.memset(step_table[j][:].bitcast(U32), 0)
+            nc.vector.memset(step_table[j][:].bitcast(U32), 0)
 
         w_listed = work.tile([P, PACK, B * N], F32, name="w_listed")
         nv = held.tile([P, D_TILES, B * N], F32, name="nv")

@@ -45,7 +45,6 @@ def tile_attend_gnce_ada_kernel(tc, xT, wT, y, wt, xm, vT, offs, out_0, out_1):
         offsets = held.tile([P, B * LIST_COLS], U16, name="offsets")
         nc.sync.dma_start(offsets[:], offs)
         row_weight = held.tile([P, B, PACK], F32, name="row_weight")
-        nc.scalar.dma_start(row_weight[:], wt.rearrange("b (p t) o -> p b (t o)", t=PACK))
         nv_table = [held.tile([P, T], F32, name=f"nv_table{j}") for j in range(D_TILES - 1)]
         last = D_TILES - 1
 
@@ -75,8 +74,9 @@ def tile_attend_gnce_ada_kernel(tc, xT, wT, y, wt, xm, vT, offs, out_0, out_1):
         w_plane = [load_table(w_rows[:, t, :]) for t in range(PACK)]
         x_raw0 = load_planes(xT[0], "x_buffer")
         v_source = [load_table(vT[tile_rows(0), :])]
-        labels0 = load_planes(y[0], "y_buffer")
         v_source.append(load_table(vT[tile_rows(1), :]))
+        load(row_weight, wt.rearrange("b (p t) o -> p b (t o)", t=PACK))
+        labels0 = load_planes(y[0], "y_buffer")
         xm_raw0 = load_planes(xm[0], "xm_buffer")
 
         step_table = []
@@ -217,25 +217,18 @@ def tile_attend_gnce_ada_kernel(tc, xT, wT, y, wt, xm, vT, offs, out_0, out_1):
         logits0 = product(x_mx0, w_mx0, E4M3)
         w_mx1 = quantize(w_staged[1], E4M3, "w1", "stage_c")
         g_planes0 = work.tile([P, PACK, N], BF16, name="g_planes0", tag="g0_planes", align_bytes=MX_ALIGN)
-        weighted = [work.tile([P, N], F32, name="weighted", tag="f32_ring", bufs=4) for t in range(PACK)]
-        probs0 = [work.tile([P, N], F32, name="prob0")[:]] + [labels0[:, t, :] for t in range(PACK - 1)]
-
-        def weigh_labels(t):
-            nc.scalar.activation(weighted[t][:], labels0[:, t, :], ACT.Copy, scale=row_weight[:, 0, t : t + 1])
-
-        nc.scalar.activation(probs0[0], logits0[0][:], ACT.Sigmoid)
+        gather_v(1)
+        probs0 = [work.tile([P, N], F32, name="prob", tag="f32_ring", bufs=4) for t in range(PACK)]
         for t in range(PACK):
-            weigh_labels(t)
+            nc.scalar.activation(probs0[t][:], logits0[t][:], ACT.Sigmoid)
         for t in range(PACK):
-            if t > 0:
-                nc.scalar.activation(probs0[t], logits0[t][:], ACT.Sigmoid)
+            weight = row_weight[:, 0, t : t + 1]
+            nc.scalar.activation(labels0[:, t, :], labels0[:, t, :], ACT.Copy, scale=weight)
             for c in range(0, N, N // 2 if t == PACK - 1 else N):
                 cols = slice(c, c + N // 2) if t == PACK - 1 else slice(0, N)
                 nc.vector.scalar_tensor_tensor(
-                    g_planes0[:, t, cols], probs0[t][:, cols], row_weight[:, 0, t : t + 1], weighted[t][:, cols], ALU.mult, ALU.subtract
+                    g_planes0[:, t, cols], probs0[t][:, cols], weight, labels0[:, t, cols], ALU.mult, ALU.subtract
                 )
-            if t == 0:
-                gather_v(1)
 
         x_raw1 = load_planes(xT[1], "x_buffer")
         v_source.append(load(work.tile([P, T], F32, name="v2_buffer", align_bytes=MX_ALIGN), vT[tile_rows(2), :]))

@@ -1,6 +1,7 @@
 from contextlib import ExitStack
 
 import concourse.mybir as mybir
+from concourse.masks import make_identity
 
 B, N, T, D, R = 2, 512, 2048, 512, 512
 LR = 0.1
@@ -218,6 +219,8 @@ def tile_attend_gnce_ada_kernel(tc, xT, wT, y, wt, xm, vT, offs, out_0, out_1):
         w_mx1 = quantize(w_staged[1], E4M3, "w1", "stage_c")
         g_planes0 = work.tile([P, PACK, N], BF16, name="g_planes0", tag="g0_planes", align_bytes=MX_ALIGN)
         gather_v(1)
+        identity = work.tile([P, P], F32, name="identity", tag="x0_codes", align_bytes=MX_ALIGN)
+        make_identity(nc, identity[:])
         probs0 = [work.tile([P, N], F32, name="prob", tag="f32_ring", bufs=4) for t in range(PACK)]
         for t in range(PACK):
             nc.scalar.activation(probs0[t][:], logits0[t][:], ACT.Sigmoid)
@@ -305,18 +308,28 @@ def tile_attend_gnce_ada_kernel(tc, xT, wT, y, wt, xm, vT, offs, out_0, out_1):
         g_mx1 = quantize(interleave(nc.scalar.copy, g_planes1[:], "stage_c"), E5M2, "g1", "g1_codes")
         dw1 = product(xm_mx1, g_mx1, E5M2)
         scatter_nv(0, last, sums0[:, last, :])
-        sums1 = work.tile([P, D_TILES, N], F32, name="sums1", tag="w_listed")
+        squares1 = work.tile([P, D_TILES, N], F32, name="squares1", tag="w_listed")
         for j in range(D_TILES):
-            for c in range(0, N, N // 2 if j == 0 else N):
-                cols = slice(c, c + N // 2) if j == 0 else slice(0, N)
-                nc.scalar.activation(sums1[:, j, cols], dw1[j][:, cols], ACT.Square)
-                nc.gpsimd.tensor_tensor(sums1[:, j, cols], nv[:, j, group_cols(1)][:, cols], sums1[:, j, cols], ALU.add)
-
+            square_of(squares1[:, j, :], dw1[j])
         descent1 = [copy_descent(dw1[j], "f32_ring") for j in range(D_TILES)]
-        rate1 = roots(sums1)
-        finish_rates(rate1)
+        blocks = [slice(i * P, (i + 1) * P) for i in range(N // P)]
+        turned_roots = work.tile([P, D_TILES, N], F32, name="turned_roots", tag="squares0")
         for j in range(D_TILES):
-            scatter_nv(1, j, sums1[:, j, :])
+            turned_sums = psum.tile([P, N], F32, name="bank")
+            for cols in blocks:
+                nc.tensor.matmul(turned_sums[:, cols], lhsT=nv[:, j, group_cols(1)][:, cols], rhs=identity[:], start=True, stop=False, is_transpose=True)
+                nc.tensor.matmul(turned_sums[:, cols], lhsT=squares1[:, j, cols], rhs=identity[:], start=False, stop=True, is_transpose=True)
+            nc.scalar.activation(turned_roots[:, j, :], turned_sums[:], ACT.Sqrt)
+        rate1 = work.tile([P, D_TILES, N], F32, name="rate", align_bytes=MX_ALIGN)
+        for j in range(D_TILES):
+            root = psum.tile([P, N], F32, name="bank")
+            for cols in blocks:
+                nc.tensor.transpose(root[:, cols], turned_roots[:, j, cols], identity[:])
+            nc.scalar.activation(rate1[:, j, :], root[:], ACT.Square, bias=EPS)
+        for j in range(D_TILES):
+            invert_rate(rate1, j)
+        for j in range(D_TILES):
+            nc.vector.tensor_tensor(nv_table[j][:].indirect(group_list(1)), nv[:, j, group_cols(1)], squares1[:, j, :], ALU.add)
             nc.sync.dma_start(out_1[tile_rows(j), :], nv_table[j][:])
         for j in range(D_TILES):
             scatter_step(1, j, descent1[j], rate1[:, j, :])

@@ -1,3 +1,4 @@
+import math
 from contextlib import ExitStack
 
 import concourse.mybir as mybir
@@ -18,36 +19,27 @@ E5M2 = mybir.dt.float8_e5m2_x4
 ACT = mybir.ActivationFunctionType
 ALU = mybir.AluOpType
 
-ORDER = 1
-YW = "S"
-GS = 512
-X1 = "S"
-XM1 = "S"
-LN = 0
-VS = 0
 P = 128
 PACK = 4
 COLS = 512
+HALF = COLS // 2
 D_TILES = D // P
+LAST = D_TILES - 1
 LIST_COLS = N // 16
 MX_ALIGN = 64
-LOAD_BUFS = 5
-GPSIMD_COLS = 512
+TABLE_BUFS = 6
 
 
 def tile_attend_gnce_ada_kernel(tc, xT, wT, y, wt, xm, vT, offs, out_0, out_1):
     nc = tc.nc
     with ExitStack() as ctx:
         held = ctx.enter_context(tc.tile_pool(name="held", bufs=1))
-        loads = ctx.enter_context(tc.tile_pool(name="loads", bufs=LOAD_BUFS))
+        tables = ctx.enter_context(tc.tile_pool(name="tables", bufs=TABLE_BUFS))
         work = ctx.enter_context(tc.tile_pool(name="work", bufs=1))
         psum = ctx.enter_context(tc.psum_pool(name="psum", bufs=8))
 
-        offsets = held.tile([P, B * LIST_COLS], U16, name="offsets")
-        nc.sync.dma_start(offsets[:], offs)
-        row_weight = held.tile([P, B, PACK], F32, name="row_weight")
-        nv_table = [held.tile([P, T], F32, name=f"nv_table{j}") for j in range(D_TILES - 1)]
-        last = D_TILES - 1
+        def buffer(shape, dtype, tag):
+            return work.tile(shape, dtype, name=tag, tag=tag, align_bytes=MX_ALIGN)
 
         def group_list(b):
             return offsets[:, b * LIST_COLS : (b + 1) * LIST_COLS]
@@ -63,274 +55,218 @@ def tile_attend_gnce_ada_kernel(tc, xT, wT, y, wt, xm, vT, offs, out_0, out_1):
             return tile
 
         def load_table(rows):
-            return load(loads.tile([P, T], F32, name="loaded"), rows)
+            return load(tables.tile([P, T], F32, name="table"), rows)
+
+        def load_v(j):
+            return load_table(vT[tile_rows(j), :])
 
         def as_planes(matrix):
             return matrix.rearrange("(p t) c -> p t c", t=PACK)
 
-        def load_planes(matrix, tag):
-            return load(work.tile([P, PACK, COLS], F32, name="raw", tag=tag, align_bytes=MX_ALIGN), as_planes(matrix))
+        def load_planes(planes, tag):
+            return load(buffer(list(planes.shape), F32, tag), planes)
 
-        w_rows = wT.rearrange("(p t) c -> p t c", t=PACK)
-        w_plane = [load_table(w_rows[:, t, :]) for t in range(PACK)]
-        x_raw0 = load_planes(xT[0], "x_buffer")
-        v_source = [load_table(vT[tile_rows(0), :])]
-        v_source.append(load_table(vT[tile_rows(1), :]))
-        load(row_weight, wt.rearrange("b (p t) o -> p b (t o)", t=PACK))
-        labels0 = load_planes(y[0], "y_buffer")
-        xm_raw0 = load_planes(xm[0], "xm_buffer")
+        def interleave(copy, staged, planes):
+            copy(staged.rearrange("p (c t) -> p c t", t=PACK), planes.rearrange("p t c -> p c t"))
 
-        step_table = []
-        for j in range(D_TILES):
-            step_table.append(work.tile([P, T], F32, name=f"step_table{j}", align_bytes=MX_ALIGN))
-            nc.vector.memset(step_table[j][:].bitcast(U32), 0)
-
-        w_listed = work.tile([P, PACK, B * N], F32, name="w_listed")
-        nv = held.tile([P, D_TILES, B * N], F32, name="nv")
-
-        def on_gpsimd(out, in0, in1, op):
-            for c in range(0, N, GPSIMD_COLS):
-                cols = slice(c, c + GPSIMD_COLS)
-                nc.gpsimd.tensor_tensor(out[:, cols], in0[:, cols], in1[:, cols], op)
-
-        def staged_tile(tag):
-            return work.tile([P, COLS * PACK], BF16, name="staged", tag=tag, align_bytes=MX_ALIGN)
-
-        def interleave(copy, planes, tag):
-            staged = staged_tile(tag)
-            copy(staged[:].rearrange("p (c t) -> p c t", t=PACK), planes.rearrange("p t c -> p c t"))
+        def interleaved(copy, planes, tag):
+            staged = buffer([P, planes.shape[2] * PACK], BF16, tag)
+            interleave(copy, staged[:], planes)
             return staged
 
-        def mx_tiles(name, codes_tag):
-            codes = work.tile([P, COLS], U32, name=name + "_codes", tag=codes_tag, align_bytes=MX_ALIGN)
-            scales = held.tile([P, COLS], U8, name=name + "_scales", align_bytes=MX_ALIGN)
-            return codes, scales
-
-        def quantize(staged, fmt, name, codes_tag):
-            codes, scales = mx_tiles(name, codes_tag)
-            nc.vector.quantize_mx(out=codes[:].bitcast(fmt), scales=scales[:], in_=staged[:])
-            return codes, scales
-
-        def stage_x(x_raw, copy, stage_tag):
-            staged = staged_tile(stage_tag)
+        def dealt(copy, x_raw, tag):
+            staged = buffer([P, COLS * PACK], BF16, tag)
             copy(
                 staged[:].rearrange("p (t m k) -> p m t k", t=PACK, k=PACK),
                 x_raw[:].rearrange("p k (m t) -> p m t k", t=PACK),
             )
             return staged
 
-        def multiply(stationary, i, moving, moving_fmt):
-            bank = psum.tile([P, COLS], F32, name="bank")
-            nc.tensor.matmul_mx(
-                out=bank[:],
-                lhsT=stationary[0][:, i * P : (i + 1) * P].bitcast(E4M3),
-                lhsT_scale=stationary[1][:, i * P : (i + 1) * P],
-                rhs=moving[0][:].bitcast(moving_fmt),
-                rhs_scale=moving[1][:],
-                start=True,
-                stop=True,
-            )
-            return bank
+        def quantize(staged, fmt, name, codes_tag):
+            words = staged.shape[1] // PACK
+            codes = buffer([P, words], U32, codes_tag)
+            scales = held.tile([P, words], U8, name=name + "_scales", align_bytes=MX_ALIGN)
+            nc.vector.quantize_mx(out=codes[:].bitcast(fmt), scales=scales[:], in_=staged[:])
+            return codes, scales
 
         def product(stationary, moving, moving_fmt):
-            return [multiply(stationary, i, moving, moving_fmt) for i in range(COLS // P)]
+            banks = []
+            for i in range(stationary[0].shape[1] // P):
+                banks.append(psum.tile([P, COLS], F32, name="bank"))
+                nc.tensor.matmul_mx(
+                    out=banks[i][:],
+                    lhsT=stationary[0][:, i * P : (i + 1) * P].bitcast(E4M3),
+                    lhsT_scale=stationary[1][:, i * P : (i + 1) * P],
+                    rhs=moving[0][:].bitcast(moving_fmt),
+                    rhs_scale=moving[1][:],
+                    start=True,
+                    stop=True,
+                )
+            return banks
 
-        def probabilities(x_mx, w_mx):
-            logits = product(x_mx, w_mx, E4M3)
-            probs = []
-            for t in range(PACK):
-                probs.append(work.tile([P, N], F32, name="prob", tag="f32_ring", bufs=4))
-                nc.scalar.activation(probs[t][:], logits[t][:], ACT.Sigmoid)
-            return probs
+        def gather_v(source, tag):
+            listed = buffer([P, B * N], F32, tag)
+            nc.vector.tensor_copy(listed[:], source[:].indirect(offsets[:]))
+            return listed
 
-        def add_squares(b, dw):
-            for j in range(D_TILES):
-                square = work.tile([P, N], F32, name="square")
-                nc.scalar.activation(square[:], dw[j][:], ACT.Square)
-                on_gpsimd(nv[:, j, group_cols(b)], nv[:, j, group_cols(b)], square[:], ALU.add)
+        def square(out, dw_bank):
+            nc.scalar.activation(out, dw_bank[:], ACT.Square)
 
-        def gp_copy(out, in_):
-            n = out.shape[1] // 8
-            for c in range(8):
-                nc.gpsimd.tensor_scalar(out[:, c * n : (c + 1) * n], in_[:, c * n : (c + 1) * n], 1.0, 0.0, ALU.mult, ALU.add)
+        def descent(out, dw_bank):
+            nc.scalar.activation(out, dw_bank[:], ACT.Copy, scale=-LR / EPS)
 
-        def roots(sums):
-            rate = work.tile([P, D_TILES, N], F32, name="rate", align_bytes=MX_ALIGN)
-            for j in range(0, D_TILES, 2):
-                nc.scalar.activation(rate[:, j : j + 2, :], sums[:, j : j + 2, :], ACT.Sqrt)
-            return rate
-
-        def square_rate(rate, j):
-            nc.scalar.activation(rate[:, j, :], rate[:, j, :], ACT.Square, bias=EPS)
-
-        def invert_rate(rate, j):
-            nc.scalar.activation(rate[:, j, :], rate[:, j, :], ACT.Abs_reciprocal_sqrt)
-
-        def finish_rates(rate):
-            square_rate(rate, 0)
-            invert_rate(rate, 0)
-            for j in range(1, D_TILES):
-                square_rate(rate, j)
-            for j in range(1, D_TILES):
-                invert_rate(rate, j)
-
-        def copy_descent(dw_bank, tag):
-            descent = work.tile([P, N], F32, name="descent", tag=tag, bufs=4 if tag == "f32_ring" else 1)
-            nc.scalar.activation(descent[:], dw_bank[:], ACT.Copy, scale=-LR)
-            return descent
-
-        def gather_v(j):
-            if VS:
-                for b in range(B):
-                    nc.vector.tensor_copy(nv[:, j, group_cols(b)], v_source[j][:].indirect(group_list(b)))
-            else:
-                nc.vector.tensor_copy(nv[:, j, :], v_source[j][:].indirect(offsets[:]))
+        def rate(out, log_nv):
+            nc.scalar.activation(out, log_nv, ACT.Sigmoid, scale=-0.5, bias=math.log(EPS))
 
         def scatter_nv(b, j, values):
             nc.vector.tensor_copy(nv_table[j][:].indirect(group_list(b)), values)
 
-        def scatter_step(b, j, descent, rate):
-            nc.vector.tensor_tensor(step_table[j][:].indirect(group_list(b)), descent[:], rate, ALU.mult)
+        def scatter_sum(b, j, squares):
+            nc.vector.tensor_tensor(nv_table[j][:].indirect(group_list(b)), v_listed[j][:, group_cols(b)], squares, ALU.add)
 
+        def scatter_step(b, j, descents, rates):
+            nc.vector.tensor_tensor(step_table[j][:].indirect(group_list(b)), descents, rates, ALU.mult)
+
+        offsets = held.tile([P, B * LIST_COLS], U16, name="offsets")
+        nc.sync.dma_start(offsets[:], offs)
+        w_plane = [load_table(as_planes(wT)[:, t, :]) for t in range(PACK)]
+        x_raw0 = load_planes(as_planes(xT[0]), "x_raw")
+        v_source = [load_v(0)]
+        row_weight = load(held.tile([P, B, PACK], F32, name="row_weight"), wt.rearrange("b (p t) o -> p b (t o)", t=PACK))
+        v_source.append(load_v(1))
+        labels0 = [load_planes(as_planes(y[0])[:, t : t + 2, :], f"labels0_{t}") for t in range(0, PACK, 2)]
+        xm_raw0 = [load_planes(as_planes(xm[0])[:, :, c : c + HALF], f"xm_raw0_{c}") for c in range(0, D, HALF)]
+        v_source.append(load_v(2))
+        nv_table = [load_v(0), load_v(1)]
+
+        step_table = []
+        for j in range(D_TILES):
+            step_table.append(held.tile([P, T], F32, name=f"step_table{j}"))
+            nc.vector.memset(step_table[j][:].bitcast(U32), 0)
+
+        w_listed = buffer([P, PACK, B * N], F32, "w_listed")
         for t in range(PACK - 1):
             nc.vector.tensor_copy(w_listed[:, t, :], w_plane[t][:].indirect(offsets[:]))
         for b in range(B):
             nc.vector.tensor_copy(w_listed[:, PACK - 1, group_cols(b)], w_plane[PACK - 1][:].indirect(group_list(b)))
-
-        def load_v(j):
-            v_source.append(load_table(vT[tile_rows(j), :]))
-
-        def load_nv_table(j):
-            load(nv_table[j], vT[tile_rows(j), :])
-
-
-        w_staged = [staged_tile("stage_a"), staged_tile("stage_b")]
+        w_staged = [buffer([P, COLS * PACK], BF16, f"w_staged{b}") for b in range(B)]
         for t in range(0, PACK, 2):
             for b in range(B):
                 nc.scalar.copy(
                     w_staged[b][:].rearrange("p (c t) -> p c t", t=PACK)[:, :, t : t + 2],
                     w_listed[:, t : t + 2, group_cols(b)].rearrange("p t c -> p c t"),
                 )
-        x_staged0 = stage_x(x_raw0, nc.vector.tensor_copy, "stage_c")
-        w_mx0 = quantize(w_staged[0], E4M3, "w0", "x_buffer")
+        x_staged0 = dealt(nc.vector.tensor_copy, x_raw0, "x_staged0")
+        w_mx0 = quantize(w_staged[0], E4M3, "w0", "x_raw")
         x_mx0 = quantize(x_staged0, E4M3, "x0", "x0_codes")
-        gather_v(0)
+        v_listed = [gather_v(v_source[j], f"v_listed{j}") for j in range(2)]
         logits0 = product(x_mx0, w_mx0, E4M3)
-        w_mx1 = quantize(w_staged[1], E4M3, "w1", "stage_c")
-        g_planes0 = work.tile([P, PACK, N], BF16, name="g_planes0", tag="g0_planes", align_bytes=MX_ALIGN)
-        gather_v(1)
-        identity = work.tile([P, P], F32, name="identity", tag="x0_codes", align_bytes=MX_ALIGN)
+        identity = buffer([P, P], F32, "x0_codes")
         make_identity(nc, identity[:])
-        probs0 = [work.tile([P, N], F32, name="prob", tag="f32_ring", bufs=4) for t in range(PACK)]
+
+        half_weight = held.tile([P, 2, PACK], F32, name="half_weight")
+        nc.scalar.activation(half_weight[:, 0, :], row_weight[:, 0, :], ACT.Copy, scale=0.5)
+        nc.scalar.activation(half_weight[:, 1, :], row_weight[:, 0, :], ACT.Copy, scale=-0.5)
+        tanh0 = [buffer([P, N], F32, f"plane{t}") for t in range(PACK)]
         for t in range(PACK):
-            nc.scalar.activation(probs0[t][:], logits0[t][:], ACT.Sigmoid)
+            nc.scalar.activation(tanh0[t][:], logits0[t][:], ACT.Tanh, scale=0.5)
+        g_planes0 = buffer([P, PACK, N], BF16, "g_planes")
         for t in range(PACK):
-            weight = row_weight[:, 0, t : t + 1]
-            nc.scalar.activation(labels0[:, t, :], labels0[:, t, :], ACT.Copy, scale=weight)
-            for c in range(0, N, N // 2 if t == PACK - 1 else N):
-                cols = slice(c, c + N // 2) if t == PACK - 1 else slice(0, N)
+            labels = labels0[t // 2][:, t % 2, :]
+            nc.scalar.activation(labels, labels, ACT.Identity, scale=row_weight[:, 0, t : t + 1], bias=half_weight[:, 1, t : t + 1])
+            width = HALF if t == PACK - 1 else N
+            for c in range(0, N, width):
+                cols = slice(c, c + width)
                 nc.vector.scalar_tensor_tensor(
-                    g_planes0[:, t, cols], probs0[t][:, cols], weight, labels0[:, t, cols], ALU.mult, ALU.subtract
+                    g_planes0[:, t, cols], tanh0[t][:, cols], half_weight[:, 0, t : t + 1], labels[:, cols], ALU.mult, ALU.subtract
                 )
+        xm_staged0 = [interleaved(nc.scalar.copy, xm_raw0[h][:], f"xm_staged0_{h}") for h in range(2)]
+        g_staged0 = buffer([P, N * PACK], BF16, "g_staged")
+        for c in range(0, N, HALF):
+            interleave(nc.vector.tensor_copy, g_staged0[:, c * PACK : (c + HALF) * PACK], g_planes0[:, :, c : c + HALF])
+        xm_mx0 = [quantize(xm_staged0[0], E4M3, "xm0_0", "xm0_0_codes")]
+        g_mx0 = quantize(g_staged0, E5M2, "g0", "xm_raw0_0")
+        dw0 = product(xm_mx0[0], g_mx0, E5M2)
+        w_mx1 = quantize(w_staged[1], E4M3, "w1", "xm_staged0_0")
+        xm_mx0.append(quantize(xm_staged0[1], E4M3, "xm0_1", "xm0_1_codes"))
+        dw0.extend(product(xm_mx0[1], g_mx0, E5M2))
+        v_listed.append(gather_v(v_source[2], "v_listed2"))
 
-        x_raw1 = load_planes(xT[1], "x_buffer")
-        v_source.append(load(work.tile([P, T], F32, name="v2_buffer", align_bytes=MX_ALIGN), vT[tile_rows(2), :]))
-        load_v(3)
-        load_nv_table(0)
-        load_nv_table(1)
-        labels1 = work.tile([P, PACK, N], F32, name="labels1", tag="y_buffer", align_bytes=MX_ALIGN)
-        nc.sync.dma_start(labels1[:, :2, :], as_planes(y[1])[:, :2, :])
-        load_nv_table(2)
-        nc.sync.dma_start(labels1[:, 2:, :], as_planes(y[1])[:, 2:, :])
+        x_raw1 = load_planes(as_planes(xT[1]), "x_raw")
+        v_source.append(load_v(LAST))
+        nv_table.append(load_v(2))
+        xm_raw1 = load_planes(as_planes(xm[1]), "xm_raw1")
+        labels1 = load_planes(as_planes(y[1]), "labels1")
+        nv_table.append(load_v(LAST))
 
-        xm_staged0 = interleave(nc.scalar.copy, xm_raw0[:], "stage_d")
-        xm_mx0 = quantize(xm_staged0, E4M3, "xm0", "xm0_codes")
-        if GS == 512:
-            g_staged0 = staged_tile("stage_a")
-            for c in range(0, N, N // 2):
-                nc.vector.tensor_copy(
-                    g_staged0[:, c * PACK : (c + N // 2) * PACK].rearrange("p (c t) -> p c t", t=PACK),
-                    g_planes0[:, :, c : c + N // 2].rearrange("p t c -> p c t"),
-                )
-            g_mx0 = quantize(g_staged0, E5M2, "g0", "xm_buffer")
-        else:
-            g_mx0 = mx_tiles("g0", "g0_codes")
-            for copy, tag, c0, c1 in ((nc.vector.tensor_copy, "stage_a", 0, GS), (nc.scalar.copy, "xm_buffer", GS, N)):
-                part = work.tile([P, (c1 - c0) * PACK], BF16, name="part", tag=tag, align_bytes=MX_ALIGN)
-                copy(part[:].rearrange("p (c t) -> p c t", t=PACK), g_planes0[:, :, c0:c1].rearrange("p t c -> p c t"))
-                for a in range(c0, c1, 256):
-                    b = min(a + 256, c1)
-                    nc.vector.quantize_mx(out=g_mx0[0][:, a:b].bitcast(E5M2), scales=g_mx0[1][:, a:b], in_=part[:, (a - c0) * PACK : (b - c0) * PACK])
-        xm_raw1 = load_planes(xm[1], "x_buffer")
-        x_staged1 = stage_x(x_raw1, nc.scalar.copy, "stage_b")
-        gather_v(2)
-        x_mx1 = quantize(x_staged1, E4M3, "x1", "v2_buffer")
-        dw0 = product(xm_mx0, g_mx0, E5M2)
+        squares0 = buffer([P, LAST, N], F32, "w_listed")
+        sums0 = buffer([P, LAST, N], F32, "sums0")
+        for j in range(LAST):
+            square(squares0[:, j, :], dw0[j])
+            nc.gpsimd.tensor_tensor(sums0[:, j, :], v_listed[j][:, group_cols(0)], squares0[:, j, :], ALU.add)
+        first = buffer([P, 2, N], F32, "first_step")
+        descent(first[:, 0, :], dw0[0])
+        logs0 = buffer([P, LAST, N], F32, "logs0")
+        for j in range(LAST):
+            nc.scalar.activation(logs0[:, j, :], sums0[:, j, :], ACT.Ln)
+        rate(first[:, 1, :], logs0[:, 0, :])
+        for j in range(2):
+            scatter_nv(0, j, sums0[:, j, :])
+        scatter_step(0, 0, first[:, 0, :], first[:, 1, :])
 
-        def square_of(square, dw_bank):
-            nc.scalar.activation(square, dw_bank[:], ACT.Square)
-            return square
-
-        def add_square(add, b, j, square):
-            add(nv[:, j, group_cols(b)], nv[:, j, group_cols(b)], square[j], ALU.add)
-
-        squares0 = work.tile([P, D_TILES, N], F32, name="squares0")
-        for j in range(D_TILES):
-            square_of(squares0[:, j, :], dw0[j])
-        sums0 = work.tile([P, D_TILES, N], F32, name="sums0", tag="stage_b", align_bytes=MX_ALIGN)
-        gather_v(3)
-        place0 = [0, 1, 2, 3]
-        for j in place0:
-            on_gpsimd(sums0[:, j, :], nv[:, j, group_cols(0)], squares0[:, j, :], ALU.add)
-
-        descent0 = [copy_descent(dw0[j], f"descent0{j}") for j in range(2)]
-        probs1 = probabilities(x_mx1, w_mx1)
-        for j in range(last):
-            scatter_nv(0, j, sums0[:, place0[j], :])
+        x_mx1 = quantize(dealt(nc.scalar.copy, x_raw1, "w_staged0"), E4M3, "x1", "x1_codes")
+        later = buffer([P, 3, N], F32, "x_raw")
+        rate(later[:, 0, :], logs0[:, 1, :])
+        descent(later[:, 1, :], dw0[1])
+        rate(later[:, 2, :], logs0[:, 2, :])
+        scatter_step(0, 1, later[:, 1, :], later[:, 0, :])
+        logits1 = product(x_mx1, w_mx1, E4M3)
+        probs1 = [buffer([P, N], F32, f"plane{t}") for t in range(PACK)]
         for t in range(PACK):
-            on_gpsimd(labels1[:, t, :], probs1[t][:], labels1[:, t, :], ALU.subtract)
-        rate0 = roots(sums0)
-        later = work.tile([P, 2, N], F32, name="later", tag="squares0")
-        descent0.append(later[:, 0, :])
-        finish_rates(rate0)
-        for j in range(2, D_TILES):
-            nc.scalar.activation(later[:, j - 2, :], dw0[j][:], ACT.Copy, scale=-LR)
-
-        g_planes1 = work.tile([P, PACK, N], BF16, name="g_planes1", tag="g0_planes", align_bytes=MX_ALIGN)
+            nc.scalar.activation(probs1[t][:], logits1[t][:], ACT.Sigmoid)
+        v_listed.append(gather_v(v_source[LAST], "logs0"))
+        scatter_nv(0, 2, sums0[:, 2, :])
+        xm_mx1 = quantize(interleaved(nc.scalar.copy, xm_raw1[:], "x_staged0"), E4M3, "xm1", "xm1_codes")
+        g_planes1 = buffer([P, PACK, N], BF16, "g_planes")
         for t in range(PACK):
+            nc.gpsimd.tensor_tensor(labels1[:, t, :], probs1[t][:], labels1[:, t, :], ALU.subtract)
             nc.scalar.activation(g_planes1[:, t, :], labels1[:, t, :], ACT.Copy, scale=row_weight[:, 1, t : t + 1])
-        descent0.append(later[:, 1, :])
-        for j in range(D_TILES):
-            scatter_step(0, j, descent0[j], rate0[:, place0[j], :])
-        xm_mx1 = quantize(interleave(nc.scalar.copy if XM1 == "S" else gp_copy, xm_raw1[:], "stage_d"), E4M3, "xm1", "xm1_codes")
-        nv_table.append(work.tile([P, T], F32, name="nv_table3", tag="y_buffer", align_bytes=MX_ALIGN))
-        load_nv_table(last)
-        g_mx1 = quantize(interleave(nc.scalar.copy, g_planes1[:], "stage_c"), E5M2, "g1", "g1_codes")
+            if t == 2:
+                descent2 = buffer([P, N], F32, "plane2")
+                descent(descent2[:], dw0[2])
+        scatter_step(0, 2, descent2[:], later[:, 2, :])
+        g_mx1 = quantize(interleaved(nc.scalar.copy, g_planes1[:], "g_staged"), E5M2, "g1", "g1_codes")
         dw1 = product(xm_mx1, g_mx1, E5M2)
-        scatter_nv(0, last, sums0[:, last, :])
-        squares1 = work.tile([P, D_TILES, N], F32, name="squares1", tag="w_listed")
+
+        last0 = buffer([P, 2, N], F32, "g_planes")
+        square(last0[:, 0, :], dw0[LAST])
+        descent(last0[:, 1, :], dw0[LAST])
+        scatter_sum(0, LAST, last0[:, 0, :])
+        squares1 = buffer([P, D_TILES, N], F32, "w_listed")
         for j in range(D_TILES):
-            square_of(squares1[:, j, :], dw1[j])
-        descent1 = [copy_descent(dw1[j], "f32_ring") for j in range(D_TILES)]
+            square(squares1[:, j, :], dw1[j])
+        descents1 = [buffer([P, N], F32, f"plane{j}") for j in range(D_TILES)]
+        for j in range(D_TILES):
+            descent(descents1[j][:], dw1[j])
+        late = [(0, LAST, last0[:, 0, :], last0[:, 1, :])] + [(1, j, squares1[:, j, :], descents1[j][:]) for j in range(D_TILES)]
         blocks = [slice(i * P, (i + 1) * P) for i in range(N // P)]
-        turned_roots = work.tile([P, D_TILES, N], F32, name="turned_roots", tag="squares0")
-        for j in range(D_TILES):
+        turned_logs = buffer([P, len(late), N], F32, "xm_raw1")
+        for i, (b, j, squares, descents) in enumerate(late):
             turned_sums = psum.tile([P, N], F32, name="bank")
             for cols in blocks:
-                nc.tensor.matmul(turned_sums[:, cols], lhsT=nv[:, j, group_cols(1)][:, cols], rhs=identity[:], start=True, stop=False, is_transpose=True)
-                nc.tensor.matmul(turned_sums[:, cols], lhsT=squares1[:, j, cols], rhs=identity[:], start=False, stop=True, is_transpose=True)
-            nc.scalar.activation(turned_roots[:, j, :], turned_sums[:], ACT.Sqrt)
-        rate1 = work.tile([P, D_TILES, N], F32, name="rate", align_bytes=MX_ALIGN)
-        for j in range(D_TILES):
-            root = psum.tile([P, N], F32, name="bank")
+                nc.tensor.matmul(turned_sums[:, cols], lhsT=v_listed[j][:, group_cols(b)][:, cols], rhs=identity[:], start=True, stop=False, is_transpose=True)
+                nc.tensor.matmul(turned_sums[:, cols], lhsT=squares[:, cols], rhs=identity[:], start=False, stop=True, is_transpose=True)
+            nc.scalar.activation(turned_logs[:, i, :], turned_sums[:], ACT.Ln)
+        rates = buffer([P, len(late), N], F32, "labels1")
+        for i in range(len(late)):
+            log_nv = psum.tile([P, N], F32, name="bank")
             for cols in blocks:
-                nc.tensor.transpose(root[:, cols], turned_roots[:, j, cols], identity[:])
-            nc.scalar.activation(rate1[:, j, :], root[:], ACT.Square, bias=EPS)
+                nc.tensor.transpose(log_nv[:, cols], turned_logs[:, i, cols], identity[:])
+            rate(rates[:, i, :], log_nv[:])
         for j in range(D_TILES):
-            invert_rate(rate1, j)
-        for j in range(D_TILES):
-            nc.vector.tensor_tensor(nv_table[j][:].indirect(group_list(1)), nv[:, j, group_cols(1)], squares1[:, j, :], ALU.add)
+            scatter_sum(1, j, squares1[:, j, :])
             nc.sync.dma_start(out_1[tile_rows(j), :], nv_table[j][:])
-        for j in range(D_TILES):
-            scatter_step(1, j, descent1[j], rate1[:, j, :])
-            nc.sync.dma_start(out_0[tile_rows(j), :], step_table[j][:])
+        for i, (b, j, squares, descents) in enumerate(late):
+            scatter_step(b, j, descents, rates[:, i, :])
+            if b == B - 1:
+                nc.sync.dma_start(out_0[tile_rows(j), :], step_table[j][:])

@@ -7,6 +7,7 @@ from concourse.masks import make_identity
 B, N, T, D, R = 2, 512, 2048, 512, 512
 LR = 0.1
 EPS = 0.001
+TINY = 1e-30
 FLOPS = 2 * 2 * B * N * D * R
 
 F32 = mybir.dt.float32
@@ -28,6 +29,8 @@ LAST = D_TILES - 1
 LIST_COLS = N // 16
 MX_ALIGN = 64
 TABLE_BUFS = 6
+PSUM_BANKS = 8
+G_SPLIT = 384
 
 
 def tile_attend_gnce_ada_kernel(tc, xT, wT, y, wt, xm, vT, offs, out_0, out_1):
@@ -36,7 +39,7 @@ def tile_attend_gnce_ada_kernel(tc, xT, wT, y, wt, xm, vT, offs, out_0, out_1):
         held = ctx.enter_context(tc.tile_pool(name="held", bufs=1))
         tables = ctx.enter_context(tc.tile_pool(name="tables", bufs=TABLE_BUFS))
         work = ctx.enter_context(tc.tile_pool(name="work", bufs=1))
-        psum = ctx.enter_context(tc.psum_pool(name="psum", bufs=8))
+        psum = ctx.enter_context(tc.psum_pool(name="psum", bufs=PSUM_BANKS))
 
         def buffer(shape, dtype, tag):
             return work.tile(shape, dtype, name=tag, tag=tag, align_bytes=MX_ALIGN)
@@ -156,6 +159,7 @@ def tile_attend_gnce_ada_kernel(tc, xT, wT, y, wt, xm, vT, offs, out_0, out_1):
                     w_staged[b][:].rearrange("p (c t) -> p c t", t=PACK)[:, :, t : t + 2],
                     w_listed[:, t : t + 2, group_cols(b)].rearrange("p t c -> p c t"),
                 )
+
         x_staged0 = dealt(nc.vector.tensor_copy, x_raw0, "x_staged0")
         w_mx0 = quantize(w_staged[0], E4M3, "w0", "x_raw")
         x_mx0 = quantize(x_staged0, E4M3, "x0", "x0_codes")
@@ -170,33 +174,35 @@ def tile_attend_gnce_ada_kernel(tc, xT, wT, y, wt, xm, vT, offs, out_0, out_1):
         tanh0 = [buffer([P, N], F32, f"plane{t}") for t in range(PACK)]
         for t in range(PACK):
             nc.scalar.activation(tanh0[t][:], logits0[t][:], ACT.Tanh, scale=0.5)
-        g_planes0 = buffer([P, PACK, N], BF16, "g_planes")
+        g_parts = [slice(0, G_SPLIT), slice(G_SPLIT, N)]
+        g_planes0 = buffer([P, PACK, N], BF16, "g_planes0")
         for t in range(PACK):
             labels = labels0[t // 2][:, t % 2, :]
             nc.scalar.activation(labels, labels, ACT.Identity, scale=row_weight[:, 0, t : t + 1], bias=half_weight[:, 1, t : t + 1])
-            width = HALF if t == PACK - 1 else N
-            for c in range(0, N, width):
-                cols = slice(c, c + width)
+            for cols in g_parts if t == PACK - 1 else [slice(0, N)]:
                 nc.vector.scalar_tensor_tensor(
                     g_planes0[:, t, cols], tanh0[t][:, cols], half_weight[:, 0, t : t + 1], labels[:, cols], ALU.mult, ALU.subtract
                 )
-        xm_staged0 = [interleaved(nc.scalar.copy, xm_raw0[h][:], f"xm_staged0_{h}") for h in range(2)]
+
+        xm_staged0 = [interleaved(nc.scalar.copy, xm_raw0[0][:], "xm_staged0_0")]
         g_staged0 = buffer([P, N * PACK], BF16, "g_staged")
-        for c in range(0, N, HALF):
-            interleave(nc.vector.tensor_copy, g_staged0[:, c * PACK : (c + HALF) * PACK], g_planes0[:, :, c : c + HALF])
+        for copy, cols in zip((nc.vector.tensor_copy, nc.scalar.copy), g_parts):
+            interleave(copy, g_staged0[:, cols.start * PACK : cols.stop * PACK], g_planes0[:, :, cols])
+        xm_staged0.append(interleaved(nc.scalar.copy, xm_raw0[1][:], "labels0_2"))
         xm_mx0 = [quantize(xm_staged0[0], E4M3, "xm0_0", "xm0_0_codes")]
         g_mx0 = quantize(g_staged0, E5M2, "g0", "xm_raw0_0")
         dw0 = product(xm_mx0[0], g_mx0, E5M2)
         w_mx1 = quantize(w_staged[1], E4M3, "w1", "xm_staged0_0")
         xm_mx0.append(quantize(xm_staged0[1], E4M3, "xm0_1", "xm0_1_codes"))
         dw0.extend(product(xm_mx0[1], g_mx0, E5M2))
-        v_listed.append(gather_v(v_source[2], "v_listed2"))
+        v_listed.append(gather_v(v_source[2], "g_planes0"))
 
         x_raw1 = load_planes(as_planes(xT[1]), "x_raw")
         v_source.append(load_v(LAST))
         nv_table.append(load_v(2))
+        labels1 = [load_planes(as_planes(y[1])[:, :2, :], "labels1_0")]
         xm_raw1 = load_planes(as_planes(xm[1]), "xm_raw1")
-        labels1 = load_planes(as_planes(y[1]), "labels1")
+        labels1.append(load_planes(as_planes(y[1])[:, 2:, :], "labels1_2"))
         nv_table.append(load_v(LAST))
 
         squares0 = buffer([P, LAST, N], F32, "w_listed")
@@ -204,41 +210,43 @@ def tile_attend_gnce_ada_kernel(tc, xT, wT, y, wt, xm, vT, offs, out_0, out_1):
         for j in range(LAST):
             square(squares0[:, j, :], dw0[j])
             nc.gpsimd.tensor_tensor(sums0[:, j, :], v_listed[j][:, group_cols(0)], squares0[:, j, :], ALU.add)
-        first = buffer([P, 2, N], F32, "first_step")
-        descent(first[:, 0, :], dw0[0])
+        step0 = buffer([P, 2, N], F32, "step0")
+        descent(step0[:, 0, :], dw0[0])
         logs0 = buffer([P, LAST, N], F32, "logs0")
         for j in range(LAST):
-            nc.scalar.activation(logs0[:, j, :], sums0[:, j, :], ACT.Ln)
-        rate(first[:, 1, :], logs0[:, 0, :])
+            nc.scalar.activation(logs0[:, j, :], sums0[:, j, :], ACT.Ln, bias=TINY)
+        rate(step0[:, 1, :], logs0[:, 0, :])
         for j in range(2):
             scatter_nv(0, j, sums0[:, j, :])
-        scatter_step(0, 0, first[:, 0, :], first[:, 1, :])
+        scatter_step(0, 0, step0[:, 0, :], step0[:, 1, :])
 
         x_mx1 = quantize(dealt(nc.scalar.copy, x_raw1, "w_staged0"), E4M3, "x1", "x1_codes")
-        later = buffer([P, 3, N], F32, "x_raw")
-        rate(later[:, 0, :], logs0[:, 1, :])
-        descent(later[:, 1, :], dw0[1])
-        rate(later[:, 2, :], logs0[:, 2, :])
-        scatter_step(0, 1, later[:, 1, :], later[:, 0, :])
+        steps12 = buffer([P, 3, N], F32, "x_raw")
+        rate(steps12[:, 0, :], logs0[:, 1, :])
+        descent(steps12[:, 1, :], dw0[1])
+        rate(steps12[:, 2, :], logs0[:, 2, :])
+        scatter_step(0, 1, steps12[:, 1, :], steps12[:, 0, :])
         logits1 = product(x_mx1, w_mx1, E4M3)
         probs1 = [buffer([P, N], F32, f"plane{t}") for t in range(PACK)]
         for t in range(PACK):
             nc.scalar.activation(probs1[t][:], logits1[t][:], ACT.Sigmoid)
+
         v_listed.append(gather_v(v_source[LAST], "logs0"))
         scatter_nv(0, 2, sums0[:, 2, :])
         xm_mx1 = quantize(interleaved(nc.scalar.copy, xm_raw1[:], "x_staged0"), E4M3, "xm1", "xm1_codes")
-        g_planes1 = buffer([P, PACK, N], BF16, "g_planes")
+        g_planes1 = buffer([P, PACK, N], BF16, "xm_raw1")
         for t in range(PACK):
-            nc.gpsimd.tensor_tensor(labels1[:, t, :], probs1[t][:], labels1[:, t, :], ALU.subtract)
-            nc.scalar.activation(g_planes1[:, t, :], labels1[:, t, :], ACT.Copy, scale=row_weight[:, 1, t : t + 1])
+            labels = labels1[t // 2][:, t % 2, :]
+            nc.gpsimd.tensor_tensor(labels, probs1[t][:], labels, ALU.subtract)
+            nc.scalar.activation(g_planes1[:, t, :], labels, ACT.Copy, scale=row_weight[:, 1, t : t + 1])
             if t == 2:
                 descent2 = buffer([P, N], F32, "plane2")
                 descent(descent2[:], dw0[2])
-        scatter_step(0, 2, descent2[:], later[:, 2, :])
+        scatter_step(0, 2, descent2[:], steps12[:, 2, :])
         g_mx1 = quantize(interleaved(nc.scalar.copy, g_planes1[:], "g_staged"), E5M2, "g1", "g1_codes")
         dw1 = product(xm_mx1, g_mx1, E5M2)
 
-        last0 = buffer([P, 2, N], F32, "g_planes")
+        last0 = buffer([P, 2, N], F32, "xm_raw1")
         square(last0[:, 0, :], dw0[LAST])
         descent(last0[:, 1, :], dw0[LAST])
         scatter_sum(0, LAST, last0[:, 0, :])
@@ -248,21 +256,23 @@ def tile_attend_gnce_ada_kernel(tc, xT, wT, y, wt, xm, vT, offs, out_0, out_1):
         descents1 = [buffer([P, N], F32, f"plane{j}") for j in range(D_TILES)]
         for j in range(D_TILES):
             descent(descents1[j][:], dw1[j])
+
         late = [(0, LAST, last0[:, 0, :], last0[:, 1, :])] + [(1, j, squares1[:, j, :], descents1[j][:]) for j in range(D_TILES)]
         blocks = [slice(i * P, (i + 1) * P) for i in range(N // P)]
-        turned_logs = buffer([P, len(late), N], F32, "xm_raw1")
+        turned_logs = buffer([P, len(late), N], F32, "x_raw")
         for i, (b, j, squares, descents) in enumerate(late):
             turned_sums = psum.tile([P, N], F32, name="bank")
             for cols in blocks:
                 nc.tensor.matmul(turned_sums[:, cols], lhsT=v_listed[j][:, group_cols(b)][:, cols], rhs=identity[:], start=True, stop=False, is_transpose=True)
                 nc.tensor.matmul(turned_sums[:, cols], lhsT=squares[:, cols], rhs=identity[:], start=False, stop=True, is_transpose=True)
-            nc.scalar.activation(turned_logs[:, i, :], turned_sums[:], ACT.Ln)
-        rates = buffer([P, len(late), N], F32, "labels1")
+            nc.scalar.activation(turned_logs[:, i, :], turned_sums[:], ACT.Ln, bias=TINY)
+        rates = buffer([P, len(late), N], F32, "sums0")
         for i in range(len(late)):
             log_nv = psum.tile([P, N], F32, name="bank")
             for cols in blocks:
                 nc.tensor.transpose(log_nv[:, cols], turned_logs[:, i, cols], identity[:])
             rate(rates[:, i, :], log_nv[:])
+
         for j in range(D_TILES):
             scatter_sum(1, j, squares1[:, j, :])
             nc.sync.dma_start(out_1[tile_rows(j), :], nv_table[j][:])

@@ -70,7 +70,7 @@ def tile_attend_gnce_ada_kernel(tc, xT, wT, y, wt, xm, vT, offs, out_0, out_1):
             return load(buffer(list(planes.shape), F32, tag), planes)
 
         def interleave(copy, staged, planes):
-            copy(staged.rearrange("p (c t) -> p c t", t=PACK), planes.rearrange("p t c -> p c t"))
+            copy(staged.rearrange("p (c i t) -> p c t i", i=PACK, t=PACK), planes.rearrange("p t (c i) -> p c t i", i=PACK))
 
         def interleaved(copy, planes, tag):
             staged = buffer([P, planes.shape[2] * PACK], BF16, tag)
@@ -80,8 +80,8 @@ def tile_attend_gnce_ada_kernel(tc, xT, wT, y, wt, xm, vT, offs, out_0, out_1):
         def dealt(copy, x_raw, tag):
             staged = buffer([P, COLS * PACK], BF16, tag)
             copy(
-                staged[:].rearrange("p (t m k) -> p m t k", t=PACK, k=PACK),
-                x_raw[:].rearrange("p k (m t) -> p m t k", t=PACK),
+                staged[:].rearrange("p (t m k) -> p m k t", t=PACK, k=PACK),
+                x_raw[:].rearrange("p k (m t) -> p m k t", t=PACK),
             )
             return staged
 
@@ -139,7 +139,7 @@ def tile_attend_gnce_ada_kernel(tc, xT, wT, y, wt, xm, vT, offs, out_0, out_1):
         v_source.append(load_v(1))
         labels0 = [load_planes(as_planes(y[0])[:, t : t + 2, :], f"labels0_{t}") for t in range(0, PACK, 2)]
         xm_raw0 = [load_planes(as_planes(xm[0])[:, :, c : c + HALF], f"xm_raw0_{c}") for c in range(0, D, HALF)]
-        v_source.append(load_v(2))
+        v_source.extend([load_v(2), load_v(LAST)])
         nv_table = [load_v(0), load_v(1)]
 
         step_table = []
@@ -196,44 +196,45 @@ def tile_attend_gnce_ada_kernel(tc, xT, wT, y, wt, xm, vT, offs, out_0, out_1):
         xm_mx0.append(quantize(xm_staged0[1], E4M3, "xm0_1", "xm0_1_codes"))
         dw0.extend(product(xm_mx0[1], g_mx0, E5M2))
         v_listed.append(gather_v(v_source[2], "g_planes0"))
+        v_listed.append(gather_v(v_source[LAST], "v_listed3"))
 
         x_raw1 = load_planes(as_planes(xT[1]), "x_raw")
-        v_source.append(load_v(LAST))
-        nv_table.append(load_v(2))
         labels1 = [load_planes(as_planes(y[1])[:, :2, :], "labels1_0")]
         xm_raw1 = load_planes(as_planes(xm[1]), "xm_raw1")
+        nv_table.extend([load_v(2), load_v(LAST)])
         labels1.append(load_planes(as_planes(y[1])[:, 2:, :], "labels1_2"))
-        nv_table.append(load_v(LAST))
 
-        squares0 = buffer([P, LAST, N], F32, "w_listed")
-        sums0 = buffer([P, LAST, N], F32, "sums0")
-        for j in range(LAST):
+        squares0 = buffer([P, D_TILES, N], F32, "w_listed")
+        sums0 = buffer([P, D_TILES, N], F32, "sums0")
+        for j in range(D_TILES):
             square(squares0[:, j, :], dw0[j])
             nc.gpsimd.tensor_tensor(sums0[:, j, :], v_listed[j][:, group_cols(0)], squares0[:, j, :], ALU.add)
-        step0 = buffer([P, 2, N], F32, "step0")
-        descent(step0[:, 0, :], dw0[0])
-        logs0 = buffer([P, LAST, N], F32, "logs0")
-        for j in range(LAST):
+        descents01 = buffer([P, 2, N], F32, "descents01")
+        descent(descents01[:, 0, :], dw0[0])
+        logs0 = buffer([P, D_TILES, N], F32, "logs0")
+        for j in range(D_TILES):
+            if j == LAST:
+                descent(descents01[:, 1, :], dw0[1])
             nc.scalar.activation(logs0[:, j, :], sums0[:, j, :], ACT.Ln, bias=TINY)
-        rate(step0[:, 1, :], logs0[:, 0, :])
+        rate0 = buffer([P, N], F32, "w_listed")
+        rate(rate0[:], logs0[:, 0, :])
         for j in range(2):
             scatter_nv(0, j, sums0[:, j, :])
-        scatter_step(0, 0, step0[:, 0, :], step0[:, 1, :])
+        scatter_step(0, 0, descents01[:, 0, :], rate0[:])
 
         x_mx1 = quantize(dealt(nc.scalar.copy, x_raw1, "w_staged0"), E4M3, "x1", "x1_codes")
-        steps12 = buffer([P, 3, N], F32, "x_raw")
-        rate(steps12[:, 0, :], logs0[:, 1, :])
-        descent(steps12[:, 1, :], dw0[1])
-        rate(steps12[:, 2, :], logs0[:, 2, :])
-        scatter_step(0, 1, steps12[:, 1, :], steps12[:, 0, :])
+        rates0 = buffer([P, LAST, N], F32, "x_raw")
+        for j in range(1, D_TILES):
+            rate(rates0[:, j - 1, :], logs0[:, j, :])
+        scatter_step(0, 1, descents01[:, 1, :], rates0[:, 0, :])
         logits1 = product(x_mx1, w_mx1, E4M3)
         probs1 = [buffer([P, N], F32, f"plane{t}") for t in range(PACK)]
         for t in range(PACK):
             nc.scalar.activation(probs1[t][:], logits1[t][:], ACT.Sigmoid)
 
-        v_listed.append(gather_v(v_source[LAST], "logs0"))
-        scatter_nv(0, 2, sums0[:, 2, :])
-        xm_mx1 = quantize(interleaved(nc.scalar.copy, xm_raw1[:], "x_staged0"), E4M3, "xm1", "xm1_codes")
+        for j in range(2, D_TILES):
+            scatter_nv(0, j, sums0[:, j, :])
+        xm_staged1 = interleaved(nc.scalar.copy, xm_raw1[:], "x_staged0")
         g_planes1 = buffer([P, PACK, N], BF16, "xm_raw1")
         for t in range(PACK):
             labels = labels1[t // 2][:, t % 2, :]
@@ -242,14 +243,14 @@ def tile_attend_gnce_ada_kernel(tc, xT, wT, y, wt, xm, vT, offs, out_0, out_1):
             if t == 2:
                 descent2 = buffer([P, N], F32, "plane2")
                 descent(descent2[:], dw0[2])
-        scatter_step(0, 2, descent2[:], steps12[:, 2, :])
+        xm_mx1 = quantize(xm_staged1, E4M3, "xm1", "plane3")
+        scatter_step(0, 2, descent2[:], rates0[:, 1, :])
         g_mx1 = quantize(interleaved(nc.scalar.copy, g_planes1[:], "g_staged"), E5M2, "g1", "g1_codes")
         dw1 = product(xm_mx1, g_mx1, E5M2)
 
-        last0 = buffer([P, 2, N], F32, "xm_raw1")
-        square(last0[:, 0, :], dw0[LAST])
-        descent(last0[:, 1, :], dw0[LAST])
-        scatter_sum(0, LAST, last0[:, 0, :])
+        descent3 = buffer([P, N], F32, "xm_raw1")
+        descent(descent3[:], dw0[LAST])
+        scatter_step(0, LAST, descent3[:], rates0[:, 2, :])
         squares1 = buffer([P, D_TILES, N], F32, "w_listed")
         for j in range(D_TILES):
             square(squares1[:, j, :], dw1[j])
@@ -257,26 +258,24 @@ def tile_attend_gnce_ada_kernel(tc, xT, wT, y, wt, xm, vT, offs, out_0, out_1):
         for j in range(D_TILES):
             descent(descents1[j][:], dw1[j])
 
-        late = [(0, LAST, last0[:, 0, :], last0[:, 1, :])] + [(1, j, squares1[:, j, :], descents1[j][:]) for j in range(D_TILES)]
         blocks = [slice(i * P, (i + 1) * P) for i in range(N // P)]
-        turned_logs = buffer([P, len(late), N], F32, "x_raw")
-        for i, (b, j, squares, descents) in enumerate(late):
+        turned_logs = buffer([P, D_TILES, N], F32, "logs0")
+        for j in range(D_TILES):
             turned_sums = psum.tile([P, N], F32, name="bank")
             for cols in blocks:
-                nc.tensor.matmul(turned_sums[:, cols], lhsT=v_listed[j][:, group_cols(b)][:, cols], rhs=identity[:], start=True, stop=False, is_transpose=True)
-                nc.tensor.matmul(turned_sums[:, cols], lhsT=squares[:, cols], rhs=identity[:], start=False, stop=True, is_transpose=True)
-            nc.scalar.activation(turned_logs[:, i, :], turned_sums[:], ACT.Ln, bias=TINY)
-        rates = buffer([P, len(late), N], F32, "sums0")
-        for i in range(len(late)):
+                nc.tensor.matmul(turned_sums[:, cols], lhsT=v_listed[j][:, group_cols(1)][:, cols], rhs=identity[:], start=True, stop=False, is_transpose=True)
+                nc.tensor.matmul(turned_sums[:, cols], lhsT=squares1[:, j, cols], rhs=identity[:], start=False, stop=True, is_transpose=True)
+            nc.scalar.activation(turned_logs[:, j, :], turned_sums[:], ACT.Ln, bias=TINY)
+        rates1 = buffer([P, D_TILES, N], F32, "sums0")
+        for j in range(D_TILES):
             log_nv = psum.tile([P, N], F32, name="bank")
             for cols in blocks:
-                nc.tensor.transpose(log_nv[:, cols], turned_logs[:, i, cols], identity[:])
-            rate(rates[:, i, :], log_nv[:])
+                nc.tensor.transpose(log_nv[:, cols], turned_logs[:, j, cols], identity[:])
+            rate(rates1[:, j, :], log_nv[:])
 
         for j in range(D_TILES):
             scatter_sum(1, j, squares1[:, j, :])
             nc.sync.dma_start(out_1[tile_rows(j), :], nv_table[j][:])
-        for i, (b, j, squares, descents) in enumerate(late):
-            scatter_step(b, j, descents, rates[:, i, :])
-            if b == B - 1:
-                nc.sync.dma_start(out_0[tile_rows(j), :], step_table[j][:])
+        for j in range(D_TILES):
+            scatter_step(1, j, descents1[j][:], rates1[:, j, :])
+            nc.sync.dma_start(out_0[tile_rows(j), :], step_table[j][:])

@@ -2,12 +2,11 @@ import math
 from contextlib import ExitStack
 
 import concourse.mybir as mybir
-from concourse.masks import make_identity
 
 B, N, T, D, R = 2, 512, 2048, 512, 512
 LR = 0.1
 EPS = 0.001
-TINY = 1e-30
+TINY = 1e-19
 FLOPS = 2 * 2 * B * N * D * R
 
 F32 = mybir.dt.float32
@@ -25,10 +24,9 @@ PACK = 4
 COLS = 512
 HALF = COLS // 2
 D_TILES = D // P
-LAST = D_TILES - 1
-LIST_COLS = N // 16
+BAND = 16
 MX_ALIGN = 64
-TABLE_BUFS = 6
+TABLE_BUFS = 5
 PSUM_BANKS = 8
 G_SPLIT = 384
 
@@ -44,10 +42,10 @@ def tile_attend_gnce_ada_kernel(tc, xT, wT, y, wt, xm, vT, offs, out_0, out_1):
         def buffer(shape, dtype, tag):
             return work.tile(shape, dtype, name=tag, tag=tag, align_bytes=MX_ALIGN)
 
-        def group_list(b):
-            return offsets[:, b * LIST_COLS : (b + 1) * LIST_COLS]
+        def listed(slots):
+            return offsets[:, slots.start // BAND : slots.stop // BAND]
 
-        def group_cols(b):
+        def group(b):
             return slice(b * N, (b + 1) * N)
 
         def tile_rows(j):
@@ -60,8 +58,8 @@ def tile_attend_gnce_ada_kernel(tc, xT, wT, y, wt, xm, vT, offs, out_0, out_1):
         def load_table(rows):
             return load(tables.tile([P, T], F32, name="table"), rows)
 
-        def load_v(j):
-            return load_table(vT[tile_rows(j), :])
+        def load_nv_table(j):
+            return load(held.tile([P, T], F32, name=f"nv_table{j}"), vT[tile_rows(j), :])
 
         def as_planes(matrix):
             return matrix.rearrange("(p t) c -> p t c", t=PACK)
@@ -77,13 +75,12 @@ def tile_attend_gnce_ada_kernel(tc, xT, wT, y, wt, xm, vT, offs, out_0, out_1):
             interleave(copy, staged[:], planes)
             return staged
 
-        def dealt(copy, x_raw, tag):
-            staged = buffer([P, COLS * PACK], BF16, tag)
+        def deal(copy, staged, x_raw, first_row):
+            m = slice(first_row // PACK, (first_row + x_raw.shape[2]) // PACK)
             copy(
-                staged[:].rearrange("p (t m k) -> p m k t", t=PACK, k=PACK),
+                staged[:].rearrange("p (t m k) -> p m k t", t=PACK, k=PACK)[:, m],
                 x_raw[:].rearrange("p k (m t) -> p m k t", t=PACK),
             )
-            return staged
 
         def quantize(staged, fmt, name, codes_tag):
             words = staged.shape[1] // PACK
@@ -107,175 +104,175 @@ def tile_attend_gnce_ada_kernel(tc, xT, wT, y, wt, xm, vT, offs, out_0, out_1):
                 )
             return banks
 
-        def gather_v(source, tag):
-            listed = buffer([P, B * N], F32, tag)
-            nc.vector.tensor_copy(listed[:], source[:].indirect(offsets[:]))
-            return listed
+        def gather_on_scalar(out, table, slots):
+            nc.scalar.activation(out, table[:].indirect(listed(slots)), ACT.Copy)
 
-        def square(out, dw_bank):
-            nc.scalar.activation(out, dw_bank[:], ACT.Square)
+        def gather_on_vector(out, table, slots):
+            nc.vector.tensor_copy(out, table[:].indirect(listed(slots)))
 
-        def descent(out, dw_bank):
-            nc.scalar.activation(out, dw_bank[:], ACT.Copy, scale=-LR / EPS)
+        def scatter_on_scalar(table, values, slots):
+            nc.scalar.activation(table[:].indirect(listed(slots)), values[:, slots], ACT.Copy)
 
-        def rate(out, log_nv):
-            nc.scalar.activation(out, log_nv, ACT.Sigmoid, scale=-0.5, bias=math.log(EPS))
+        def scatter_on_vector(table, values, slots):
+            nc.vector.tensor_copy(table[:].indirect(listed(slots)), values[:, slots])
 
-        def scatter_nv(b, j, values):
-            nc.vector.tensor_copy(nv_table[j][:].indirect(group_list(b)), values)
+        def tanh_planes(logits):
+            planes = [buffer([P, N], F32, f"tanh{t}") for t in range(PACK)]
+            for t in range(PACK):
+                nc.scalar.activation(planes[t][:], logits[t][:], ACT.Tanh, scale=0.5)
+            return planes
 
-        def scatter_sum(b, j, squares):
-            nc.vector.tensor_tensor(nv_table[j][:].indirect(group_list(b)), v_listed[j][:, group_cols(b)], squares, ALU.add)
+        def weigh_labels(b, labels):
+            for t in range(PACK):
+                nc.vector.tensor_scalar(
+                    labels[t], labels[t], row_weight[:, b, t : t + 1], half_weight[:, b, t : t + 1], ALU.mult, ALU.subtract
+                )
 
-        def scatter_step(b, j, descents, rates):
-            nc.vector.tensor_tensor(step_table[j][:].indirect(group_list(b)), descents, rates, ALU.mult)
+        def gradient_planes(b, tanh, labels):
+            planes = buffer([P, PACK, N], BF16, "g_planes")
+            for t in range(PACK):
+                nc.vector.scalar_tensor_tensor(
+                    planes[:, t, :], tanh[t][:], half_weight[:, b, t : t + 1], labels[t], ALU.mult, ALU.subtract
+                )
+            return planes
 
-        offsets = held.tile([P, B * LIST_COLS], U16, name="offsets")
+        def square(j, b):
+            nc.scalar.activation(squares[j][:, group(b)], dw[b][j][:], ACT.Square)
+
+        def add_squares(engine, j, slots):
+            engine.tensor_tensor(nv[j][:, slots], v_listed[j][:, slots], squares[j][:, slots], ALU.add)
+
+        def log_nv(j, slots):
+            nc.scalar.activation(logs[j // 2][:, j % 2, slots], nv[j][:, slots], ACT.Ln, bias=TINY)
+
+        every_slot = slice(0, B * N)
+        thirds = [slice(0, 384), slice(384, 768), slice(768, 1024)]
+
+        offsets = held.tile([P, B * N // BAND], U16, name="offsets")
         nc.sync.dma_start(offsets[:], offs)
         w_plane = [load_table(as_planes(wT)[:, t, :]) for t in range(PACK)]
-        x_raw0 = load_planes(as_planes(xT[0]), "x_raw")
-        v_source = [load_v(0)]
+        x_raw0 = [load_planes(as_planes(xT[0])[:, :, r : r + HALF], f"x_raw0_{r}") for r in range(0, R, HALF)]
         row_weight = load(held.tile([P, B, PACK], F32, name="row_weight"), wt.rearrange("b (p t) o -> p b (t o)", t=PACK))
-        v_source.append(load_v(1))
-        labels0 = [load_planes(as_planes(y[0])[:, t : t + 2, :], f"labels0_{t}") for t in range(0, PACK, 2)]
+        y_raw0 = [load_planes(as_planes(y[0])[:, t : t + 2, :], f"y_raw0_{t}") for t in range(0, PACK, 2)]
         xm_raw0 = [load_planes(as_planes(xm[0])[:, :, c : c + HALF], f"xm_raw0_{c}") for c in range(0, D, HALF)]
-        v_source.extend([load_v(2), load_v(LAST)])
-        nv_table = [load_v(0), load_v(1)]
+        v_source = [load_table(vT[tile_rows(0), :])]
+        nv_table = [load_nv_table(0)]
+        x_raw1 = load_planes(as_planes(xT[1]), "x_raw1")
 
         step_table = []
         for j in range(D_TILES):
             step_table.append(held.tile([P, T], F32, name=f"step_table{j}"))
             nc.vector.memset(step_table[j][:].bitcast(U32), 0)
 
-        w_listed = buffer([P, PACK, B * N], F32, "w_listed")
-        for t in range(PACK - 1):
-            nc.vector.tensor_copy(w_listed[:, t, :], w_plane[t][:].indirect(offsets[:]))
-        for b in range(B):
-            nc.vector.tensor_copy(w_listed[:, PACK - 1, group_cols(b)], w_plane[PACK - 1][:].indirect(group_list(b)))
-        w_staged = [buffer([P, COLS * PACK], BF16, f"w_staged{b}") for b in range(B)]
-        for t in range(0, PACK, 2):
-            for b in range(B):
-                nc.scalar.copy(
-                    w_staged[b][:].rearrange("p (c t) -> p c t", t=PACK)[:, :, t : t + 2],
-                    w_listed[:, t : t + 2, group_cols(b)].rearrange("p t c -> p c t"),
-                )
+        w_staged0 = buffer([P, N * PACK], BF16, "w_staged0")
+        w_planes1 = buffer([P, PACK, N], BF16, "w_planes1")
+        for t in range(PACK):
+            gather_on_vector(w_staged0[:].rearrange("p (c t) -> p c t", t=PACK)[:, :, t], w_plane[t], group(0))
+            gather_on_scalar(w_planes1[:, t, :], w_plane[t], group(1))
 
-        x_staged0 = dealt(nc.vector.tensor_copy, x_raw0, "x_staged0")
-        w_mx0 = quantize(w_staged[0], E4M3, "w0", "x_raw")
+        y_raw1 = load_planes(as_planes(y[1]), "y_raw1")
+        xm_raw1 = load_planes(as_planes(xm[1]), "xm_raw1")
+        v_source.extend(load_table(vT[tile_rows(j), :]) for j in (1, 2, 3))
+        nv_table.extend(load_nv_table(j) for j in (1, 2, 3))
+
+        x_staged0 = buffer([P, R * PACK], BF16, "x_staged")
+        deal(nc.scalar.copy, x_staged0, x_raw0[0], 0)
+        w_mx0 = quantize(w_staged0, E4M3, "w0", "w0_codes")
+        deal(nc.vector.tensor_copy, x_staged0, x_raw0[1], HALF)
+        w_staged1 = interleaved(nc.scalar.copy, w_planes1[:], "x_raw0_0")
+        half_weight = held.tile([P, B, PACK], F32, name="half_weight")
+        nc.scalar.activation(half_weight[:], row_weight[:], ACT.Copy, scale=0.5)
         x_mx0 = quantize(x_staged0, E4M3, "x0", "x0_codes")
-        v_listed = [gather_v(v_source[j], f"v_listed{j}") for j in range(2)]
         logits0 = product(x_mx0, w_mx0, E4M3)
-        identity = buffer([P, P], F32, "x0_codes")
-        make_identity(nc, identity[:])
-
-        half_weight = held.tile([P, 2, PACK], F32, name="half_weight")
-        nc.scalar.activation(half_weight[:, 0, :], row_weight[:, 0, :], ACT.Copy, scale=0.5)
-        nc.scalar.activation(half_weight[:, 1, :], row_weight[:, 0, :], ACT.Copy, scale=-0.5)
-        tanh0 = [buffer([P, N], F32, f"plane{t}") for t in range(PACK)]
-        for t in range(PACK):
-            nc.scalar.activation(tanh0[t][:], logits0[t][:], ACT.Tanh, scale=0.5)
-        g_parts = [slice(0, G_SPLIT), slice(G_SPLIT, N)]
-        g_planes0 = buffer([P, PACK, N], BF16, "g_planes0")
-        for t in range(PACK):
-            labels = labels0[t // 2][:, t % 2, :]
-            nc.scalar.activation(labels, labels, ACT.Identity, scale=row_weight[:, 0, t : t + 1], bias=half_weight[:, 1, t : t + 1])
-            for cols in g_parts if t == PACK - 1 else [slice(0, N)]:
-                nc.vector.scalar_tensor_tensor(
-                    g_planes0[:, t, cols], tanh0[t][:, cols], half_weight[:, 0, t : t + 1], labels[:, cols], ALU.mult, ALU.subtract
-                )
+        labels0 = [y_raw0[t // 2][:, t % 2, :] for t in range(PACK)]
+        weigh_labels(0, labels0)
+        g_planes0 = gradient_planes(0, tanh_planes(logits0), labels0)
 
         xm_staged0 = [interleaved(nc.scalar.copy, xm_raw0[0][:], "xm_staged0_0")]
-        g_staged0 = buffer([P, N * PACK], BF16, "g_staged")
-        for copy, cols in zip((nc.vector.tensor_copy, nc.scalar.copy), g_parts):
+        g_staged0 = buffer([P, N * PACK], BF16, "x_raw0_256")
+        for copy, cols in ((nc.vector.tensor_copy, slice(0, G_SPLIT)), (nc.scalar.copy, slice(G_SPLIT, N))):
             interleave(copy, g_staged0[:, cols.start * PACK : cols.stop * PACK], g_planes0[:, :, cols])
-        xm_staged0.append(interleaved(nc.scalar.copy, xm_raw0[1][:], "labels0_2"))
+        xm_staged0.append(interleaved(nc.scalar.copy, xm_raw0[1][:], "y_raw0_2"))
         xm_mx0 = [quantize(xm_staged0[0], E4M3, "xm0_0", "xm0_0_codes")]
         g_mx0 = quantize(g_staged0, E5M2, "g0", "xm_raw0_0")
-        dw0 = product(xm_mx0[0], g_mx0, E5M2)
-        w_mx1 = quantize(w_staged[1], E4M3, "w1", "xm_staged0_0")
+        dw = [product(xm_mx0[0], g_mx0, E5M2)]
+
+        v_listed = [buffer([P, B * N], F32, f"v_listed{j}") for j in range(D_TILES)]
+        nv = [v_listed[0]]
+        squares = [buffer([P, B * N], F32, f"squares{j}") for j in range(3)]
+        squares.append(buffer([P, B * N], F32, "w_planes1"))
+        w_mx1 = quantize(w_staged1, E4M3, "w1", "xm_staged0_0")
         xm_mx0.append(quantize(xm_staged0[1], E4M3, "xm0_1", "xm0_1_codes"))
-        dw0.extend(product(xm_mx0[1], g_mx0, E5M2))
-        v_listed.append(gather_v(v_source[2], "g_planes0"))
-        v_listed.append(gather_v(v_source[LAST], "v_listed3"))
+        dw[0].extend(product(xm_mx0[1], g_mx0, E5M2))
+        gather_on_vector(v_listed[0][:, group(0)], v_source[0], group(0))
+        gather_on_scalar(v_listed[0][:, group(1)], v_source[0], group(1))
+        for j in range(3):
+            square(j, 0)
+        add_squares(nc.vector, 0, group(0))
+        scatter_on_scalar(nv_table[0], nv[0], thirds[0])
+        square(3, 0)
 
-        x_raw1 = load_planes(as_planes(xT[1]), "x_raw")
-        labels1 = [load_planes(as_planes(y[1])[:, :2, :], "labels1_0")]
-        xm_raw1 = load_planes(as_planes(xm[1]), "xm_raw1")
-        nv_table.extend([load_v(2), load_v(LAST)])
-        labels1.append(load_planes(as_planes(y[1])[:, 2:, :], "labels1_2"))
-
-        squares0 = buffer([P, D_TILES, N], F32, "w_listed")
-        sums0 = buffer([P, D_TILES, N], F32, "sums0")
-        for j in range(D_TILES):
-            square(squares0[:, j, :], dw0[j])
-            nc.gpsimd.tensor_tensor(sums0[:, j, :], v_listed[j][:, group_cols(0)], squares0[:, j, :], ALU.add)
-        descents01 = buffer([P, 2, N], F32, "descents01")
-        descent(descents01[:, 0, :], dw0[0])
-        logs0 = buffer([P, D_TILES, N], F32, "logs0")
-        for j in range(D_TILES):
-            if j == LAST:
-                descent(descents01[:, 1, :], dw0[1])
-            nc.scalar.activation(logs0[:, j, :], sums0[:, j, :], ACT.Ln, bias=TINY)
-        rate0 = buffer([P, N], F32, "w_listed")
-        rate(rate0[:], logs0[:, 0, :])
-        for j in range(2):
-            scatter_nv(0, j, sums0[:, j, :])
-        scatter_step(0, 0, descents01[:, 0, :], rate0[:])
-
-        x_mx1 = quantize(dealt(nc.scalar.copy, x_raw1, "w_staged0"), E4M3, "x1", "x1_codes")
-        rates0 = buffer([P, LAST, N], F32, "x_raw")
-        for j in range(1, D_TILES):
-            rate(rates0[:, j - 1, :], logs0[:, j, :])
-        scatter_step(0, 1, descents01[:, 1, :], rates0[:, 0, :])
+        x_staged1 = buffer([P, R * PACK], BF16, "x_staged")
+        deal(nc.vector.tensor_copy, x_staged1, x_raw1, 0)
+        x_mx1 = quantize(x_staged1, E4M3, "x1", "x_raw1")
         logits1 = product(x_mx1, w_mx1, E4M3)
-        probs1 = [buffer([P, N], F32, f"plane{t}") for t in range(PACK)]
-        for t in range(PACK):
-            nc.scalar.activation(probs1[t][:], logits1[t][:], ACT.Sigmoid)
+        labels1 = [y_raw1[:, t, :] for t in range(PACK)]
+        weigh_labels(1, labels1)
+        g_planes1 = gradient_planes(1, tanh_planes(logits1), labels1)
+        logs = [buffer([P, 2, B * N], F32, "x_raw1"), buffer([P, 2, B * N], F32, "y_raw1")]
+        log_nv(0, group(0))
+        gather_on_scalar(v_listed[1][:], v_source[1], every_slot)
+        xm_staged1 = interleaved(nc.vector.tensor_copy, xm_raw1[:], "w_staged0")
+        g_staged1 = interleaved(nc.vector.tensor_copy, g_planes1[:], "x_raw0_256")
+        xm_mx1 = quantize(xm_staged1, E4M3, "xm1", "w0_codes")
+        g_mx1 = quantize(g_staged1, E5M2, "g1", "x0_codes")
+        dw.append(product(xm_mx1, g_mx1, E5M2))
+        for j in (2, 3):
+            gather_on_vector(v_listed[j][:], v_source[j], every_slot)
 
-        for j in range(2, D_TILES):
-            scatter_nv(0, j, sums0[:, j, :])
-        xm_staged1 = interleaved(nc.scalar.copy, xm_raw1[:], "x_staged0")
-        g_planes1 = buffer([P, PACK, N], BF16, "xm_raw1")
-        for t in range(PACK):
-            labels = labels1[t // 2][:, t % 2, :]
-            nc.gpsimd.tensor_tensor(labels, probs1[t][:], labels, ALU.subtract)
-            nc.scalar.activation(g_planes1[:, t, :], labels, ACT.Copy, scale=row_weight[:, 1, t : t + 1])
-            if t == 2:
-                descent2 = buffer([P, N], F32, "plane2")
-                descent(descent2[:], dw0[2])
-        xm_mx1 = quantize(xm_staged1, E4M3, "xm1", "plane3")
-        scatter_step(0, 2, descent2[:], rates0[:, 1, :])
-        g_mx1 = quantize(interleaved(nc.scalar.copy, g_planes1[:], "g_staged"), E5M2, "g1", "g1_codes")
-        dw1 = product(xm_mx1, g_mx1, E5M2)
+        nv.extend([buffer([P, B * N], F32, "x_raw0_256"), v_listed[2], v_listed[3]])
+        add_squares(nc.gpsimd, 1, group(0))
+        for j in range(2):
+            square(j, 1)
+        log_nv(1, group(0))
+        for j in (2, 3):
+            square(j, 1)
+        for j in range(2):
+            add_squares(nc.gpsimd, j, group(1))
+        for j in (2, 3):
+            add_squares(nc.gpsimd, j, every_slot)
+        for j in range(2):
+            scatter_on_scalar(nv_table[0], nv[0], thirds[1 + j])
+            log_nv(j, group(1))
+        nc.sync.dma_start(out_1[tile_rows(0), :], nv_table[0][:])
+        for j in (2, 3):
+            log_nv(j, every_slot)
+        for b in range(B):
+            scatter_on_vector(nv_table[1], nv[1], group(b))
+        nc.sync.dma_start(out_1[tile_rows(1), :], nv_table[1][:])
+        scatter_on_vector(nv_table[2], nv[2], every_slot)
+        nc.sync.dma_start(out_1[tile_rows(2), :], nv_table[2][:])
 
-        descent3 = buffer([P, N], F32, "xm_raw1")
-        descent(descent3[:], dw0[LAST])
-        scatter_step(0, LAST, descent3[:], rates0[:, 2, :])
-        squares1 = buffer([P, D_TILES, N], F32, "w_listed")
+        all_steps = buffer([P, D_TILES, B * N], F32, "w_planes1")
+        steps = [all_steps[:, j, :] for j in range(D_TILES)]
         for j in range(D_TILES):
-            square(squares1[:, j, :], dw1[j])
-        descents1 = [buffer([P, N], F32, f"plane{j}") for j in range(D_TILES)]
+            nc.scalar.activation(steps[j], logs[j // 2][:, j % 2, :], ACT.Sigmoid, scale=-0.5, bias=math.log(EPS))
         for j in range(D_TILES):
-            descent(descents1[j][:], dw1[j])
-
-        blocks = [slice(i * P, (i + 1) * P) for i in range(N // P)]
-        turned_logs = buffer([P, D_TILES, N], F32, "logs0")
-        for j in range(D_TILES):
-            turned_sums = psum.tile([P, N], F32, name="bank")
-            for cols in blocks:
-                nc.tensor.matmul(turned_sums[:, cols], lhsT=v_listed[j][:, group_cols(1)][:, cols], rhs=identity[:], start=True, stop=False, is_transpose=True)
-                nc.tensor.matmul(turned_sums[:, cols], lhsT=squares1[:, j, cols], rhs=identity[:], start=False, stop=True, is_transpose=True)
-            nc.scalar.activation(turned_logs[:, j, :], turned_sums[:], ACT.Ln, bias=TINY)
-        rates1 = buffer([P, D_TILES, N], F32, "sums0")
-        for j in range(D_TILES):
-            log_nv = psum.tile([P, N], F32, name="bank")
-            for cols in blocks:
-                nc.tensor.transpose(log_nv[:, cols], turned_logs[:, j, cols], identity[:])
-            rate(rates1[:, j, :], log_nv[:])
-
-        for j in range(D_TILES):
-            scatter_sum(1, j, squares1[:, j, :])
-            nc.sync.dma_start(out_1[tile_rows(j), :], nv_table[j][:])
-        for j in range(D_TILES):
-            scatter_step(1, j, descents1[j][:], rates1[:, j, :])
-            nc.sync.dma_start(out_0[tile_rows(j), :], step_table[j][:])
+            for b in range(B):
+                rate = steps[j][:, group(b)]
+                nc.vector.scalar_tensor_tensor(rate, dw[b][j][:], -LR / EPS, rate, ALU.mult, ALU.mult)
+        for slots in thirds[:2]:
+            scatter_on_scalar(nv_table[3], nv[3], slots)
+            scatter_on_scalar(step_table[0], steps[0], slots)
+        scatter_on_vector(step_table[2], steps[2], every_slot)
+        scatter_on_scalar(nv_table[3], nv[3], thirds[2])
+        nc.sync.dma_start(out_1[tile_rows(3), :], nv_table[3][:])
+        nc.sync.dma_start(out_0[tile_rows(2), :], step_table[2][:])
+        scatter_on_scalar(step_table[1], steps[1], thirds[0])
+        scatter_on_scalar(step_table[0], steps[0], thirds[2])
+        nc.sync.dma_start(out_0[tile_rows(0), :], step_table[0][:])
+        scatter_on_vector(step_table[3], steps[3], every_slot)
+        nc.sync.dma_start(out_0[tile_rows(3), :], step_table[3][:])
+        for slots in thirds[1:]:
+            scatter_on_scalar(step_table[1], steps[1], slots)
+        nc.sync.dma_start(out_0[tile_rows(1), :], step_table[1][:])

import math
from contextlib import ExitStack

import concourse.mybir as mybir

B, N, T, D, R = 2, 512, 2048, 512, 512
LR = 0.1
EPS = 0.001
TINY = 1e-19
FLOPS = 2 * 2 * B * N * D * R

F32 = mybir.dt.float32
BF16 = mybir.dt.bfloat16
U32 = mybir.dt.uint32
U16 = mybir.dt.uint16
U8 = mybir.dt.uint8
E4M3 = mybir.dt.float8_e4m3fn_x4
E5M2 = mybir.dt.float8_e5m2_x4
ACT = mybir.ActivationFunctionType
ALU = mybir.AluOpType

P = 128
PACK = 4
COLS = 512
HALF = COLS // 2
D_TILES = D // P
BAND = 16
MX_ALIGN = 64
TABLE_BUFS = 5
PSUM_BANKS = 8
G_SPLIT = 384


def tile_attend_gnce_ada_kernel(tc, xT, wT, y, wt, xm, vT, offs, out_0, out_1):
    nc = tc.nc
    with ExitStack() as ctx:
        held = ctx.enter_context(tc.tile_pool(name="held", bufs=1))
        tables = ctx.enter_context(tc.tile_pool(name="tables", bufs=TABLE_BUFS))
        work = ctx.enter_context(tc.tile_pool(name="work", bufs=1))
        psum = ctx.enter_context(tc.psum_pool(name="psum", bufs=PSUM_BANKS))

        def buffer(shape, dtype, tag):
            return work.tile(shape, dtype, name=tag, tag=tag, align_bytes=MX_ALIGN)

        def listed(slots):
            return offsets[:, slots.start // BAND : slots.stop // BAND]

        def group(b):
            return slice(b * N, (b + 1) * N)

        def tile_rows(j):
            return slice(j * P, (j + 1) * P)

        def load(tile, source):
            nc.sync.dma_start(tile[:], source)
            return tile

        def load_table(rows):
            return load(tables.tile([P, T], F32, name="table"), rows)

        def load_nv_table(j):
            return load(held.tile([P, T], F32, name=f"nv_table{j}"), vT[tile_rows(j), :])

        def as_planes(matrix):
            return matrix.rearrange("(p t) c -> p t c", t=PACK)

        def load_planes(planes, tag):
            return load(buffer(list(planes.shape), F32, tag), planes)

        def interleave(copy, staged, planes):
            copy(staged.rearrange("p (c i t) -> p c t i", i=PACK, t=PACK), planes.rearrange("p t (c i) -> p c t i", i=PACK))

        def interleaved(copy, planes, tag):
            staged = buffer([P, planes.shape[2] * PACK], BF16, tag)
            interleave(copy, staged[:], planes)
            return staged

        def deal(copy, staged, x_raw, first_row):
            m = slice(first_row // PACK, (first_row + x_raw.shape[2]) // PACK)
            copy(
                staged[:].rearrange("p (t m k) -> p m k t", t=PACK, k=PACK)[:, m],
                x_raw[:].rearrange("p k (m t) -> p m k t", t=PACK),
            )

        def quantize(staged, fmt, name, codes_tag):
            words = staged.shape[1] // PACK
            codes = buffer([P, words], U32, codes_tag)
            scales = held.tile([P, words], U8, name=name + "_scales", align_bytes=MX_ALIGN)
            nc.vector.quantize_mx(out=codes[:].bitcast(fmt), scales=scales[:], in_=staged[:])
            return codes, scales

        def product(stationary, moving, moving_fmt):
            banks = []
            for i in range(stationary[0].shape[1] // P):
                banks.append(psum.tile([P, COLS], F32, name="bank"))
                nc.tensor.matmul_mx(
                    out=banks[i][:],
                    lhsT=stationary[0][:, i * P : (i + 1) * P].bitcast(E4M3),
                    lhsT_scale=stationary[1][:, i * P : (i + 1) * P],
                    rhs=moving[0][:].bitcast(moving_fmt),
                    rhs_scale=moving[1][:],
                    start=True,
                    stop=True,
                )
            return banks

        def gather_on_scalar(out, table, slots):
            nc.scalar.activation(out, table[:].indirect(listed(slots)), ACT.Copy)

        def gather_on_vector(out, table, slots):
            nc.vector.tensor_copy(out, table[:].indirect(listed(slots)))

        def scatter_on_scalar(table, values, slots):
            nc.scalar.activation(table[:].indirect(listed(slots)), values[:, slots], ACT.Copy)

        def scatter_on_vector(table, values, slots):
            nc.vector.tensor_copy(table[:].indirect(listed(slots)), values[:, slots])

        def tanh_planes(logits):
            planes = [buffer([P, N], F32, f"tanh{t}") for t in range(PACK)]
            for t in range(PACK):
                nc.scalar.activation(planes[t][:], logits[t][:], ACT.Tanh, scale=0.5)
            return planes

        def weigh_labels(b, labels):
            for t in range(PACK):
                nc.vector.tensor_scalar(
                    labels[t], labels[t], row_weight[:, b, t : t + 1], half_weight[:, b, t : t + 1], ALU.mult, ALU.subtract
                )

        def gradient_planes(b, tanh, labels):
            planes = buffer([P, PACK, N], BF16, "g_planes")
            for t in range(PACK):
                nc.vector.scalar_tensor_tensor(
                    planes[:, t, :], tanh[t][:], half_weight[:, b, t : t + 1], labels[t], ALU.mult, ALU.subtract
                )
            return planes

        def square(j, b):
            nc.scalar.activation(squares[j][:, group(b)], dw[b][j][:], ACT.Square)

        def add_squares(engine, j, slots):
            engine.tensor_tensor(nv[j][:, slots], v_listed[j][:, slots], squares[j][:, slots], ALU.add)

        def log_nv(j, slots):
            nc.scalar.activation(logs[j // 2][:, j % 2, slots], nv[j][:, slots], ACT.Ln, bias=TINY)

        every_slot = slice(0, B * N)
        thirds = [slice(0, 384), slice(384, 768), slice(768, 1024)]

        offsets = held.tile([P, B * N // BAND], U16, name="offsets")
        nc.sync.dma_start(offsets[:], offs)
        w_plane = [load_table(as_planes(wT)[:, t, :]) for t in range(PACK)]
        x_raw0 = [load_planes(as_planes(xT[0])[:, :, r : r + HALF], f"x_raw0_{r}") for r in range(0, R, HALF)]
        row_weight = load(held.tile([P, B, PACK], F32, name="row_weight"), wt.rearrange("b (p t) o -> p b (t o)", t=PACK))
        y_raw0 = [load_planes(as_planes(y[0])[:, t : t + 2, :], f"y_raw0_{t}") for t in range(0, PACK, 2)]
        xm_raw0 = [load_planes(as_planes(xm[0])[:, :, c : c + HALF], f"xm_raw0_{c}") for c in range(0, D, HALF)]
        v_source = [load_table(vT[tile_rows(0), :])]
        nv_table = [load_nv_table(0)]
        x_raw1 = load_planes(as_planes(xT[1]), "x_raw1")

        step_table = []
        for j in range(D_TILES):
            step_table.append(held.tile([P, T], F32, name=f"step_table{j}"))
            nc.vector.memset(step_table[j][:].bitcast(U32), 0)

        w_staged0 = buffer([P, N * PACK], BF16, "w_staged0")
        w_planes1 = buffer([P, PACK, N], BF16, "w_planes1")
        for t in range(PACK):
            gather_on_vector(w_staged0[:].rearrange("p (c t) -> p c t", t=PACK)[:, :, t], w_plane[t], group(0))
            gather_on_scalar(w_planes1[:, t, :], w_plane[t], group(1))

        y_raw1 = load_planes(as_planes(y[1]), "y_raw1")
        xm_raw1 = load_planes(as_planes(xm[1]), "xm_raw1")
        v_source.extend(load_table(vT[tile_rows(j), :]) for j in (1, 2, 3))
        nv_table.extend(load_nv_table(j) for j in (1, 2, 3))

        x_staged0 = buffer([P, R * PACK], BF16, "x_staged")
        deal(nc.scalar.copy, x_staged0, x_raw0[0], 0)
        w_mx0 = quantize(w_staged0, E4M3, "w0", "w0_codes")
        deal(nc.vector.tensor_copy, x_staged0, x_raw0[1], HALF)
        w_staged1 = interleaved(nc.scalar.copy, w_planes1[:], "x_raw0_0")
        half_weight = held.tile([P, B, PACK], F32, name="half_weight")
        nc.scalar.activation(half_weight[:], row_weight[:], ACT.Copy, scale=0.5)
        x_mx0 = quantize(x_staged0, E4M3, "x0", "x0_codes")
        logits0 = product(x_mx0, w_mx0, E4M3)
        labels0 = [y_raw0[t // 2][:, t % 2, :] for t in range(PACK)]
        weigh_labels(0, labels0)
        g_planes0 = gradient_planes(0, tanh_planes(logits0), labels0)

        xm_staged0 = [interleaved(nc.scalar.copy, xm_raw0[0][:], "xm_staged0_0")]
        g_staged0 = buffer([P, N * PACK], BF16, "x_raw0_256")
        for copy, cols in ((nc.vector.tensor_copy, slice(0, G_SPLIT)), (nc.scalar.copy, slice(G_SPLIT, N))):
            interleave(copy, g_staged0[:, cols.start * PACK : cols.stop * PACK], g_planes0[:, :, cols])
        xm_staged0.append(interleaved(nc.scalar.copy, xm_raw0[1][:], "y_raw0_2"))
        xm_mx0 = [quantize(xm_staged0[0], E4M3, "xm0_0", "xm0_0_codes")]
        g_mx0 = quantize(g_staged0, E5M2, "g0", "xm_raw0_0")
        dw = [product(xm_mx0[0], g_mx0, E5M2)]

        v_listed = [buffer([P, B * N], F32, f"v_listed{j}") for j in range(D_TILES)]
        nv = [v_listed[0]]
        squares = [buffer([P, B * N], F32, f"squares{j}") for j in range(3)]
        squares.append(buffer([P, B * N], F32, "w_planes1"))
        w_mx1 = quantize(w_staged1, E4M3, "w1", "xm_staged0_0")
        xm_mx0.append(quantize(xm_staged0[1], E4M3, "xm0_1", "xm0_1_codes"))
        dw[0].extend(product(xm_mx0[1], g_mx0, E5M2))
        gather_on_vector(v_listed[0][:, group(0)], v_source[0], group(0))
        gather_on_scalar(v_listed[0][:, group(1)], v_source[0], group(1))
        for j in range(3):
            square(j, 0)
        add_squares(nc.vector, 0, group(0))
        scatter_on_scalar(nv_table[0], nv[0], thirds[0])
        square(3, 0)

        x_staged1 = buffer([P, R * PACK], BF16, "x_staged")
        deal(nc.vector.tensor_copy, x_staged1, x_raw1, 0)
        x_mx1 = quantize(x_staged1, E4M3, "x1", "x_raw1")
        logits1 = product(x_mx1, w_mx1, E4M3)
        labels1 = [y_raw1[:, t, :] for t in range(PACK)]
        weigh_labels(1, labels1)
        g_planes1 = gradient_planes(1, tanh_planes(logits1), labels1)
        logs = [buffer([P, 2, B * N], F32, "x_raw1"), buffer([P, 2, B * N], F32, "y_raw1")]
        log_nv(0, group(0))
        gather_on_scalar(v_listed[1][:], v_source[1], every_slot)
        xm_staged1 = interleaved(nc.vector.tensor_copy, xm_raw1[:], "w_staged0")
        g_staged1 = interleaved(nc.vector.tensor_copy, g_planes1[:], "x_raw0_256")
        xm_mx1 = quantize(xm_staged1, E4M3, "xm1", "w0_codes")
        g_mx1 = quantize(g_staged1, E5M2, "g1", "x0_codes")
        dw.append(product(xm_mx1, g_mx1, E5M2))
        for j in (2, 3):
            gather_on_vector(v_listed[j][:], v_source[j], every_slot)

        nv.extend([buffer([P, B * N], F32, "x_raw0_256"), v_listed[2], v_listed[3]])
        add_squares(nc.gpsimd, 1, group(0))
        for j in range(2):
            square(j, 1)
        log_nv(1, group(0))
        for j in (2, 3):
            square(j, 1)
        for j in range(2):
            add_squares(nc.gpsimd, j, group(1))
        for j in (2, 3):
            add_squares(nc.gpsimd, j, every_slot)
        for j in range(2):
            scatter_on_scalar(nv_table[0], nv[0], thirds[1 + j])
            log_nv(j, group(1))
        nc.sync.dma_start(out_1[tile_rows(0), :], nv_table[0][:])
        for j in (2, 3):
            log_nv(j, every_slot)
        for b in range(B):
            scatter_on_vector(nv_table[1], nv[1], group(b))
        nc.sync.dma_start(out_1[tile_rows(1), :], nv_table[1][:])
        scatter_on_vector(nv_table[2], nv[2], every_slot)
        nc.sync.dma_start(out_1[tile_rows(2), :], nv_table[2][:])

        all_steps = buffer([P, D_TILES, B * N], F32, "w_planes1")
        steps = [all_steps[:, j, :] for j in range(D_TILES)]
        for j in range(D_TILES):
            nc.scalar.activation(steps[j], logs[j // 2][:, j % 2, :], ACT.Sigmoid, scale=-0.5, bias=math.log(EPS))
        for j in range(D_TILES):
            for b in range(B):
                rate = steps[j][:, group(b)]
                nc.vector.scalar_tensor_tensor(rate, dw[b][j][:], -LR / EPS, rate, ALU.mult, ALU.mult)
        for slots in thirds[:2]:
            scatter_on_scalar(nv_table[3], nv[3], slots)
            scatter_on_scalar(step_table[0], steps[0], slots)
        scatter_on_vector(step_table[2], steps[2], every_slot)
        scatter_on_scalar(nv_table[3], nv[3], thirds[2])
        nc.sync.dma_start(out_1[tile_rows(3), :], nv_table[3][:])
        nc.sync.dma_start(out_0[tile_rows(2), :], step_table[2][:])
        scatter_on_scalar(step_table[1], steps[1], thirds[0])
        scatter_on_scalar(step_table[0], steps[0], thirds[2])
        nc.sync.dma_start(out_0[tile_rows(0), :], step_table[0][:])
        scatter_on_vector(step_table[3], steps[3], every_slot)
        nc.sync.dma_start(out_0[tile_rows(3), :], step_table[3][:])
        for slots in thirds[1:]:
            scatter_on_scalar(step_table[1], steps[1], slots)
        nc.sync.dma_start(out_0[tile_rows(1), :], step_table[1][:])
